import numpy as np, ml_dtypes
CORES = [66,74,82,90,194,202,210,218]
N = 8
import mx_ref
BF = ml_dtypes.bfloat16
def gcols(t, e):
    v = np.concatenate([t.reshape(8, 16, -1, 4), np.zeros((8, 16, 1, 4), BF)], axis=2)
    return np.ascontiguousarray(np.stack([v[g][:, e[g]] for g in range(8)])).reshape(128, -1)
def tile(rs):
    return np.stack(rs, axis=2).reshape(128, -1).astype(BF)
def cut(t, i, w=512):
    return t[:, w * i:w * i + w]
def pick(q, e):
    c = np.concatenate([q[0].reshape(128, -1, 4), np.zeros((128, 1, 4), np.uint8)], axis=1); s = np.concatenate([q[1], np.ones((16, 1), np.uint8)], axis=1)
    return (np.ascontiguousarray(c[:, e].reshape(128, -1)), np.ascontiguousarray(s[:, e]))
def join(*qs):
    return (np.concatenate([q[0] for q in qs], axis=1), np.concatenate([q[1] for q in qs], axis=1))
def put(q, e, v):
    c, s = q[0].reshape(128, -1, 4).copy(), q[1].copy(); c[:, e] = v[0].reshape(128, -1, 4); s[:, e] = v[1]
    return (c.reshape(128, -1), s)
def pk(c, s):
    return (np.ascontiguousarray(c), mx_ref.live(s))
def emit(q):
    return q[0], q[1]
def packed(v, rng):
    q = [mx_ref.quantize(np.ascontiguousarray(v[r])) for r in range(N)]
    return np.stack([a for a, b in q]), np.stack([mx_ref.plane(b, rng) for a, b in q])
def values_of_codes():
    e, c = np.zeros((128, 128, 4), np.float32), np.zeros((128, 2, 4), np.uint8)
    e[np.arange(128), np.arange(128), 0] = 1
    c[:127, :, 0] = np.arange(256).reshape(2, 128).T[:127]
    return mx_ref.matmul(mx_ref.quantize(e.reshape(128, 512).astype(BF)), (c.reshape(128, 8), np.full((16, 2), 127, np.uint8))).T.reshape(-1).astype(np.float64)
CODE_VALUE, SCALE_VALUE = values_of_codes(), 2.0 ** (np.arange(256) - 127.0)
def decode(q):
    return (CODE_VALUE[q[0]].reshape(16, 8, -1, 4) * SCALE_VALUE[q[1]][:, None, :, None] + 0.0).reshape(128, -1).astype(np.float32)
def f(rng, *shape):
    return mx_ref.flush((rng.standard_normal(shape, dtype=np.float32) * np.exp2(rng.integers(-2, 3, shape[:-1] + (1,)))).astype(BF))
def wide(rng, *shape, cols=0):
    v = rng.standard_normal(shape, dtype=np.float32) * np.exp2(rng.integers(-12, 13, shape)).astype(np.float32)
    if cols: v *= np.repeat(np.exp2(rng.integers(-cols, cols + 1, shape[:-2] + (1, shape[-1] // 4))) * (rng.random(shape[:-2] + (1, shape[-1] // 4)) > 0.0625), 4, axis=-1).astype(np.float32)
    return mx_ref.flush(v.astype(BF))
C, K, R = 224, 80, 3
STEP = [1, 2, 4]
PAIRS = np.array([(i, j) for i in range(K) for j in range(K) if (i + 1) * (j + 1) <= K])
PI, PJ = PAIRS[:, 0], PAIRS[:, 1]
def partner(r, t):
    return r ^ STEP[t]
def best(s, n):
    return np.argsort(-s, axis=1, kind="stable")[:, :n]
def big(v):
    v = v.astype(np.float32)
    v[np.abs(v) < np.float32(2.0 ** -16)] = 0
    return v.astype(BF)
def numbers_of(rng):
    return {"x": big(f(rng, N, 128, 4 * C)), "u": np.array(f(rng, N, 128, 512)), "v": np.array(f(rng, N, 128, 512))}
def weights(rng, w):
    c, p = packed(w, rng)
    return {"wc": c, "ws": p}
def signs(rng):
    return np.stack([rng.permutation(8) % 2 * 2.0 - 1.0 for r in range(N)])
def half(rng):
    return (np.arange(N) >> int(rng.integers(1, N.bit_length() - 1))) & 1 == int(rng.integers(2))
def setup_inputs(rng):
    return {**numbers_of(rng), **weights(rng, big(f(rng, N, 128, 2048)))}
def setup_inputs_ties(rng):
    d = numbers_of(rng)
    e = rng.permutation(N)
    x = d["x"].reshape(N, 8, 16, C, 4)
    for r in range(N):
        k = np.zeros(C, int) if r == e[0] else rng.permutation(C) % 3
        a = x[r][:, :8, :3].copy()
        a[:, :, 2] = 0
        x[r][:, :8] = a[:, :, k]
    x[e[1]] = 0
    u = d["u"].reshape(N, 8, 16, 128, 4)
    u[:, :, 8:, ::16] = 0
    w = big(f(rng, N, 128, 2048)).reshape(N, 8, 16, 4, 8, 16, 4)
    w[:, :, 8:, :, :, :8] = 0
    return {"x": x.reshape(N, 128, 4 * C), "u": u.reshape(N, 128, 512), "v": d["v"], **weights(rng, w.reshape(N, 128, 2048))}
def setup_inputs_near(rng):
    d = numbers_of(rng)
    x = d["x"].astype(np.float32).reshape(N, 8, 16, C, 4)
    a, low = signs(rng), half(rng)
    m = low[:, None] & (a < 0)
    s = np.arange(C) // 2
    s = np.where(m[:, :, None], C // 2 - 1 - s, s)
    g = ((s[:, :, :, None] >> np.arange(8)) & 1) * np.exp2(np.arange(8) - 23.0) * np.where(m, -1.0, 1.0)[:, :, None, None] + 0.0
    x[:, :, 0] = 0
    x[:, :, 0, :, 0] = np.where(low[:, None], 0.0, a)[:, :, None]
    x[:, :, 8] = g[:, :, :, :4]
    x[:, :, 9] = g[:, :, :, 4:]
    x[:, :, 10:] = rng.integers(4, 8, (N, 8, 6, C, 4)) * rng.choice([-1.0, 1.0], (N, 8, 6, C, 4)) * 2.0 ** -20
    x[low, :, 8:] *= np.float32(2.0 ** -4)
    u = d["u"].reshape(N, 128, 128, 4)
    k = np.where(low, 2.0 ** -30, 1.0).astype(np.float32).astype(BF)
    u[:, :, ::16] = 0
    for h in range(0, 128, 16):
        u[:, h, h, 0] = k
        u[:, h + 8:h + 10, h] = k[:, None, None]
    w = big(f(rng, N, 128, 2048)).reshape(N, 128, 4, 8, 16, 4)
    w[:, :, :, :, 0] = 0
    w[:, :, :, :, 8:] = 0
    return {"x": x.reshape(N, 128, 4 * C).astype(BF), "u": u.reshape(N, 128, 512), "v": d["v"], **weights(rng, w.reshape(N, 128, 2048))}
def setup_inputs_huge(rng):
    d = numbers_of(rng)
    x = 2.0 ** 30 * (0.9 + 0.1 * rng.random((N, 128, C, 4)))
    c = np.stack([np.where(rng.permutation(C) % 4 == 0, 1.0, -1.0) for r in range(N)])
    c[half(rng)] = 1
    x *= c[:, None, :, None]
    u = d["u"].reshape(N, 128, 128, 4)
    a = 2.0 ** 30 * (0.9 + 0.1 * rng.random((N, 128, 8, 4))) * signs(rng)[np.arange(N) // 2][:, None, :, None]
    u[:, :, ::16] = a.astype(np.float32).astype(BF)
    w = np.zeros((N, 128, 4, 128, 4), np.float32)
    i = np.arange(128)
    for b in range(4): w[:, i, b, i, b] = -4
    return {"x": x.astype(np.float32).reshape(N, 128, 4 * C).astype(BF), "u": u.reshape(N, 128, 512), "v": d["v"], **weights(rng, w.reshape(N, 128, 2048).astype(BF))}
def setup_inputs_steep(rng):
    d = numbers_of(rng)
    x = d["x"].astype(np.float32).reshape(N, 8, 16, C, 4)
    k = np.argsort(rng.random((N, 8, C)), axis=2)
    x[:, :, 0] = 0
    x[:, :, 0, :, 0] = k // 16 * 16
    x[:, :, 0, :, 1] = k % 16
    x[:, :, 0, :, 2] = 256
    flat = np.arange(N) % 2 == int(rng.integers(2))
    x[flat, :, :8] *= np.float32(2.0 ** -10)
    for r in range(N):
        for g in rng.permutation(8)[:4]: x[r, g, 0, int(rng.integers(C)), 0] = 2.0 ** 30
    u = d["u"].reshape(N, 128, 128, 4)
    u[:, :, ::16] = 0
    for h in range(0, 128, 16): u[:, h, h, :2] = 1
    w = big(f(rng, N, 128, 2048))
    w[:, ::16] = 0
    return {"x": x.reshape(N, 128, 4 * C).astype(BF), "u": u.reshape(N, 128, 512), "v": d["v"], **weights(rng, w)}
def setup_inputs_spread(rng):
    d = setup_inputs(rng)
    d["x"] = big(wide(rng, N, 128, 4 * C, cols=6))
    return d
def check_inputs(d):
    b = []
    for k in ("x", "u", "v"):
        a = np.abs(d[k].astype(np.float32))
        if not (np.isfinite(a).all() and ((a == 0) | (a >= 2.0 ** -30) & (a <= 2.0 ** 30)).all()): b.append("a value of " + k)
    return b
def reference(x, u, v, wc, ws):
    qu = [mx_ref.quantize(u[r]) for r in range(N)]
    lay = [pk(wc[r], ws[r]) for r in range(N)]
    now = [x[r] for r in range(N)]
    taken = [None] * N
    for t in range(R):
        first, score, sent = [], [], []
        for r in range(N):
            s = mx_ref.matmul(qu[r], mx_ref.quantize(now[r]))[::16] + np.float32(0.0)
            o = best(s, K)
            first.append(o)
            score.append(np.take_along_axis(s, o, axis=1))
            sent.append(mx_ref.quantize(gcols(now[r], o)))
        came = decode(join(*sent)).astype(BF)
        for r in range(N):
            e = partner(r, t)
            n = best(score[r][:, PI] + score[e][:, PJ], C)
            taken[r] = n
            one = gcols(now[r], np.take_along_axis(first[r], PI[n], axis=1))
            two = gcols(cut(came, e, 4 * K), PJ[n])
            z = ((one.astype(np.float32) + two.astype(np.float32)) * np.float32(0.5)).astype(BF)
            q, zf = mx_ref.quantize(z), z.astype(np.float32)
            now[r] = tile([np.maximum(mx_ref.matmul(pick(lay[r], np.arange(128 * b, 128 * b + 128)), q), np.float32(0.0)) * np.float32(0.03125) + zf[:, b::4] for b in range(4)])
    y, ol = np.zeros((N, 128, C), np.float32), np.zeros((N, 8, C), np.float32)
    oc, osc = np.zeros((N, 128, 4 * C), np.uint8), np.zeros((N, 16, C), np.uint8)
    for r in range(N):
        q = mx_ref.quantize(now[r])
        y[r] = mx_ref.matmul(mx_ref.quantize(v[r]), q)
        ol[r] = taken[r]
        oc[r], osc[r] = emit(q)
    return {"y": y, "ol": ol, "oc": oc, "osc": osc}

@@ -1,0 +1,556 @@
+from concourse.bass import DstId, RemoteDMATransfer
+from concourse.mybir import dt, AluOpType, ActivationFunctionType
+
+C, K, R = 224, 80, 3
+STEP = [1, 2, 4]
+LEN = [K // (i + 1) for i in range(K)]
+START = [sum(LEN[:i]) for i in range(K)]
+NP = sum(LEN)
+BIG = 1.0e29
+KK = 2.0 ** 21
+JW = 168
+GA, GB = 176, 336
+
+OWN_TILES = [(224, [13, 12, 11, "d"]), (160, [10, 9, 8, 7]), (128, [6, 5, 4, 3]), (128, [2, 1])]
+OWN_V = [13, 12, 11, 10]
+OWN_S = [9, 8, 7, 6, 5, 4, 3, 2, 1]
+OWN_RANGE = {m: (0, 16 * m) for m in range(1, 14)}
+PAIR_TILES = [(336, [22, 21, 20, "d"]), (304, [19, 18, 17, 16]), (240, [15, 14, 13, 12]), (176, [11, 10, 9, 8]), (128, [7, 6, 5])]
+PAIR_V = [20, 19, 18, 17, 16, 15]
+PAIR_S = [22, 21, 5, 6, 14, 13, 12, 11, 10, 9, 8, 7]
+PAIR_RANGE = {m: (0, 16 * m) for m in range(7, 21)}
+PAIR_RANGE.update({5: (0, 80), 6: (16, 80), 21: (0, 328), 22: (0, 328)})
+WO = sum(w for w, _ in OWN_TILES)
+WP = sum(w for w, _ in PAIR_TILES)
+
+F, B, I, U, Q, S8 = "float32", "bfloat16", "int32", "uint16", "float8_e4m3fn_x4", "uint8"
+SCRATCH = {}
+for _n, _w, _d in [
+    ("xb", 896, B), ("ub", 512, B), ("vb", 512, B), ("wq", 512, Q), ("wp", 512, S8),
+    ("uq", 128, Q), ("us", 128, S8), ("vq", 128, Q), ("vs", 128, S8), ("urq", 128, Q), ("urs", 128, S8),
+    ("u16q", 16, Q), ("u16s", 16, S8),
+    ("zb", 512, B), ("eb", 2048, B), ("eq", 512, Q), ("es", 512, S8), ("cb", 1024, B), ("cq", 256, Q), ("cs", 256, S8),
+    ("grp", 512, B), ("li", 3, I), ("col", 8, F), ("xm", 32, B), ("b16", 24, F), ("nf", 368, F), ("x0", 368, F),
+    ("xc", 368, F), ("xd", 368, F), ("m1", 224, B), ("m3", 32, B), ("d0", 224, B), ("keep0", 224, B), ("keepk", 336, B),
+    ("tmpa", 96, B), ("dist", 128, F),
+    ("l16", 8, U), ("l2", 8, U), ("l8", 2, U), ("pil", 10, U), ("pjl", 10, U), ("ci", 10, I),
+    ("baseo", 14, F), ("basep", 24, F),
+    ("mo", 4 * WO, B), ("moq", WO, Q), ("mos", WO, S8), ("mp", 4 * WP, B), ("mpq", WP, Q), ("mps", WP, S8),
+    ("yy", 224, F), ("vsc", 368, F), ("tau", 2400, B), ("junk", 6 * JW, B), ("dgo", 224, B), ("dgp", 368, B),
+    ("rso", 14, F), ("rsp", 24, F), ("p1", 24, F), ("ext", 368, F), ("yr", 24, F), ("rk", 24, U),
+    ("ow", 224, F), ("oext", 96, F), ("off4", 24, U), ("ssb", 224, F), ("spb", 224, F), ("sv80", 80, F), ("ew", 224, F),
+    ("sp", GB - GA, F), ("row", 368, F), ("xw", 368, F), ("xi", 14, I), ("a16", 14, U), ("bl16", 14, U),
+    ("ts", 320, B), ("eh", 896, B), ("ess", 320, B), ("bg", 896, B), ("zt", 896, B), ("zq", 224, Q), ("zs", 224, S8),
+    ("rr", 896, F), ("oi", 224, I), ("olf", 224, F), ("yf", 224, F),
+    ("rko", 16 * R, U), ("lr", 16 * R, U), ("o16", 8 * R, U), ("ll", 8 * R, U), ("tq3", 224, Q), ("tsc3", 224, S8),
+] + [(n + str(t + k), w, d) for t in range(R) for n, k, w, d in [
+    ("t", 1, 896, B), ("lq", 0, 224, Q), ("ls", 0, 224, S8), ("ulq", 0, 16, Q), ("uls", 0, 16, S8), ("upq", 0, 128, Q),
+    ("ups", 0, 128, S8), ("tq", 0, 224, Q), ("tsc", 0, 224, S8)]]:
+    SCRATCH[_n] = ("sbuf", [128, _w], _d)
+for _t in range(8):
+    SCRATCH["ps%d" % _t] = ("psum", [128, 512], F)
+
+SEMAPHORES = (["qv", "qs", "qp", "qg", "ldx", "ldu", "ldv", "ldw", "lds", "loc", "st"]
+              + [n + str(t) for n in ("big", "lst", "rnk", "ua") for t in range(R)])
+
+A = AluOpType
+AF = ActivationFunctionType
+
+
+def rank_program(g, core, T, topo):
+    rank = T.rank_of(core)
+    if rank is None:
+        return
+    queues = {"v": g.vector, "s": g.scalar, "p": g.tensor, "g": g, "y": g.sync}
+    qsem = {"v": "qv", "s": "qs", "p": "qp", "g": "qg"}
+    ops = []
+    writer, readers, totals = {}, {}, {"loc": 0}
+
+    def op(q, fn, reads=(), writes=(), kind="c"):
+        deps = []
+        me = len(ops)
+        for k in reads:
+            if k in writer:
+                deps.append(writer[k])
+            if k.startswith("ps"):
+                deps.extend(d for d in readers.get(k, []) if ops[d[1]][0] != q)
+        for k in writes:
+            if k in writer and not (q == "p" and writer[k][0] == "op" and ops[writer[k][1]][0] == "p"):
+                deps.append(writer[k])
+            deps.extend(readers.get(k, []))
+        ops.append([q, fn, deps, kind])
+        if kind == "c":
+            for k in reads:
+                readers.setdefault(k, []).append(("op", me))
+            for k in writes:
+                writer[k] = ("op", me)
+                readers[k] = []
+
+    def arrives(keys, sem, count):
+        for k in keys:
+            writer[k] = ("sem", sem, count)
+
+    def dma(q, out, in_, sem, reads=(), writes=()):
+        totals[sem] = totals.get(sem, 0) + 16
+        op(q, lambda: queues[q].dma_start(out, in_).then_inc(T.sem[sem], 16), reads, (), "d")
+        arrives(writes, sem, totals[sem])
+
+    V, S, P = g.vector, g.scalar, g.tensor
+
+    def vts(out, in0, s1, s2, o0, o1, r, w):
+        if o1 is None:
+            op("v", lambda: V.tensor_scalar(out, in0, s1, None, o0), r, w)
+        else:
+            op("v", lambda: V.tensor_scalar(out, in0, s1, s2, o0, o1), r, w)
+
+    def vtt(out, a, b, o, r, w):
+        op("v", lambda: V.tensor_tensor(out, a, b, o), r, w)
+
+    def vcp(out, a, r, w):
+        op("v", lambda: V.tensor_copy(out, a), r, w)
+
+    def vms(out, c, w):
+        op("v", lambda: V.memset(out, c), (), w)
+
+    def vsc(out, d0, d1, init, o0, o1, r, w):
+        op("v", lambda: V.tensor_tensor_scan(out, d0, d1, init, o0, o1), r, w)
+
+    def vq(out, sc, a, r, w):
+        op("v", lambda: V.quantize_mx(out, sc, a), r, w)
+
+    def act(out, a, f, r, w, **kw):
+        op("s", lambda: S.activation(out, a, f, **kw), r, w)
+
+    def mm(out, lq, ls, rq, rs, start, stop, r, w):
+        op("p", lambda: P.matmul_mx(out, lq, ls, rq, rs, start, stop), r, w)
+
+    def iota(out, pat, base, cm, w, fl=True):
+        if fl:
+            op("g", lambda: g.iota(out, pat, base, cm, allow_small_or_imprecise_dtypes=True), (), w)
+        else:
+            op("g", lambda: g.iota(out, pat, base, cm), (), w)
+
+    peers = [T.cores[rank ^ STEP[t]] for t in range(R)]
+
+    def send(t, out, in_, sem, reads, lands):
+        rid, pid = topo.addr(peers[t], core)
+        m = topo.mask(core, peers[t])
+        totals["loc"] += len(topo.engines(core, peers[t]))
+        op("g", lambda: g.remote_dma(out, in_, T.sem[sem], T.sem.loc, pid, rid, m), reads, (), "d")
+        totals[sem] = totals.get(sem, 0) + len(topo.engines(peers[t], core))
+        arrives(lands, sem, totals[sem])
+
+    def u8(ap):
+        return ap.bitcast(dt.uint8)
+
+    def u32(ap):
+        return ap.bitcast(dt.uint32)
+
+    ps = [T["ps%d" % i] for i in range(8)]
+    lcol, l1col, gcol, npcol, cp, kp, cp4, kp0 = [T.col[:, i:i + 1] for i in range(8)]
+    grpk = ["grp%d" % k for k in range(8)]
+
+    dma("y", T.ub[:], T.u[:], "ldu", (), ["ub"])
+    dma("s", T.xb[:], T.x[:], "ldx", (), ["t0"])
+    dma("y", u8(T.wq[:]), T.wc[:], "ldw", ["t0"], ["wq"])
+    dma("y", T.wp[:], T.ws[:], "lds", (), ["wp"])
+    dma("y", T.vb[:], T.v[:], "ldv", (), ["vb"])
+
+    iota(T.li[:, 2:3], [[0, 1]], 0, 1, ["pi"], False)
+    iota(T.xm[:], [[0, 2], [1, 16]], 0, 0, ["xm"])
+    iota(T.b16[:], [[16, 24]], 0, 0, ["b16"])
+    iota(T.nf[:], [[1, NP]], 0, 0, ["nf"])
+    segs = []
+    i = 0
+    while i < K:
+        j = i
+        while j < K and LEN[j] == LEN[i]:
+            j += 1
+        segs.append((i, j - i))
+        i = j
+    xk = ["x0.%d" % i for i, n in segs]
+
+    def seg_iota(i, n):
+        iota(T.x0[:, START[i]:START[i] + n * LEN[i]], [[1, n], [256, LEN[i]]], i, 0, ["x0.%d" % i])
+    for i, n in segs[5:]:
+        seg_iota(i, n)
+
+    vms(T.zb[:], 0.0, ["zb"])
+    vms(T.d0[:], -BIG, ["d0"])
+    vms(T.keep0[:], 1.0, ["keep0"])
+    vts(T.li[:, 0:1], T.li[:, 2:3], 15, None, A.bitwise_and, None, ["pi"], ["li0"])
+    vts(T.li[:, 1:2], T.li[:, 2:3], 4, None, A.logical_shift_right, None, ["pi"], ["li1"])
+    for k in range(8):
+        vms(T.grp[:, 64 * k:64 * k + 64], float(k), ["grp%d" % k])
+    vcp(lcol, T.li[:, 0:1], ["li0"], ["lcol"])
+    vcp(gcol, T.li[:, 1:2], ["li1"], ["gcol"])
+    vms(T.d0[:, 0:224:16], BIG, ["d0"])
+    vms(T.keep0[:, 0:224:16], 0.0, ["keep0"])
+    vts(l1col, lcol, 1.0, None, A.add, None, ["lcol"], ["l1col"])
+    vts(T.l8[:, 0:1], lcol, 8.0, None, A.mult, None, ["lcol"], ["l8"])
+    vts(T.tmpa[:, 0:32], T.xm[:], lcol, -2 * BIG, A.is_equal, A.mult, ["xm", "lcol"], ["tmp0"])
+    vts(T.tmpa[:, 32:64], T.xm[:], l1col, KK, A.is_equal, A.mult, ["xm", "l1col"], ["tmp1"])
+    vts(T.tmpa[:, 64:96], T.xm[:], lcol, None, A.not_equal, None, ["xm", "lcol"], ["tmp2"])
+    vts(T.m1[:, 0:32], T.tmpa[:, 0:32], BIG, None, A.add, None, ["tmp0"], ["m1"])
+    vcp(T.l16[:], T.b16[:, 0:8], ["b16"], ["l16"])
+    vtt(T.keepk[:, 0:32], T.tmpa[:, 32:64], T.tmpa[:, 64:96], A.max, ["tmp1", "tmp2"], ["keepk"])
+    vts(T.cb[:, 0:512], T.grp[:], gcol, None, A.is_equal, None, ["gcol"] + grpk, ["cb0"])
+    vts(cp, lcol, 15.0, 1.0 / KK, A.is_ge, A.max, ["lcol"], ["cp"])
+    vts(kp0, lcol, 15.0, KK, A.is_lt, A.mult, ["lcol"], ["kp0"])
+    vts(npcol, T.li[:, 2:3], -1.0, None, A.mult, None, ["pi"], ["npcol"])
+    vts(T.baseo[:], T.b16[:, 0:14], lcol, 0.3, A.add, A.add, ["b16", "lcol"], ["baseo"])
+    vts(kp, kp0, 1.0, None, A.max, None, ["kp0"], ["kp"])
+    vts(T.l2[:], T.b16[:, 0:8], 0.125, None, A.mult, None, ["b16"], ["l2"])
+    lo = min(OWN_V)
+    vts(T.baseo[:, lo:lo + len(OWN_V)], T.baseo[:, lo:lo + len(OWN_V)], -128.0, None, A.add, None, ["baseo"], ["baseo"])
+
+    def tile_offsets(tiles):
+        return [sum(w for w, _ in tiles[:k]) for k in range(len(tiles))]
+
+    def slot_key(name, k, t):
+        return "%s.%d.%d" % (name, k, t)
+
+    def tile_keys(name, k):
+        return [slot_key(name, k, t) for t in range(4)]
+
+    oo, po = tile_offsets(OWN_TILES), tile_offsets(PAIR_TILES)
+
+    def zero(out, n, w):
+        act(out, T.zb[:, 0:n], AF.Copy, ["zb"], w)
+
+    def zero_tile(buf, name, tiles, offs, k, lo):
+        n = 4 * (tiles[k][0] - lo)
+        zero(buf[:, 4 * (offs[k] + lo):4 * (offs[k] + lo) + n], n, tile_keys(name, k))
+
+    for k, lo in enumerate([176, 112, 48, 0]):
+        zero_tile(T.mo, "mo", OWN_TILES, oo, k, lo)
+    zero(T.rso[:], 14, ["rso"])
+    for n in (32, 64, 128, 256):
+        if n < C:
+            act(T.m1[:, n:min(2 * n, C)], T.m1[:, 0:min(n, C - n)], AF.Copy, ["m1"], ["m1"])
+        act(T.keepk[:, n:min(2 * n, GB)], T.keepk[:, 0:min(n, GB - n)], AF.Copy, ["keepk"], ["keepk"])
+    act(T.cb[:, 512:1024], T.cb[:, 0:512], AF.Copy, ["cb0"], ["cb1"])
+    act(T.cb[:, 515:1024:4], T.cb[:, 3:512:4], AF.Copy, ["cb0"], ["cb1"], scale=-1.0)
+
+    def place_of(tiles, m):
+        for k, (w, bl) in enumerate(tiles):
+            if m in bl:
+                return k, bl.index(m)
+
+    def slot(buf, offs, k, t, lo, hi):
+        return buf[:, 4 * (offs[k] + lo) + t:4 * (offs[k] + hi - 1) + t + 1:4]
+
+    def rowsum(buf, name, tiles, offs, rng, vblocks, m):
+        k, t = place_of(tiles, m)
+        lo, hi = rng[m]
+        h = (hi - lo) // 2
+        x = sorted(vblocks).index(m)
+        vsc(T.junk[:, (x + 1) * JW - h:(x + 1) * JW], slot(buf, offs, k, t, lo, lo + h), slot(buf, offs, k, t, lo + h, hi),
+            -128.0, A.add, A.add, [slot_key(name, k, t)], ["junk%d" % x])
+
+    def v_compare(buf, name, tiles, offs, rng, m, src, skeys, vkey):
+        k, t = place_of(tiles, m)
+        lo, hi = rng[m]
+        vts(slot(buf, offs, k, t, lo, hi), src[:, lo:hi], T.vsc[:, 16 * m + 15:16 * m + 16], None, A.is_lt, None,
+            skeys + [vkey], [slot_key(name, k, t)])
+
+    def s_compares(buf, name, tiles, offs, rng, blocks, src, skeys, vkeys, rs, rkey):
+        pos, o = {}, 0
+        for m in blocks:
+            pos[m] = o
+            o += rng[m][1] - rng[m][0]
+
+        def one(m):
+            lo, hi = rng[m]
+            act(T.tau[:, pos[m]:pos[m] + hi - lo], src[:, lo:hi], AF.Sign, skeys + [vkeys(m)], ["tau%d" % blocks.index(m)],
+                bias=T.vsc[:, 16 * m + 15:16 * m + 16], scale=-1.0)
+
+        def two(m):
+            lo, hi = rng[m]
+            k, t = place_of(tiles, m)
+            act(slot(buf, offs, k, t, lo, hi), T.tau[:, pos[m]:pos[m] + hi - lo], AF.Relu, ["tau%d" % blocks.index(m), rkey],
+                [slot_key(name, k, t), rkey + ".%d" % m], accum_out=rs[:, m:m + 1])
+        one(blocks[0])
+        for x in range(1, len(blocks)):
+            one(blocks[x])
+            two(blocks[x - 1])
+        two(blocks[-1])
+
+    def count(buf, bq, bs, name, tiles, offs, k):
+        w = tiles[k][0]
+        vq(bq[:, offs[k]:offs[k] + w], bs[:, offs[k]:offs[k] + w], buf[:, 4 * offs[k]:4 * (offs[k] + w)], tile_keys(name, k), [name + "q%d" % k])
+        c = 128 if k == 0 else 0
+        mm(ps[2][:, 0:w], T.cq[:, c:c + 128], T.cs[:, c:c + 128], bq[:, offs[k]:offs[k] + w], bs[:, offs[k]:offs[k] + w],
+           k == 0, k == len(tiles) - 1, ["cq", name + "q%d" % k], ["ps2"])
+
+    def partial(nb, base, bkey, dg, dkey):
+        vtt(T.p1[:, 0:nb], base[:, 0:nb], dg[:, 15:16 * nb:16], A.add, [bkey, dkey], ["p1"])
+
+    def partial2(vblocks):
+        lo, n = min(vblocks), len(vblocks)
+        vtt(T.p1[:, lo:lo + n], T.p1[:, lo:lo + n], T.junk[:, JW - 1:n * JW:JW], A.subtract, ["p1"] + ["junk%d" % x for x in range(n)], ["p1"])
+
+    def finish(nb, rs, rkey, sblocks, out, okey):
+        vtt(T.p1[:, 0:nb], T.p1[:, 0:nb], rs[:, 0:nb], A.subtract, ["p1", rkey] + [rkey + ".%d" % m for m in sblocks], ["p1"])
+        vts(T.p1[:, 0:nb], T.p1[:, 0:nb], kp, None, A.mult, None, ["p1", "kp"], ["p1"])
+        n = min(16 * nb, GB)
+        vsc(T.ext[:, 0:n], T.keepk[:, 0:n], ps[2][:, 0:n], 0.0, A.mult, A.add, ["keepk", "ps2"], ["ext"])
+        vtt(T.yr[:, 0:nb], T.ext[:, 15:16 * nb:16], T.p1[:, 0:nb], A.add, ["ext", "ext0", "p1"], ["yr"])
+        vts(out, T.yr[:, 0:nb], cp, None, A.mult, None, ["yr", "cp"], [okey])
+
+    def state(t):
+        return T.xb if t == 0 else T["t%d" % t]
+
+    def tkeys(t):
+        return ["t0"] if t == 0 else ["t%d.%d" % (t, b) for b in range(4)]
+
+    def pick_codes(t):
+        vcp(u32(T["upq%d" % t][:]), u32(T["ulq%d" % t][:]).indirect(T.l2[:]), ["ul%d" % t, "l2"], ["upq%d" % t])
+
+    def pick_scales(t):
+        act(T["ups%d" % t][:], T["uls%d" % t][:].indirect(T.l2[:]), AF.Copy, ["ul%d" % t, "l2"], ["ups%d" % t])
+
+    def unpack(t):
+        for b in range(4):
+            mm(ps[4 + b][:, 0:C], T.eq[:, 128 * b:128 * b + 128], T.es[:, 128 * b:128 * b + 128], T["lq%d" % t][:], T["ls%d" % t][:],
+               True, True, ["eq", "lq%d" % t], ["ps%d" % (4 + b)])
+
+    def halve():
+        for b in range(4):
+            act(T.eh[:, C * b:C * b + C], ps[4 + b][:, 0:C], AF.Copy, ["ps%d" % (4 + b)], ["eh%d" % b], scale=0.5)
+
+    for t in range(R):
+        tq, tsc, lq, ls = T["tq%d" % t], T["tsc%d" % t], T["lq%d" % t], T["ls%d" % t]
+        rko, lr = T.rko[:, 16 * t:16 * t + 14], T.lr[:, 16 * t:16 * t + 14]
+        o16, ll = T.o16[:, 8 * t:8 * t + 6], T.ll[:, 8 * t:8 * t + 6]
+        o5, l5 = T.o16[:, 8 * t:8 * t + 5], T.ll[:, 8 * t:8 * t + 5]
+        if t == 0:
+            vq(T.uq[:], T.us[:], T.ub[:], ["ub"], ["uq"])
+            vcp(u32(T.u16q[:]), u32(T.uq[:]).indirect(T.l8[:, 0:1]), ["uq", "l8"], ["u16q"])
+            act(T.u16s[:], T.us[:].indirect(T.l8[:, 0:1]), AF.Copy, ["uq", "l8"], ["u16s"])
+            vcp(u32(T.urq[:]), u32(T.uq[:]).indirect(T.l16[:]), ["uq", "l16"], ["urq"])
+            act(T.urs[:], T.us[:].indirect(T.l16[:]), AF.Copy, ["uq", "l16"], ["urs"])
+            zero(T.eb[:, 0:512], 512, ["eb0"])
+            for which in range(2):
+                trs = []
+                for r in range(R):
+                    rid, pid = topo.addr(peers[r], core)
+                    e = topo.engines(core, peers[r])[2 * r:2 * r + 2]
+                    src = u8(T.u16q[:]) if which == 0 else T.u16s[:]
+                    dst = u8(T["ulq%d" % r][:]) if which == 0 else T["uls%d" % r][:]
+                    trs.append(RemoteDMATransfer(dst_ids=[DstId(rid=rid, pnc=pid)], dma_engine_mask=sum(1 << x for x in e),
+                                                 remote_sem=T.sem["ua%d" % r], src=src, dst=dst))
+                totals["loc"] += 2 * R
+                op("g", lambda trs=trs: g.remote_dma_fused(trs, local_sem=T.sem.loc), ["u16q" if which == 0 else "u16s"], (), "d")
+            for r in range(R):
+                totals["ua%d" % r] = 4
+                arrives(["ul%d" % r], "ua%d" % r, 4)
+        vq(tq[:], tsc[:], state(t)[:], tkeys(t), ["tq%d" % t])
+        send(t, u8(lq[:]), u8(tq[:]), "big%d" % t, ["tq%d" % t], ["lq%d" % t])
+        send(t, ls[:], tsc[:], "big%d" % t, ["tq%d" % t], ["lq%d" % t])
+        if t == 0:
+            for i, n in segs[:5]:
+                seg_iota(i, n)
+            vq(T.cq[:], T.cs[:], T.cb[:], ["cb0", "cb1"], ["cq"])
+        if t == 1:
+            vq(T.vq[:], T.vs[:], T.vb[:], ["vb"], ["vq"])
+        for b in range(2):
+            mm(ps[b][:, 0:C], T.urq[:], T.urs[:], tq[:], tsc[:], True, True, ["urq", "urs", "tq%d" % t], ["ps%d" % b])
+
+        def ov(m):
+            v_compare(T.mo, "mo", OWN_TILES, oo, OWN_RANGE, m, ps[0], ["ps0"], "vsc")
+
+        def oc(k):
+            count(T.mo, T.moq, T.mos, "mo", OWN_TILES, oo, k)
+        act(T.ssb[:], ps[1][:, 0:C], AF.Copy, ["ps1"], ["ssb"])
+        vtt(T.yy[:], ps[0][:, 0:C], T.m1[:], A.max, ["ps0", "m1"], ["yy"])
+        vsc(T.vsc[:, 0:C], T.d0[:], T.yy[:], 0.0, A.max, A.min, ["d0", "yy"], ["vsc", "vsc.a", "vsc.b"])
+        s_compares(T.mo, "mo", OWN_TILES, oo, OWN_RANGE, OWN_S, ps[1], ["ps1"], lambda m: "vsc", T.rso, "rso")
+        for m in OWN_V[:3]:
+            ov(m)
+        vtt(slot(T.mo, oo, 0, 3, 0, C), ps[0][:, 0:C], T.vsc[:, 0:C], A.is_gt, ["ps0", "vsc"], [slot_key("mo", 0, 3)])
+        ov(OWN_V[3])
+        oc(0)
+        vsc(T.dgo[:], T.keep0[:], slot(T.mo, oo, 0, 3, 0, C), 0.0, A.mult, A.add, ["keep0", slot_key("mo", 0, 3)], ["dgo"])
+        for m in OWN_V:
+            rowsum(T.mo, "mo", OWN_TILES, oo, OWN_RANGE, OWN_V, m)
+        partial(14, T.baseo, "baseo", T.dgo, "dgo")
+        oc(1)
+        partial2(OWN_V)
+        oc(2)
+        oc(3)
+        if t == 0:
+            for b in range(1, 4):
+                zero(T.eb[:, 512 * b:512 * b + 512], 512, ["eb%d" % b])
+            pick_scales(0)
+            act(T.dist[:], T.nf[:, 0:128], AF.Abs, ["nf", "npcol"], ["dist"], bias=npcol)
+        if t == 1:
+            act(T.xd[:], T.x0[:], AF.Copy, xk, ["xd"], scale=512.0)
+        finish(14, T.rso, "rso", OWN_S, rko, "rko%d" % t)
+        send(t, lr, rko, "rnk%d" % t, ["rko%d" % t], ["lr%d" % t])
+
+        if t == 0:
+            pick_codes(0)
+            for b in range(4):
+                act(T.eb[:, 512 * b + b:512 * b + 512:4], T.dist[:], AF.Relu, ["dist"], ["eb%d" % b], bias=1.0, scale=-1.0)
+        mm(ps[3][:, 0:C], T["upq%d" % t][:], T["ups%d" % t][:], lq[:], ls[:], True, True, ["upq%d" % t, "ups%d" % t, "lq%d" % t], ["ps3"])
+        act(T.spb[:], ps[3][:, 0:C], AF.Copy, ["ps3"], ["spb"])
+        if t == 0:
+            for k, lo in enumerate([320, 256, 192, 128, 0]):
+                zero_tile(T.mp, "mp", PAIR_TILES, po, k, lo)
+        vcp(T.ow[:].indirect(rko), T.nf[:, 0:C], ["rko%d" % t, "nf"], ["ow"])
+        vsc(T.oext[:], T.keepk[:, 0:96], T.ow[:, 0:96], 0.0, A.mult, A.add, ["keepk", "ow"], ["oext"])
+        if t == 0:
+            vsc(T.ext[:, 0:GB - GA], T.keepk[:, 0:GB - GA], T.x0[:, GA:GB], 0.0, A.mult, A.add, ["keepk"] + xk, ["ext"])
+        vts(o16, T.oext[:, 15:96:16], cp, None, A.mult, None, ["oext", "cp"], ["o16_%d" % t])
+        send(t, ll, o16, "lst%d" % t, ["o16_%d" % t], ["ll%d" % t])
+        if t == 0:
+            vts(T.ci[:], T.ext[:, 15:GB - GA:16], cp, None, A.mult, None, ["ext", "cp"], ["ci"])
+            vts(T.pjl[:], T.ext[:, 15:GB - GA:16], cp, 1.0 / 256, A.mult, A.mult, ["ext", "cp"], ["pjl"])
+        act(T.sv80[:], T.ssb[:].indirect(o5), AF.Copy, ["ssb", "o16_%d" % t], ["sv80"])
+        if t == 0:
+            vts(T.ci[:], T.ci[:], 255, None, A.bitwise_and, None, ["ci"], ["ci"])
+            vts(cp4, cp, 4.0, None, A.mult, None, ["cp"], ["cp4"])
+            vcp(T.pil[:], T.ci[:], ["ci"], ["pil"])
+            vts(T.m3[:], T.xm[:], lcol, -BIG, A.is_equal, A.mult, ["xm", "lcol"], ["m3"])
+        act(T.sp[:], T.sv80[:].indirect(T.pil[:]), AF.Copy, ["sv80", "pil"], ["sp"])
+        for b in range(4):
+            vts(T.off4[:, 6 * b:6 * b + 6], T.oext[:, 15:96:16], cp4, float(b), A.mult, A.add, ["oext", "cp4"], ["off4.%d" % b])
+        if t == 0:
+            zero(T.mp[:, 3:4 * 112:4], 112, [slot_key("mp", 0, 3)])
+            zero(T.rsp[:], 24, ["rsp"])
+            zero(T.ext[:, GB:NP], NP - GB, ["ext0"])
+            zero(T.dgp[:, 0:112], 112, ["dgp"])
+            zero(T.dgp[:, GB:NP], NP - GB, ["dgp"])
+            vts(T.basep[:], T.b16[:], lcol, 0.3, A.add, A.add, ["b16", "lcol"], ["basep"])
+            vq(T.eq[:], T.es[:], T.eb[:], ["eb%d" % b for b in range(4)], ["eq"])
+            lo = min(PAIR_V)
+            vts(T.basep[:, lo:lo + len(PAIR_V)], T.basep[:, lo:lo + len(PAIR_V)], -128.0, None, A.add, None, ["basep"], ["basep"])
+        else:
+            unpack(t)
+            halve()
+        if t == 1:
+            vtt(T.xc[:], T.xd[:], T.nf[:], A.add, ["xd", "nf"], ["xc"])
+
+        rows = ["row.v"]
+
+        def pv(m):
+            v_compare(T.mp, "mp", PAIR_TILES, po, PAIR_RANGE, m, T.row, rows, "vsc")
+
+        def pc(k):
+            count(T.mp, T.mpq, T.mps, "mp", PAIR_TILES, po, k)
+        vcp(T.ew[:].indirect(lr), T.spb[:], ["spb", "lr%d" % t], ["ew"])
+        act(T.row[:, GB:NP], T.sv80[:, K - (NP - GB):K], AF.Identity, ["sv80", "ew"], ["row.t"], bias=T.ew[:, 0:1])
+        for i in (1, 0, 2, 3, 4):
+            n = min(LEN[i], GA - START[i])
+            act(T.row[:, START[i]:START[i] + n], T.ew[:, 0:n], AF.Identity, ["sv80", "ew"], ["row.%d" % i], bias=T.sv80[:, i:i + 1])
+            rows.append("row.%d" % i)
+        vtt(T.row[:, GA:GB], T.ew[:].indirect(T.pjl[:]), T.sp[:], A.add, ["ew", "pjl", "sp"], ["row.v"])
+        vsc(T.vsc[:, GB:NP], T.m3[:], T.row[:, GB:NP], -BIG, A.add, A.max, ["m3", "row.t"], ["vsc.b"])
+        vsc(T.vsc[:, 80:112], T.m3[:], T.row[:, 80:112], -BIG, A.add, A.max, ["m3", "row.1"], ["vsc.a", "vsc"])
+        vtt(T.yy[:], T.row[:, 112:GB], T.m1[:], A.max, rows + ["m1"], ["yy"])
+        vsc(T.vsc[:, 112:GB], T.d0[:], T.yy[:], 0.0, A.max, A.min, ["d0", "yy"], ["vsc"])
+        s_compares(T.mp, "mp", PAIR_TILES, po, PAIR_RANGE, PAIR_S, T.row, rows,
+                   lambda m: "vsc.b" if m > 20 else ("vsc.a" if m < 7 else "vsc"), T.rsp, "rsp")
+        pv(20)
+        vtt(slot(T.mp, po, 0, 3, 112, GB), T.row[:, 112:GB], T.vsc[:, 112:GB], A.is_gt, rows + ["vsc"], [slot_key("mp", 0, 3)])
+        pv(19)
+        pc(0)
+        for m in PAIR_V[2:]:
+            pv(m)
+        pc(1)
+        vsc(T.dgp[:, 112:GB], T.keep0[:], slot(T.mp, po, 0, 3, 112, GB), 0.0, A.mult, A.add, ["keep0", slot_key("mp", 0, 3)], ["dgp"])
+        for m in PAIR_V:
+            rowsum(T.mp, "mp", PAIR_TILES, po, PAIR_RANGE, PAIR_V, m)
+        partial(23, T.basep, "basep", T.dgp, "dgp")
+        pc(2)
+        partial2(PAIR_V)
+        pc(3)
+        pc(4)
+        finish(23, T.rsp, "rsp", PAIR_S, T.rk[:, 0:23], "rk")
+        if t == 0:
+            unpack(t)
+        for b in range(4):
+            act(T.ts[:, K * b:K * b + K], state(t)[:].indirect(T.off4[:, 6 * b:6 * b + 5]), AF.Copy, tkeys(t) + ["off4.%d" % b], ["ts%d" % b], scale=0.5)
+        if t == 0:
+            halve()
+        for b in range(4):
+            act(T.ess[:, K * b:K * b + K], T.eh[:, C * b:C * b + C].indirect(l5), AF.Copy, ["eh%d" % b, "ll%d" % t], ["ess%d" % b])
+        last = t == R - 1
+        vcp(T.xw[:].indirect(T.rk[:, 0:23]), T.xc[:] if last else T.x0[:], ["rk", "xc"] + xk, ["xw"])
+        vsc(T.ext[:, 0:C], T.keepk[:, 0:C], T.xw[:, 0:C], 0.0, A.mult, A.add, ["keepk", "xw"], ["ext"])
+        vts(T.bl16[:], T.ext[:, 15:C:16], cp, 2.0 ** -17 if last else 2.0 ** -8, A.mult, A.mult, ["ext", "cp"], ["bl16"])
+        vts(T.xi[:], T.ext[:, 15:C:16], cp, None, A.mult, None, ["ext", "cp"], ["xi"])
+        vts(T.xi[:], T.xi[:], 9 if last else 0, 127, A.logical_shift_right, A.bitwise_and, ["xi"], ["xi"])
+        vcp(T.a16[:], T.xi[:], ["xi"], ["a16"])
+
+        for b in range(4):
+            act(T.bg[:, C * b:C * b + C], T.ess[:, K * b:K * b + K].indirect(T.bl16[:]), AF.Copy, ["ess%d" % b, "bl16"], ["bg%d" % b])
+        for b in range(4):
+            vtt(T.zt[:, b:4 * C:4], T.ts[:, K * b:K * b + K].indirect(T.a16[:]), T.bg[:, C * b:C * b + C], A.add,
+                ["ts%d" % b, "a16", "bg%d" % b], ["z%d" % b])
+        vq(T.zq[:], T.zs[:], T.zt[:], ["z%d" % b for b in range(4)], ["zq"])
+        for b in range(4):
+            mm(ps[4 + b][:, 0:C], T.wq[:, 128 * b:128 * b + 128], T.wp[:, 128 * b:128 * b + 128], T.zq[:], T.zs[:], True, True,
+               ["wq", "wp", "zq"], ["ps%d" % (4 + b)])
+        for b in range(4):
+            act(T.rr[:, C * b:C * b + C], ps[4 + b][:, 0:C], AF.Relu, ["ps%d" % (4 + b)], ["rr%d" % b], scale=0.03125)
+        if last:
+            vcp(T.oi[:], T.xw[:, 0:C], ["xw"], ["oi"])
+            vts(T.oi[:], T.oi[:], 511, None, A.bitwise_and, None, ["oi"], ["oi"])
+        else:
+            pick_codes(t + 1)
+            pick_scales(t + 1)
+        for b in range(4):
+            vtt(state(t + 1)[:, b:4 * C:4], T.rr[:, C * b:C * b + C], T.zt[:, b:4 * C:4], A.add, ["rr%d" % b, "z%d" % b], ["t%d.%d" % (t + 1, b)])
+
+    tq, tsc = T.tq3, T.tsc3
+    vq(tq[:], tsc[:], state(R)[:], tkeys(R), ["tq3"])
+    vcp(T.olf[:], T.oi[:], ["oi"], ["olf"])
+    mm(ps[0][:, 0:C], T.vq[:], T.vs[:], tq[:], tsc[:], True, True, ["vq", "tq3"], ["ps0"])
+    dma("y", T.oc[:], u8(tq[:]), "st", ["tq3"])
+    dma("s", T.osc[0:4, :], tsc[0:4, :], "st", ["tq3"])
+    act(T.yf[:], ps[0][:, 0:C], AF.Copy, ["ps0"], ["yf"])
+    dma("y", T.osc[4:8, :], tsc[32:36, :], "st", ["tq3"])
+    dma("y", T.ol[:], T.olf[0:128:16, :], "st", ["olf"])
+    dma("s", T.y[:], T.yf[:], "st", ["yf"])
+    dma("y", T.osc[8:12, :], tsc[64:68, :], "st", ["tq3"])
+    dma("s", T.osc[12:16, :], tsc[96:100, :], "st", ["tq3"])
+
+    known = {q: {} for q in queues}
+    snap, need, waits = [], set(), []
+    for x, (q, fn, deps, kind) in enumerate(ops):
+        want = {}
+        for d in deps:
+            key, val = (ops[d[1]][0], d[1]) if d[0] == "op" else (d[1], d[2])
+            if known[q].get(key, -1) < val:
+                want[key] = max(want.get(key, -1), val)
+        mine = []
+        for key, val in sorted(want.items(), key=lambda kv: -kv[1] if kv[0] in qsem else 0):
+            if known[q].get(key, -1) >= val:
+                continue
+            mine.append((key, val))
+            known[q][key] = val
+            if key in qsem:
+                need.add(val)
+                for k2, v2 in snap[val].items():
+                    if known[q].get(k2, -1) < v2:
+                        known[q][k2] = v2
+        waits.append(mine)
+        snap.append(dict(known[q]))
+    number, cnt = {}, {q: 0 for q in qsem}
+    for x, o in enumerate(ops):
+        if x in need:
+            cnt[o[0]] += 1
+            number[x] = cnt[o[0]]
+    for x, (q, fn, deps, kind) in enumerate(ops):
+        for key, val in waits[x]:
+            if key in qsem:
+                queues[q].wait_ge(T.sem[qsem[key]], number[val])
+            else:
+                queues[q].wait_ge(T.sem[key], val)
+        ins = fn()
+        if x in need:
+            ins.then_inc(T.sem[qsem[q]], 1)
+    for name, val in totals.items():
+        g.wait_ge(T.sem[name], val)

@@ -1,60 +1,113 @@
-from concourse.bass import DstId, RemoteDMATransfer
-from concourse.mybir import dt, AluOpType, ActivationFunctionType
+from concourse.mybir import dt, AluOpType, AxisListType, ActivationFunctionType
 
 C, K, R = 224, 80, 3
 STEP = [1, 2, 4]
 LEN = [K // (i + 1) for i in range(K)]
 START = [sum(LEN[:i]) for i in range(K)]
 NP = sum(LEN)
-BIG = 1.0e29
-KK = 2.0 ** 21
+BIG = 2.0 ** 93
+OFF = 1024.0
+KK = 2.0 ** 26
+MID = 5100
+MAGIC = 1.5 * 2.0 ** 23
 JW = 168
-GA, GB = 176, 336
+GA, GM, GB = 112, 224, 336
+H, W = 96, 128
+UO = 16
+PIECES = [(0, 32), (32, 64), (64, 96), (128, 160), (160, 224), (96, 128)]
+LISTS = [(0, 64), (64, 224)]
 
-OWN_TILES = [(224, [13, 12, 11, "d"]), (160, [10, 9, 8, 7]), (128, [6, 5, 4, 3]), (128, [2, 1])]
-OWN_V = [13, 12, 11, 10]
-OWN_S = [9, 8, 7, 6, 5, 4, 3, 2, 1]
+OWN_TILES = [(224, [13, 12, 11, "d"]), (128, [2, 1]), (128, [6, 5, 4, 3]), (160, [10, 9, 8, 7])]
+OWN_ZERO = [176, 0, 48, 112]
+OWN_V = [13, 12, 11]
+OWN_S = [5, 4, 3, 2, 1, 6, 7, 8, 9, 10]
 OWN_RANGE = {m: (0, 16 * m) for m in range(1, 14)}
-PAIR_TILES = [(336, [22, 21, 20, "d"]), (304, [19, 18, 17, 16]), (240, [15, 14, 13, 12]), (176, [11, 10, 9, 8]), (128, [7, 6, 5])]
+PAIR_TILES = [(336, [22, 21, 20, "d"]), (128, [7, 6, 5]), (304, [19, 18, 17, 16]), (240, [15, 14, 13, 12]), (176, [11, 10, 9, 8])]
+PAIR_ZERO = [320, 0, 256, 192, 128]
 PAIR_V = [20, 19, 18, 17, 16, 15]
-PAIR_S = [22, 21, 5, 6, 14, 13, 12, 11, 10, 9, 8, 7]
+PAIR_S = [22, 21, 5, 6, 7, 14, 13, 12, 11, 10, 9, 8]
 PAIR_RANGE = {m: (0, 16 * m) for m in range(7, 21)}
 PAIR_RANGE.update({5: (0, 80), 6: (16, 80), 21: (0, 328), 22: (0, 328)})
+OWN_CUT, PAIR_CUT = (10, 96), (12, 112)
+SPLIT_SEND = True
 WO = sum(w for w, _ in OWN_TILES)
 WP = sum(w for w, _ in PAIR_TILES)
 
 F, B, I, U, Q, S8 = "float32", "bfloat16", "int32", "uint16", "float8_e4m3fn_x4", "uint8"
 SCRATCH = {}
 for _n, _w, _d in [
-    ("xb", 896, B), ("ub", 512, B), ("vb", 512, B), ("wq", 512, Q), ("wp", 512, S8),
-    ("uq", 128, Q), ("us", 128, S8), ("vq", 128, Q), ("vs", 128, S8), ("urq", 128, Q), ("urs", 128, S8),
-    ("u16q", 16, Q), ("u16s", 16, S8),
-    ("zb", 512, B), ("eb", 2048, B), ("eq", 512, Q), ("es", 512, S8), ("cb", 1024, B), ("cq", 256, Q), ("cs", 256, S8),
-    ("grp", 512, B), ("li", 3, I), ("col", 8, F), ("xm", 32, B), ("b16", 24, F), ("nf", 368, F), ("x0", 368, F),
-    ("xc", 368, F), ("xd", 368, F), ("m1", 224, B), ("m3", 32, B), ("d0", 224, B), ("keep0", 224, B), ("keepk", 336, B),
-    ("tmpa", 96, B), ("dist", 128, F),
-    ("l16", 8, U), ("l2", 8, U), ("l8", 2, U), ("pil", 10, U), ("pjl", 10, U), ("ci", 10, I),
+    ("xb", 4 * C, B), ("ub", 512, B), ("vb", 512, B), ("wq", 512, Q), ("wp", 512, S8),
+    ("uq", W, Q), ("us", W, S8), ("vq", W, Q), ("vs", W, S8), ("urq", W, Q), ("urs", W, S8),
+    ("zb", 516, B), ("eb", 516, B), ("eq", 512, Q), ("es", 512, S8), ("cb", 512, B), ("cq", W, Q), ("cs", W, S8),
+    ("grp", W, B), ("pi", 1, I), ("li", 4, I), ("col", 12, F), ("xm", GB, B), ("xm4", C, B), ("b16", 24, F),
+    ("nf", C, F), ("x0", NP, F), ("xl", NP, F),
+    ("m3", GB, B), ("am", GB, B), ("ym", C, B), ("d0", C, B), ("keep0", C, B), ("k4", C, B),
+    ("l16", 8, U), ("l2", 8, U), ("l8", 2, U), ("pil", 14, U), ("pjl", 14, U),
     ("baseo", 14, F), ("basep", 24, F),
     ("mo", 4 * WO, B), ("moq", WO, Q), ("mos", WO, S8), ("mp", 4 * WP, B), ("mpq", WP, Q), ("mps", WP, S8),
-    ("yy", 224, F), ("vsc", 368, F), ("tau", 2400, B), ("junk", 6 * JW, B), ("dgo", 224, B), ("dgp", 368, B),
-    ("rso", 14, F), ("rsp", 24, F), ("p1", 24, F), ("ext", 368, F), ("yr", 24, F), ("rk", 24, U),
-    ("ow", 224, F), ("oext", 96, F), ("off4", 24, U), ("ssb", 224, F), ("spb", 224, F), ("sv80", 80, F), ("ew", 224, F),
-    ("sp", GB - GA, F), ("row", 368, F), ("xw", 368, F), ("xi", 14, I), ("a16", 14, U), ("bl16", 14, U),
-    ("ts", 320, B), ("eh", 896, B), ("ess", 320, B), ("bg", 896, B), ("zt", 896, B), ("zq", 224, Q), ("zs", 224, S8),
-    ("rr", 896, F), ("oi", 224, I), ("olf", 224, F), ("yf", 224, F),
-    ("rko", 16 * R, U), ("lr", 16 * R, U), ("o16", 8 * R, U), ("ll", 8 * R, U), ("tq3", 224, Q), ("tsc3", 224, S8),
-] + [(n + str(t + k), w, d) for t in range(R) for n, k, w, d in [
-    ("t", 1, 896, B), ("lq", 0, 224, Q), ("ls", 0, 224, S8), ("ulq", 0, 16, Q), ("uls", 0, 16, S8), ("upq", 0, 128, Q),
-    ("ups", 0, 128, S8), ("tq", 0, 224, Q), ("tsc", 0, 224, S8)]]:
+    ("yo", C, F), ("vo", C, F), ("yp", NP, F), ("vp", NP, F), ("tao", 1200, B), ("tap", 2400, B),
+    ("jo", 8 * JW, B), ("jp", 8 * JW, B), ("dgo", C, B), ("dgp", NP, B),
+    ("rso", 14, F), ("rsp", 24, F), ("po", 14, F), ("pp", 24, F), ("qo", 14, F), ("qp", 24, F), ("exo", C, F), ("exq", NP, F),
+    ("yro", 14, F), ("yrp", 24, F), ("rk", 24, U), ("ow", C, F), ("oex", K, F), ("oe1", K, F), ("o1", 6, U), ("ssb", C, F), ("spb", C, F), ("sw", C, F),
+    ("ew", C, F), ("sp", NP, F), ("row", NP, F), ("xw", NP, F), ("ex4", C, F), ("xi", 56, I), ("xj", 56, I), ("xk", 56, I),
+    ("a4", 56, U), ("b4", 56, U),
+    ("ts", 4 * K, B), ("eh", 4 * C, B), ("ess", 4 * K, B), ("bg", 4 * C, B), ("zt", 4 * C, B), ("zq", 2 * W, Q), ("zs", 2 * W, S8),
+    ("rr", 4 * C, F), ("olt", C, F), ("olf", C, F), ("yf", C, F),
+    ("rko", 16 * R, U), ("lr", 16 * R, U), ("o4", 24 * R, U), ("ll", 24 * R, U),
+    ("tq3", UO + C, Q), ("tsc3", UO + C, S8),
+] + [(n + str(t), w, d) for t in range(R) for n, w, d in [
+    ("lq", UO + C, Q), ("ls", UO + C, S8), ("upq", W, Q), ("ups", W, S8), ("tq", UO + C, Q), ("tsc", UO + C, S8)]]:
     SCRATCH[_n] = ("sbuf", [128, _w], _d)
 for _t in range(8):
     SCRATCH["ps%d" % _t] = ("psum", [128, 512], F)
 
-SEMAPHORES = (["qv", "qs", "qp", "qg", "ldx", "ldu", "ldv", "ldw", "lds", "loc", "st"]
-              + [n + str(t) for n in ("big", "lst", "rnk", "ua") for t in range(R)])
+SEMAPHORES = ["qv", "qs", "qp", "qg", "loc", "st"] + ["d%d" % k for k in range(40)]
 
 A = AluOpType
 AF = ActivationFunctionType
+SIZE = {F: 4, B: 2, I: 4, U: 2, Q: 4, S8: 1}
+HOP = 250
+FAR = 1500
+
+
+def schedule(ops):
+    n = len(ops)
+    succ = [[] for _ in ops]
+    for x, o in enumerate(ops):
+        for d, soft in o[2]:
+            succ[d].append((x, soft))
+    chain = [0] * n
+    for x in range(n - 1, -1, -1):
+        chain[x] = ops[x][3] + max([(0 if soft else ops[x][4]) + chain[y] for y, soft in succ[x]] + [ops[x][4]])
+    left = [len(o[2]) for o in ops]
+    ready = [0] * n
+    free, cand = {}, {}
+    for x, o in enumerate(ops):
+        free[o[0]] = 0
+        cand.setdefault(o[0], [])
+        if not left[x]:
+            cand[o[0]].append(x)
+    order = []
+    while len(order) < n:
+        q = min((q for q in cand if cand[q]), key=lambda q: max(free[q], min(ready[x] for x in cand[q])))
+        now = max(free[q], min(ready[x] for x in cand[q]))
+        pick = max((x for x in cand[q] if ready[x] <= now), key=lambda x: (chain[x], -x))
+        for y in sorted((x for x in cand[q] if now < ready[x] < now + ops[pick][3] and chain[x] > chain[pick]), key=lambda x: -chain[x])[:1]:
+            fits = [x for x in cand[q] if ready[x] <= now and now + ops[x][3] <= ready[y] + 20]
+            if fits:
+                pick = max(fits, key=lambda x: (chain[x], -x))
+            elif max(ready[y] + chain[y], ready[y] + ops[y][3] + chain[pick]) < max(now + chain[pick], now + ops[pick][3] + chain[y]):
+                pick = y
+        start = max(now, ready[pick])
+        free[q] = start + ops[pick][3]
+        cand[q].remove(pick)
+        order.append(pick)
+        for y, soft in succ[pick]:
+            ready[y] = max(ready[y], free[q] + (0 if soft else ops[pick][4]))
+            left[y] -= 1
+            if not left[y]:
+                cand[ops[y][0]].append(y)
+    return order
 
 
 def rank_program(g, core, T, topo):
@@ -64,493 +117,435 @@ def rank_program(g, core, T, topo):
     queues = {"v": g.vector, "s": g.scalar, "p": g.tensor, "g": g, "y": g.sync}
     qsem = {"v": "qv", "s": "qs", "p": "qp", "g": "qg"}
     ops = []
-    writer, readers, totals = {}, {}, {"loc": 0}
+    wrote, read = {}, {}
+    counts = {"loc": 0, "st": 0}
 
-    def op(q, fn, reads=(), writes=(), kind="c"):
-        deps = []
-        me = len(ops)
-        for k in reads:
-            if k in writer:
-                deps.append(writer[k])
-            if k.startswith("ps"):
-                deps.extend(d for d in readers.get(k, []) if ops[d[1]][0] != q)
-        for k in writes:
-            if k in writer and not (q == "p" and writer[k][0] == "op" and ops[writer[k][1]][0] == "p"):
-                deps.append(writer[k])
-            deps.extend(readers.get(k, []))
-        ops.append([q, fn, deps, kind])
-        if kind == "c":
-            for k in reads:
-                readers.setdefault(k, []).append(("op", me))
-            for k in writes:
-                writer[k] = ("op", me)
-                readers[k] = []
+    def X(name, lo=0, hi=None, step=1):
+        where, shape, d = SCRATCH[name]
+        hi = shape[1] if hi is None else hi
+        cols = range(lo, hi, step)
+        mask = 1 if where == "psum" else sum(1 << c for c in cols) if step > 1 else ((1 << (hi - lo)) - 1) << lo
+        return (T[name][:, lo:hi:step] if step > 1 else T[name][:, lo:hi], len(cols), [(name, mask)], SIZE[d] == 2, where)
 
-    def arrives(keys, sem, count):
-        for k in keys:
-            writer[k] = ("sem", sem, count)
+    def by(win, off, cast=None):
+        a = win[0].bitcast(cast) if cast else win[0]
+        return (a.indirect(off[0]), 16 * off[1], win[2] + off[2], False, "list")
 
-    def dma(q, out, in_, sem, reads=(), writes=()):
-        totals[sem] = totals.get(sem, 0) + 16
-        op(q, lambda: queues[q].dma_start(out, in_).then_inc(T.sem[sem], 16), reads, (), "d")
-        arrives(writes, sem, totals[sem])
+    def val(a):
+        return a[0] if isinstance(a, tuple) else a
+
+    def op(q, fn, ins, outs, cycles, lag=HOP, sem=None, after=()):
+        me, deps = len(ops), {x: False for x in after}
+        rd = [r for a in ins if isinstance(a, tuple) for r in a[2]]
+        wr = [a[2][0] for a in outs]
+        rd += [r for a in outs for r in a[2][1:]]
+        for name, mask in rd:
+            deps.update({x: False for m, x in wrote.get(name, []) if m & mask})
+            if name.startswith("ps"):
+                deps.update({x: False for m, x in read.get(name, []) if ops[x][0] != q})
+        for name, mask in wr:
+            for m, x in wrote.get(name, []):
+                if m & mask:
+                    deps[x] = q == "p" and ops[x][0] == "p"
+            deps.update({x: False for m, x in read.get(name, []) if m & mask})
+        ops.append([q, fn, sorted(deps.items()), cycles, lag, sem])
+        for name, mask in rd:
+            read.setdefault(name, []).append((mask, me))
+        for name, mask in wr:
+            wrote[name] = [(m & ~mask, x) for m, x in wrote.get(name, []) if m & ~mask] + [(mask, me)]
+            read[name] = [(m & ~mask, x) for m, x in read.get(name, []) if m & ~mask]
+        return me
+
+    turn = {}
+
+    def in_turn(name, again):
+        if again:
+            ops[-1][2].append((turn[name], True))
+        turn[name] = len(ops) - 1
 
     V, S, P = g.vector, g.scalar, g.tensor
 
-    def vts(out, in0, s1, s2, o0, o1, r, w):
-        if o1 is None:
-            op("v", lambda: V.tensor_scalar(out, in0, s1, None, o0), r, w)
-        else:
-            op("v", lambda: V.tensor_scalar(out, in0, s1, s2, o0, o1), r, w)
+    def cost(out, ins, rate=1.0):
+        if out[4] == "list":
+            return 60 + 3.8 * out[1]
+        if ins[0][4] == "list":
+            return 70 + 1.56 * out[1]
+        return max(64, out[1] * rate * (0.5 if out[3] and all(a[3] for a in ins) else 1))
 
-    def vtt(out, a, b, o, r, w):
-        op("v", lambda: V.tensor_tensor(out, a, b, o), r, w)
+    def vts(out, a, s1, s2, o0, o1=None):
+        more = () if o1 is None else (o1,)
+        op("v", lambda: V.tensor_scalar(out[0], a[0], val(s1), val(s2), o0, *more), [a, s1, s2], [out], cost(out, [a]))
 
-    def vcp(out, a, r, w):
-        op("v", lambda: V.tensor_copy(out, a), r, w)
+    def vtt(out, a, b, o):
+        both = a[4] == b[4] == "sbuf"
+        op("v", lambda: V.tensor_tensor(out[0], a[0], b[0], o), [a, b], [out], max(64, 2 * out[1]) if both else cost(out, [a, b]))
 
-    def vms(out, c, w):
-        op("v", lambda: V.memset(out, c), (), w)
+    def vcp(out, a):
+        op("v", lambda: V.tensor_copy(out[0], a[0]), [a], [out], cost(out, [a]))
 
-    def vsc(out, d0, d1, init, o0, o1, r, w):
-        op("v", lambda: V.tensor_tensor_scan(out, d0, d1, init, o0, o1), r, w)
+    def vms(out, c):
+        op("v", lambda: V.memset(out[0], c), [], [out], cost(out, [out]))
 
-    def vq(out, sc, a, r, w):
-        op("v", lambda: V.quantize_mx(out, sc, a), r, w)
+    def vsc(out, d0, d1, init, o0, o1):
+        op("v", lambda: V.tensor_tensor_scan(out[0], d0[0], d1[0], init, o0, o1), [d0, d1], [out], cost(out, [d0, d1]))
 
-    def act(out, a, f, r, w, **kw):
-        op("s", lambda: S.activation(out, a, f, **kw), r, w)
+    def vq(q, s, lo, n, a):
+        out, sc = X(q, lo, lo + n), X(s, lo, lo + n)
+        op("v", lambda: V.quantize_mx(out[0], sc[0], a[0]), [a], [out, sc], 15 + 0.265 * a[1])
 
-    def mm(out, lq, ls, rq, rs, start, stop, r, w):
-        op("p", lambda: P.matmul_mx(out, lq, ls, rq, rs, start, stop), r, w)
+    def act(out, a, f, bias=0.0, scale=1.0, acc=None):
+        kw = {} if acc is None else {"accum_out": acc[0]}
+        op("s", lambda: S.activation(out[0], a[0], f, bias=val(bias), scale=val(scale), **kw), [a, bias, scale],
+           [out] + ([] if acc is None else [acc]), (cost(out, [a]) if a[4] == "list" else max(64, out[1])) + (0 if acc is None else 24))
 
-    def iota(out, pat, base, cm, w, fl=True):
-        if fl:
-            op("g", lambda: g.iota(out, pat, base, cm, allow_small_or_imprecise_dtypes=True), (), w)
-        else:
-            op("g", lambda: g.iota(out, pat, base, cm), (), w)
+    def pick(q2, s2, lo, q, s, n, off):
+        out, a = X(q2, lo, lo + 16 * off[1]), by(X(q, 0, n), off, dt.uint32)
+        op("v", lambda: V.tensor_copy(out[0].bitcast(dt.uint32), a[0]), [a], [out], cost(out, [a]))
+        so, sa = X(s2, lo, lo + 16 * off[1]), by(X(s, 0, n), off)
+        op("s", lambda: S.activation(so[0], sa[0], AF.Copy), [sa], [so], cost(so, [sa]))
+
+    def mm(bank, lq, ls, l0, rq, rs, r0, n, start=True, stop=True):
+        a = [X("ps%d" % bank, 0, n), X(lq, l0, l0 + W), X(ls, l0, l0 + W), X(rq, r0, r0 + n), X(rs, r0, r0 + n)]
+        op("p", lambda: P.matmul_mx(*[x[0] for x in a], start, stop), a[1:], a[:1], n + 16)
+
+    def iota(out, pat, base, cm=0):
+        kw = {} if SCRATCH[out[2][0][0]][2] == I else {"allow_small_or_imprecise_dtypes": True}
+        op("g", lambda: g.iota(out[0], pat, base, cm, **kw), [], [out], 160 + 2 * out[1])
+
+    def new_sem(n):
+        name = "d%d" % (len(counts) - 2)
+        counts[name] = n
+        return name
+
+    def raw(a):
+        return a[0].bitcast(dt.uint8) if SCRATCH[a[2][0][0]][2] == Q else a[0]
+
+    def row_bytes(a):
+        return a[1] * SIZE[SCRATCH[a[2][0][0]][2]]
+
+    def load(q, out, src, after=()):
+        sem = new_sem(16)
+        ins = [src] if isinstance(src, tuple) else []
+        op(q, lambda: queues[q].dma_start(raw(out), val(src)).then_inc(T.sem[sem], 16), ins, [out], 60, FAR + row_bytes(out) // 2, sem, after)
+
+    def store(q, out, a, part=None):
+        counts["st"] += 16
+        src = raw(a) if part is None else part
+        op(q, lambda: queues[q].dma_start(out, src).then_inc(T.sem.st, 16), [a], [], 60, FAR + row_bytes(a) // 2, "st")
 
     peers = [T.cores[rank ^ STEP[t]] for t in range(R)]
 
-    def send(t, out, in_, sem, reads, lands):
+    def send(t, out, a):
         rid, pid = topo.addr(peers[t], core)
-        m = topo.mask(core, peers[t])
-        totals["loc"] += len(topo.engines(core, peers[t]))
-        op("g", lambda: g.remote_dma(out, in_, T.sem[sem], T.sem.loc, pid, rid, m), reads, (), "d")
-        totals[sem] = totals.get(sem, 0) + len(topo.engines(peers[t], core))
-        arrives(lands, sem, totals[sem])
+        counts["loc"] += len(topo.engines(core, peers[t]))
+        sem = new_sem(len(topo.engines(peers[t], core)))
+        op("g", lambda: g.remote_dma(raw(out), raw(a), T.sem[sem], T.sem.loc, pid, rid, topo.mask(core, peers[t])), [a], [out],
+           360, FAR + row_bytes(a) + (FAR if t == 0 and a[1] > W else 0), sem)
 
-    def u8(ap):
-        return ap.bitcast(dt.uint8)
+    lcol, gcol, qcol, rcol, offc, c1, cp, cpo, cpb = [X("col", i, i + 1) for i in range(9)]
 
-    def u32(ap):
-        return ap.bitcast(dt.uint32)
-
-    ps = [T["ps%d" % i] for i in range(8)]
-    lcol, l1col, gcol, npcol, cp, kp, cp4, kp0 = [T.col[:, i:i + 1] for i in range(8)]
-    grpk = ["grp%d" % k for k in range(8)]
-
-    dma("y", T.ub[:], T.u[:], "ldu", (), ["ub"])
-    dma("s", T.xb[:], T.x[:], "ldx", (), ["t0"])
-    dma("y", u8(T.wq[:]), T.wc[:], "ldw", ["t0"], ["wq"])
-    dma("y", T.wp[:], T.ws[:], "lds", (), ["wp"])
-    dma("y", T.vb[:], T.v[:], "ldv", (), ["vb"])
-
-    iota(T.li[:, 2:3], [[0, 1]], 0, 1, ["pi"], False)
-    iota(T.xm[:], [[0, 2], [1, 16]], 0, 0, ["xm"])
-    iota(T.b16[:], [[16, 24]], 0, 0, ["b16"])
-    iota(T.nf[:], [[1, NP]], 0, 0, ["nf"])
-    segs = []
-    i = 0
-    while i < K:
-        j = i
-        while j < K and LEN[j] == LEN[i]:
-            j += 1
-        segs.append((i, j - i))
-        i = j
-    xk = ["x0.%d" % i for i, n in segs]
-
-    def seg_iota(i, n):
-        iota(T.x0[:, START[i]:START[i] + n * LEN[i]], [[1, n], [256, LEN[i]]], i, 0, ["x0.%d" % i])
-    for i, n in segs[5:]:
-        seg_iota(i, n)
-
-    vms(T.zb[:], 0.0, ["zb"])
-    vms(T.d0[:], -BIG, ["d0"])
-    vms(T.keep0[:], 1.0, ["keep0"])
-    vts(T.li[:, 0:1], T.li[:, 2:3], 15, None, A.bitwise_and, None, ["pi"], ["li0"])
-    vts(T.li[:, 1:2], T.li[:, 2:3], 4, None, A.logical_shift_right, None, ["pi"], ["li1"])
-    for k in range(8):
-        vms(T.grp[:, 64 * k:64 * k + 64], float(k), ["grp%d" % k])
-    vcp(lcol, T.li[:, 0:1], ["li0"], ["lcol"])
-    vcp(gcol, T.li[:, 1:2], ["li1"], ["gcol"])
-    vms(T.d0[:, 0:224:16], BIG, ["d0"])
-    vms(T.keep0[:, 0:224:16], 0.0, ["keep0"])
-    vts(l1col, lcol, 1.0, None, A.add, None, ["lcol"], ["l1col"])
-    vts(T.l8[:, 0:1], lcol, 8.0, None, A.mult, None, ["lcol"], ["l8"])
-    vts(T.tmpa[:, 0:32], T.xm[:], lcol, -2 * BIG, A.is_equal, A.mult, ["xm", "lcol"], ["tmp0"])
-    vts(T.tmpa[:, 32:64], T.xm[:], l1col, KK, A.is_equal, A.mult, ["xm", "l1col"], ["tmp1"])
-    vts(T.tmpa[:, 64:96], T.xm[:], lcol, None, A.not_equal, None, ["xm", "lcol"], ["tmp2"])
-    vts(T.m1[:, 0:32], T.tmpa[:, 0:32], BIG, None, A.add, None, ["tmp0"], ["m1"])
-    vcp(T.l16[:], T.b16[:, 0:8], ["b16"], ["l16"])
-    vtt(T.keepk[:, 0:32], T.tmpa[:, 32:64], T.tmpa[:, 64:96], A.max, ["tmp1", "tmp2"], ["keepk"])
-    vts(T.cb[:, 0:512], T.grp[:], gcol, None, A.is_equal, None, ["gcol"] + grpk, ["cb0"])
-    vts(cp, lcol, 15.0, 1.0 / KK, A.is_ge, A.max, ["lcol"], ["cp"])
-    vts(kp0, lcol, 15.0, KK, A.is_lt, A.mult, ["lcol"], ["kp0"])
-    vts(npcol, T.li[:, 2:3], -1.0, None, A.mult, None, ["pi"], ["npcol"])
-    vts(T.baseo[:], T.b16[:, 0:14], lcol, 0.3, A.add, A.add, ["b16", "lcol"], ["baseo"])
-    vts(kp, kp0, 1.0, None, A.max, None, ["kp0"], ["kp"])
-    vts(T.l2[:], T.b16[:, 0:8], 0.125, None, A.mult, None, ["b16"], ["l2"])
-    lo = min(OWN_V)
-    vts(T.baseo[:, lo:lo + len(OWN_V)], T.baseo[:, lo:lo + len(OWN_V)], -128.0, None, A.add, None, ["baseo"], ["baseo"])
+    def ps(bank, lo, hi):
+        return X("ps%d" % bank, lo, hi)
 
     def tile_offsets(tiles):
         return [sum(w for w, _ in tiles[:k]) for k in range(len(tiles))]
 
-    def slot_key(name, k, t):
-        return "%s.%d.%d" % (name, k, t)
+    load("y", X("ub"), T.u[:])
+    load("s", X("xb"), T.x[:])
 
-    def tile_keys(name, k):
-        return [slot_key(name, k, t) for t in range(4)]
+    iota(X("pi"), [[0, 1]], 0, 1)
+    iota(X("b16"), [[16, 24]], 0)
+    iota(X("xm"), [[0, GB // 16], [1, 16]], 0)
+    iota(X("grp"), [[1, 8], [0, 16]], 0)
+    iota(X("xm4"), [[0, C // 4], [1, 4]], 0)
+    iota(X("nf"), [[1, C]], 0)
+    for i in range(K):
+        if i == 0 or LEN[i] != LEN[i - 1]:
+            n = LEN.count(LEN[i])
+            iota(X("x0", START[i], START[i] + n * LEN[i]), [[1, n], [1024, LEN[i]]], i)
+        if i == 0 or LEN[i - 1] > 1:
+            step, n = (16384 + 128, LEN[i]) if LEN[i] > 1 else (16384 + 1, K - i)
+            iota(X("xl", START[i], START[i] + n), [[step, n]], 16384 * START[i] + i - MID)
 
-    oo, po = tile_offsets(OWN_TILES), tile_offsets(PAIR_TILES)
+    vms(X("zb"), 0.0)
+    vms(X("d0"), BIG)
+    vms(X("d0", 0, C, 16), -BIG)
+    vms(X("rso"), 0.0)
+    vms(X("rsp"), 0.0)
+    vms(X("exq", GB, NP), 0.0)
+    vts(X("li", 0, 1), X("pi"), 15, None, A.bitwise_and)
+    vts(X("li", 1, 2), X("pi"), 4, None, A.logical_shift_right)
+    vts(X("li", 2, 3), X("pi"), 2, 3, A.logical_shift_right, A.bitwise_and)
+    vts(X("li", 3, 4), X("pi"), 3, None, A.bitwise_and)
+    vcp(X("col", 0, 4), X("li"))
+    vcp(X("l16"), X("b16", 0, 8))
+    vts(X("l8", 0, 1), lcol, 8.0, None, A.mult)
+    vts(X("l2"), X("b16", 0, 8), 0.125, None, A.mult)
+    vts(X("m3"), X("xm"), lcol, -BIG, A.is_equal, A.mult)
+    vts(offc, lcol, -OFF, 15 * OFF, A.mult, A.add)
+    vts(c1, lcol, OFF - 1, -15 * (OFF - 1), A.mult, A.add)
+    for k in range(4):
+        vts(X("cb", k, 512, 4), X("grp"), gcol, None, A.is_equal)
+    vq("cq", "cs", 0, W, X("cb"))
+    vts(X("col", 9, 12), X("xm", 0, 3), qcol, 1.0 / KK, A.is_lt, A.max)
+    op("v", lambda: V.tensor_reduce(cp[0], T.col[:, 9:12], AxisListType.X, A.mult), [X("col", 9, 12)], [cp], 64)
+    vts(cpo, cp, 4.0, None, A.mult)
+    vts(cpb, cp, 1.0 / 256, None, A.mult)
+    vts(X("k4"), X("xm4"), qcol, KK, A.not_equal, A.mult)
+    lo = min(PAIR_V)
+    vts(X("baseo"), X("b16", 0, 14), c1, None, A.add)
+    vts(X("pp", 0, 7), X("b16", 0, 7), lcol, offc, A.add, A.subtract)
+    vts(X("pp", 21, 23), X("b16", 21, 23), lcol, None, A.add)
+    vts(X("basep", 7, lo), X("b16", 7, lo), c1, None, A.add)
+    vts(X("basep", lo, 21), X("b16", lo, 21), c1, -128.0, A.add, A.add)
+    act(X("ym"), X("m3", 0, C), AF.Identity, -BIG, -33.0)
+    act(X("am"), X("m3"), AF.Identity, OFF, 65.0 * OFF / BIG)
+    act(X("keep0"), X("d0"), AF.Relu, 0.0, 1.0 / BIG)
+    op("g", lambda: g.affine_select(T.eb[:], T.zb[:], [[1, 516]], A.not_equal, 1.0, -3, -4), [X("zb")], [X("eb")], 205 + 2 * 516)
+    for b in range(4):
+        vq("eq", "es", W * b, W, X("eb", 3 - b, 515 - b))
+    act(X("olt"), X("x0", GA, GB), AF.Copy, 0.0, 1.0 / 128)
+    vsc(X("olf"), X("am", 0, C), X("olt"), 0.0, A.add, A.max)
+    vts(X("xi", 0, 14), X("olf", 15, C, 16), offc, 128.0, A.subtract, A.mult)
+    vts(X("pjl"), X("olf", 15, C, 16), offc, 0.125, A.subtract, A.mult)
+    vts(X("xk", 0, 14), X("xi", 0, 14), 127, None, A.bitwise_and)
+    vcp(X("pil"), X("xk", 0, 14))
 
-    def zero(out, n, w):
-        act(out, T.zb[:, 0:n], AF.Copy, ["zb"], w)
+    OWN = dict(m="mo", q="moq", s="mos", tiles=OWN_TILES, offs=tile_offsets(OWN_TILES), rng=OWN_RANGE, v=OWN_V, y="yo", val="vo",
+               tau="tao", junk="jo", dg="dgo", rs="rso", p="po", p2="qo", ext="exo", yr="yro", init=0.0, nb=14,
+               cut=OWN_CUT[0], y0=OWN_CUT[1], bank=3)
+    PAIR = dict(m="mp", q="mpq", s="mps", tiles=PAIR_TILES, offs=tile_offsets(PAIR_TILES), rng=PAIR_RANGE, v=PAIR_V, y="yp", val="vp",
+                tau="tap", junk="jp", dg="dgp", rs="rsp", p="pp", p2="qp", ext="exq", yr="yrp", init=-128.0, nb=23,
+                cut=PAIR_CUT[0], y0=PAIR_CUT[1], bank=0)
 
-    def zero_tile(buf, name, tiles, offs, k, lo):
-        n = 4 * (tiles[k][0] - lo)
-        zero(buf[:, 4 * (offs[k] + lo):4 * (offs[k] + lo) + n], n, tile_keys(name, k))
+    def zeros(Z, lows):
+        return [(4 * (Z["offs"][k] + lo), 4 * (Z["offs"][k] + Z["tiles"][k][0])) for k, lo in enumerate(lows)]
+    for a, b in zeros(OWN, OWN_ZERO):
+        act(X("mo", a, b), X("zb", 0, b - a), AF.Copy)
+    for a, b in zeros(PAIR, PAIR_ZERO) + [(0, 4 * GA)]:
+        load("y", X("mp", a, b), X("zb", 0, b - a))
+    load("y", X("zt", 4 * H, 4 * W), X("zb", 0, 4 * (W - H)))
 
-    for k, lo in enumerate([176, 112, 48, 0]):
-        zero_tile(T.mo, "mo", OWN_TILES, oo, k, lo)
-    zero(T.rso[:], 14, ["rso"])
-    for n in (32, 64, 128, 256):
-        if n < C:
-            act(T.m1[:, n:min(2 * n, C)], T.m1[:, 0:min(n, C - n)], AF.Copy, ["m1"], ["m1"])
-        act(T.keepk[:, n:min(2 * n, GB)], T.keepk[:, 0:min(n, GB - n)], AF.Copy, ["keepk"], ["keepk"])
-    act(T.cb[:, 512:1024], T.cb[:, 0:512], AF.Copy, ["cb0"], ["cb1"])
-    act(T.cb[:, 515:1024:4], T.cb[:, 3:512:4], AF.Copy, ["cb0"], ["cb1"], scale=-1.0)
+    def slot(Z, m, lo, hi):
+        k = [m in bl for w, bl in Z["tiles"]].index(True)
+        t = Z["tiles"][k][1].index(m)
+        return X(Z["m"], 4 * (Z["offs"][k] + lo) + t, 4 * (Z["offs"][k] + hi - 1) + t + 1, 4)
 
-    def place_of(tiles, m):
-        for k, (w, bl) in enumerate(tiles):
-            if m in bl:
-                return k, bl.index(m)
+    def mine(Z, m):
+        return X(Z["val"], 16 * m + 15, 16 * m + 16)
 
-    def slot(buf, offs, k, t, lo, hi):
-        return buf[:, 4 * (offs[k] + lo) + t:4 * (offs[k] + hi - 1) + t + 1:4]
+    def in_block(Z, lo, hi, src):
+        vsc(X(Z["y"], lo, hi), X("ym", 0, hi - lo), src, 0.0, A.add, A.min)
+        vsc(X(Z["val"], lo, hi), X("d0", 0, hi - lo), X(Z["y"], lo, hi), 0.0, A.min, A.max)
+        vtt(slot(Z, "d", lo, hi), src, X(Z["val"], lo, hi), A.is_le)
+        vsc(X(Z["dg"], lo, hi), X("keep0", 0, hi - lo), slot(Z, "d", lo, hi), 0.0, A.mult, A.add)
 
-    def rowsum(buf, name, tiles, offs, rng, vblocks, m):
-        k, t = place_of(tiles, m)
-        lo, hi = rng[m]
-        h = (hi - lo) // 2
-        x = sorted(vblocks).index(m)
-        vsc(T.junk[:, (x + 1) * JW - h:(x + 1) * JW], slot(buf, offs, k, t, lo, lo + h), slot(buf, offs, k, t, lo + h, hi),
-            -128.0, A.add, A.add, [slot_key(name, k, t)], ["junk%d" % x])
+    def compares(Z, sblocks, vsrc, ssrc):
+        pos = 0
+        for m in sblocks:
+            lo, hi = Z["rng"][m]
+            act(X(Z["tau"], pos, pos + hi - lo), ssrc(m, lo, hi), AF.Sign, mine(Z, m), -1.0)
+            act(slot(Z, m, lo, hi), X(Z["tau"], pos, pos + hi - lo), AF.Relu, acc=X(Z["rs"], m, m + 1))
+            pos += hi - lo
+        for m in Z["v"]:
+            lo, hi = Z["rng"][m]
+            h, x = (hi - lo) // 2, sorted(Z["v"]).index(m)
+            vts(slot(Z, m, lo, hi), vsrc(lo, hi), mine(Z, m), None, A.is_lt)
+            vsc(X(Z["junk"], (x + 1) * JW - h, (x + 1) * JW), slot(Z, m, lo, lo + h), slot(Z, m, lo + h, hi), Z["init"], A.add, A.add)
 
-    def v_compare(buf, name, tiles, offs, rng, m, src, skeys, vkey):
-        k, t = place_of(tiles, m)
-        lo, hi = rng[m]
-        vts(slot(buf, offs, k, t, lo, hi), src[:, lo:hi], T.vsc[:, 16 * m + 15:16 * m + 16], None, A.is_lt, None,
-            skeys + [vkey], [slot_key(name, k, t)])
+    def places(Z, base, lo, hi, out, o0):
+        nb, v0, nv, cut, y0 = Z["nb"], min(Z["v"]), len(Z["v"]), Z["cut"], Z["y0"]
+        high = [k for k, (w, bl) in enumerate(Z["tiles"]) if w > 16 * cut]
+        for k, (w, bl) in enumerate(Z["tiles"]):
+            o = Z["offs"][k]
+            vq(Z["q"], Z["s"], o, w, X(Z["m"], 4 * o, 4 * (o + w)))
+            if k in high:
+                mm(Z["bank"], "cq", "cs", 0, Z["q"], Z["s"], o + y0, w - y0, k == high[0], k == high[-1])
+            if cut:
+                mm(1, "cq", "cs", 0, Z["q"], Z["s"], o, min(w, 16 * cut), k == 0, k == len(Z["tiles"]) - 1)
+        vtt(X(Z["p"], lo, hi), X(base, lo, hi), X(Z["dg"], 16 * lo + 15, 16 * hi, 16), A.subtract)
+        vtt(X(Z["p"], v0, v0 + nv), X(Z["p"], v0, v0 + nv), X(Z["junk"], JW - 1, nv * JW, JW), A.subtract)
+        for a, b, src in [(cut, nb, ps(Z["bank"], 16 * cut - y0, min(16 * nb, GB) - y0)), (0, cut, ps(1, 0, 16 * cut))][:2 if cut else 1]:
+            vtt(X(Z["p2"], a, b), X(Z["p"], a, b), X(Z["rs"], a, b), A.subtract)
+            vsc(X(Z["ext"], 16 * a, 16 * a + src[1]), X("am", 0, src[1]), src, 0.0, A.add, A.max)
+            vtt(X(Z["yr"], a, b), X(Z["ext"], 16 * a + 15, 16 * b, 16), X(Z["p2"], a, b), A.add)
+            vcp(X(out, o0 + a, o0 + b), X(Z["yr"], a, b))
 
-    def s_compares(buf, name, tiles, offs, rng, blocks, src, skeys, vkeys, rs, rkey):
-        pos, o = {}, 0
-        for m in blocks:
-            pos[m] = o
-            o += rng[m][1] - rng[m][0]
+    def parts(Z):
+        return [(Z["cut"], Z["nb"]), (0, Z["cut"])][:2 if Z["cut"] else 1]
 
-        def one(m):
-            lo, hi = rng[m]
-            act(T.tau[:, pos[m]:pos[m] + hi - lo], src[:, lo:hi], AF.Sign, skeys + [vkeys(m)], ["tau%d" % blocks.index(m)],
-                bias=T.vsc[:, 16 * m + 15:16 * m + 16], scale=-1.0)
-
-        def two(m):
-            lo, hi = rng[m]
-            k, t = place_of(tiles, m)
-            act(slot(buf, offs, k, t, lo, hi), T.tau[:, pos[m]:pos[m] + hi - lo], AF.Relu, ["tau%d" % blocks.index(m), rkey],
-                [slot_key(name, k, t), rkey + ".%d" % m], accum_out=rs[:, m:m + 1])
-        one(blocks[0])
-        for x in range(1, len(blocks)):
-            one(blocks[x])
-            two(blocks[x - 1])
-        two(blocks[-1])
-
-    def count(buf, bq, bs, name, tiles, offs, k):
-        w = tiles[k][0]
-        vq(bq[:, offs[k]:offs[k] + w], bs[:, offs[k]:offs[k] + w], buf[:, 4 * offs[k]:4 * (offs[k] + w)], tile_keys(name, k), [name + "q%d" % k])
-        c = 128 if k == 0 else 0
-        mm(ps[2][:, 0:w], T.cq[:, c:c + 128], T.cs[:, c:c + 128], bq[:, offs[k]:offs[k] + w], bs[:, offs[k]:offs[k] + w],
-           k == 0, k == len(tiles) - 1, ["cq", name + "q%d" % k], ["ps2"])
-
-    def partial(nb, base, bkey, dg, dkey):
-        vtt(T.p1[:, 0:nb], base[:, 0:nb], dg[:, 15:16 * nb:16], A.add, [bkey, dkey], ["p1"])
-
-    def partial2(vblocks):
-        lo, n = min(vblocks), len(vblocks)
-        vtt(T.p1[:, lo:lo + n], T.p1[:, lo:lo + n], T.junk[:, JW - 1:n * JW:JW], A.subtract, ["p1"] + ["junk%d" % x for x in range(n)], ["p1"])
-
-    def finish(nb, rs, rkey, sblocks, out, okey):
-        vtt(T.p1[:, 0:nb], T.p1[:, 0:nb], rs[:, 0:nb], A.subtract, ["p1", rkey] + [rkey + ".%d" % m for m in sblocks], ["p1"])
-        vts(T.p1[:, 0:nb], T.p1[:, 0:nb], kp, None, A.mult, None, ["p1", "kp"], ["p1"])
-        n = min(16 * nb, GB)
-        vsc(T.ext[:, 0:n], T.keepk[:, 0:n], ps[2][:, 0:n], 0.0, A.mult, A.add, ["keepk", "ps2"], ["ext"])
-        vtt(T.yr[:, 0:nb], T.ext[:, 15:16 * nb:16], T.p1[:, 0:nb], A.add, ["ext", "ext0", "p1"], ["yr"])
-        vts(out, T.yr[:, 0:nb], cp, None, A.mult, None, ["yr", "cp"], [okey])
-
-    def state(t):
-        return T.xb if t == 0 else T["t%d" % t]
-
-    def tkeys(t):
-        return ["t0"] if t == 0 else ["t%d.%d" % (t, b) for b in range(4)]
-
-    def pick_codes(t):
-        vcp(u32(T["upq%d" % t][:]), u32(T["ulq%d" % t][:]).indirect(T.l2[:]), ["ul%d" % t, "l2"], ["upq%d" % t])
-
-    def pick_scales(t):
-        act(T["ups%d" % t][:], T["uls%d" % t][:].indirect(T.l2[:]), AF.Copy, ["ul%d" % t, "l2"], ["ups%d" % t])
-
-    def unpack(t):
-        for b in range(4):
-            mm(ps[4 + b][:, 0:C], T.eq[:, 128 * b:128 * b + 128], T.es[:, 128 * b:128 * b + 128], T["lq%d" % t][:], T["ls%d" % t][:],
-               True, True, ["eq", "lq%d" % t], ["ps%d" % (4 + b)])
-
-    def halve():
-        for b in range(4):
-            act(T.eh[:, C * b:C * b + C], ps[4 + b][:, 0:C], AF.Copy, ["ps%d" % (4 + b)], ["eh%d" % b], scale=0.5)
+    vq("uq", "us", 0, W, X("ub"))
+    pick("urq", "urs", 0, "uq", "us", W, X("l16"))
+    for t in range(R):
+        pick("tq%d" % t, "tsc%d" % t, 0, "uq", "us", W, X("l8", 0, 1))
 
     for t in range(R):
-        tq, tsc, lq, ls = T["tq%d" % t], T["tsc%d" % t], T["lq%d" % t], T["ls%d" % t]
-        rko, lr = T.rko[:, 16 * t:16 * t + 14], T.lr[:, 16 * t:16 * t + 14]
-        o16, ll = T.o16[:, 8 * t:8 * t + 6], T.ll[:, 8 * t:8 * t + 6]
-        o5, l5 = T.o16[:, 8 * t:8 * t + 5], T.ll[:, 8 * t:8 * t + 5]
-        if t == 0:
-            vq(T.uq[:], T.us[:], T.ub[:], ["ub"], ["uq"])
-            vcp(u32(T.u16q[:]), u32(T.uq[:]).indirect(T.l8[:, 0:1]), ["uq", "l8"], ["u16q"])
-            act(T.u16s[:], T.us[:].indirect(T.l8[:, 0:1]), AF.Copy, ["uq", "l8"], ["u16s"])
-            vcp(u32(T.urq[:]), u32(T.uq[:]).indirect(T.l16[:]), ["uq", "l16"], ["urq"])
-            act(T.urs[:], T.us[:].indirect(T.l16[:]), AF.Copy, ["uq", "l16"], ["urs"])
-            zero(T.eb[:, 0:512], 512, ["eb0"])
-            for which in range(2):
-                trs = []
-                for r in range(R):
-                    rid, pid = topo.addr(peers[r], core)
-                    e = topo.engines(core, peers[r])[2 * r:2 * r + 2]
-                    src = u8(T.u16q[:]) if which == 0 else T.u16s[:]
-                    dst = u8(T["ulq%d" % r][:]) if which == 0 else T["uls%d" % r][:]
-                    trs.append(RemoteDMATransfer(dst_ids=[DstId(rid=rid, pnc=pid)], dma_engine_mask=sum(1 << x for x in e),
-                                                 remote_sem=T.sem["ua%d" % r], src=src, dst=dst))
-                totals["loc"] += 2 * R
-                op("g", lambda trs=trs: g.remote_dma_fused(trs, local_sem=T.sem.loc), ["u16q" if which == 0 else "u16s"], (), "d")
-            for r in range(R):
-                totals["ua%d" % r] = 4
-                arrives(["ul%d" % r], "ua%d" % r, 4)
-        vq(tq[:], tsc[:], state(t)[:], tkeys(t), ["tq%d" % t])
-        send(t, u8(lq[:]), u8(tq[:]), "big%d" % t, ["tq%d" % t], ["lq%d" % t])
-        send(t, ls[:], tsc[:], "big%d" % t, ["tq%d" % t], ["lq%d" % t])
-        if t == 0:
-            for i, n in segs[:5]:
-                seg_iota(i, n)
-            vq(T.cq[:], T.cs[:], T.cb[:], ["cb0", "cb1"], ["cq"])
-        if t == 1:
-            vq(T.vq[:], T.vs[:], T.vb[:], ["vb"], ["vq"])
-        for b in range(2):
-            mm(ps[b][:, 0:C], T.urq[:], T.urs[:], tq[:], tsc[:], True, True, ["urq", "urs", "tq%d" % t], ["ps%d" % b])
-
-        def ov(m):
-            v_compare(T.mo, "mo", OWN_TILES, oo, OWN_RANGE, m, ps[0], ["ps0"], "vsc")
-
-        def oc(k):
-            count(T.mo, T.moq, T.mos, "mo", OWN_TILES, oo, k)
-        act(T.ssb[:], ps[1][:, 0:C], AF.Copy, ["ps1"], ["ssb"])
-        vtt(T.yy[:], ps[0][:, 0:C], T.m1[:], A.max, ["ps0", "m1"], ["yy"])
-        vsc(T.vsc[:, 0:C], T.d0[:], T.yy[:], 0.0, A.max, A.min, ["d0", "yy"], ["vsc", "vsc.a", "vsc.b"])
-        s_compares(T.mo, "mo", OWN_TILES, oo, OWN_RANGE, OWN_S, ps[1], ["ps1"], lambda m: "vsc", T.rso, "rso")
-        for m in OWN_V[:3]:
-            ov(m)
-        vtt(slot(T.mo, oo, 0, 3, 0, C), ps[0][:, 0:C], T.vsc[:, 0:C], A.is_gt, ["ps0", "vsc"], [slot_key("mo", 0, 3)])
-        ov(OWN_V[3])
-        oc(0)
-        vsc(T.dgo[:], T.keep0[:], slot(T.mo, oo, 0, 3, 0, C), 0.0, A.mult, A.add, ["keep0", slot_key("mo", 0, 3)], ["dgo"])
-        for m in OWN_V:
-            rowsum(T.mo, "mo", OWN_TILES, oo, OWN_RANGE, OWN_V, m)
-        partial(14, T.baseo, "baseo", T.dgo, "dgo")
-        oc(1)
-        partial2(OWN_V)
-        oc(2)
-        oc(3)
-        if t == 0:
-            for b in range(1, 4):
-                zero(T.eb[:, 512 * b:512 * b + 512], 512, ["eb%d" % b])
-            pick_scales(0)
-            act(T.dist[:], T.nf[:, 0:128], AF.Abs, ["nf", "npcol"], ["dist"], bias=npcol)
-        if t == 1:
-            act(T.xd[:], T.x0[:], AF.Copy, xk, ["xd"], scale=512.0)
-        finish(14, T.rso, "rso", OWN_S, rko, "rko%d" % t)
-        send(t, lr, rko, "rnk%d" % t, ["rko%d" % t], ["lr%d" % t])
-
-        if t == 0:
-            pick_codes(0)
-            for b in range(4):
-                act(T.eb[:, 512 * b + b:512 * b + 512:4], T.dist[:], AF.Relu, ["dist"], ["eb%d" % b], bias=1.0, scale=-1.0)
-        mm(ps[3][:, 0:C], T["upq%d" % t][:], T["ups%d" % t][:], lq[:], ls[:], True, True, ["upq%d" % t, "ups%d" % t, "lq%d" % t], ["ps3"])
-        act(T.spb[:], ps[3][:, 0:C], AF.Copy, ["ps3"], ["spb"])
-        if t == 0:
-            for k, lo in enumerate([320, 256, 192, 128, 0]):
-                zero_tile(T.mp, "mp", PAIR_TILES, po, k, lo)
-        vcp(T.ow[:].indirect(rko), T.nf[:, 0:C], ["rko%d" % t, "nf"], ["ow"])
-        vsc(T.oext[:], T.keepk[:, 0:96], T.ow[:, 0:96], 0.0, A.mult, A.add, ["keepk", "ow"], ["oext"])
-        if t == 0:
-            vsc(T.ext[:, 0:GB - GA], T.keepk[:, 0:GB - GA], T.x0[:, GA:GB], 0.0, A.mult, A.add, ["keepk"] + xk, ["ext"])
-        vts(o16, T.oext[:, 15:96:16], cp, None, A.mult, None, ["oext", "cp"], ["o16_%d" % t])
-        send(t, ll, o16, "lst%d" % t, ["o16_%d" % t], ["ll%d" % t])
-        if t == 0:
-            vts(T.ci[:], T.ext[:, 15:GB - GA:16], cp, None, A.mult, None, ["ext", "cp"], ["ci"])
-            vts(T.pjl[:], T.ext[:, 15:GB - GA:16], cp, 1.0 / 256, A.mult, A.mult, ["ext", "cp"], ["pjl"])
-        act(T.sv80[:], T.ssb[:].indirect(o5), AF.Copy, ["ssb", "o16_%d" % t], ["sv80"])
-        if t == 0:
-            vts(T.ci[:], T.ci[:], 255, None, A.bitwise_and, None, ["ci"], ["ci"])
-            vts(cp4, cp, 4.0, None, A.mult, None, ["cp"], ["cp4"])
-            vcp(T.pil[:], T.ci[:], ["ci"], ["pil"])
-            vts(T.m3[:], T.xm[:], lcol, -BIG, A.is_equal, A.mult, ["xm", "lcol"], ["m3"])
-        act(T.sp[:], T.sv80[:].indirect(T.pil[:]), AF.Copy, ["sv80", "pil"], ["sp"])
-        for b in range(4):
-            vts(T.off4[:, 6 * b:6 * b + 6], T.oext[:, 15:96:16], cp4, float(b), A.mult, A.add, ["oext", "cp4"], ["off4.%d" % b])
-        if t == 0:
-            zero(T.mp[:, 3:4 * 112:4], 112, [slot_key("mp", 0, 3)])
-            zero(T.rsp[:], 24, ["rsp"])
-            zero(T.ext[:, GB:NP], NP - GB, ["ext0"])
-            zero(T.dgp[:, 0:112], 112, ["dgp"])
-            zero(T.dgp[:, GB:NP], NP - GB, ["dgp"])
-            vts(T.basep[:], T.b16[:], lcol, 0.3, A.add, A.add, ["b16", "lcol"], ["basep"])
-            vq(T.eq[:], T.es[:], T.eb[:], ["eb%d" % b for b in range(4)], ["eq"])
-            lo = min(PAIR_V)
-            vts(T.basep[:, lo:lo + len(PAIR_V)], T.basep[:, lo:lo + len(PAIR_V)], -128.0, None, A.add, None, ["basep"], ["basep"])
-        else:
-            unpack(t)
-            halve()
-        if t == 1:
-            vtt(T.xc[:], T.xd[:], T.nf[:], A.add, ["xd", "nf"], ["xc"])
-
-        rows = ["row.v"]
-
-        def pv(m):
-            v_compare(T.mp, "mp", PAIR_TILES, po, PAIR_RANGE, m, T.row, rows, "vsc")
-
-        def pc(k):
-            count(T.mp, T.mpq, T.mps, "mp", PAIR_TILES, po, k)
-        vcp(T.ew[:].indirect(lr), T.spb[:], ["spb", "lr%d" % t], ["ew"])
-        act(T.row[:, GB:NP], T.sv80[:, K - (NP - GB):K], AF.Identity, ["sv80", "ew"], ["row.t"], bias=T.ew[:, 0:1])
-        for i in (1, 0, 2, 3, 4):
-            n = min(LEN[i], GA - START[i])
-            act(T.row[:, START[i]:START[i] + n], T.ew[:, 0:n], AF.Identity, ["sv80", "ew"], ["row.%d" % i], bias=T.sv80[:, i:i + 1])
-            rows.append("row.%d" % i)
-        vtt(T.row[:, GA:GB], T.ew[:].indirect(T.pjl[:]), T.sp[:], A.add, ["ew", "pjl", "sp"], ["row.v"])
-        vsc(T.vsc[:, GB:NP], T.m3[:], T.row[:, GB:NP], -BIG, A.add, A.max, ["m3", "row.t"], ["vsc.b"])
-        vsc(T.vsc[:, 80:112], T.m3[:], T.row[:, 80:112], -BIG, A.add, A.max, ["m3", "row.1"], ["vsc.a", "vsc"])
-        vtt(T.yy[:], T.row[:, 112:GB], T.m1[:], A.max, rows + ["m1"], ["yy"])
-        vsc(T.vsc[:, 112:GB], T.d0[:], T.yy[:], 0.0, A.max, A.min, ["d0", "yy"], ["vsc"])
-        s_compares(T.mp, "mp", PAIR_TILES, po, PAIR_RANGE, PAIR_S, T.row, rows,
-                   lambda m: "vsc.b" if m > 20 else ("vsc.a" if m < 7 else "vsc"), T.rsp, "rsp")
-        pv(20)
-        vtt(slot(T.mp, po, 0, 3, 112, GB), T.row[:, 112:GB], T.vsc[:, 112:GB], A.is_gt, rows + ["vsc"], [slot_key("mp", 0, 3)])
-        pv(19)
-        pc(0)
-        for m in PAIR_V[2:]:
-            pv(m)
-        pc(1)
-        vsc(T.dgp[:, 112:GB], T.keep0[:], slot(T.mp, po, 0, 3, 112, GB), 0.0, A.mult, A.add, ["keep0", slot_key("mp", 0, 3)], ["dgp"])
-        for m in PAIR_V:
-            rowsum(T.mp, "mp", PAIR_TILES, po, PAIR_RANGE, PAIR_V, m)
-        partial(23, T.basep, "basep", T.dgp, "dgp")
-        pc(2)
-        partial2(PAIR_V)
-        pc(3)
-        pc(4)
-        finish(23, T.rsp, "rsp", PAIR_S, T.rk[:, 0:23], "rk")
-        if t == 0:
-            unpack(t)
-        for b in range(4):
-            act(T.ts[:, K * b:K * b + K], state(t)[:].indirect(T.off4[:, 6 * b:6 * b + 5]), AF.Copy, tkeys(t) + ["off4.%d" % b], ["ts%d" % b], scale=0.5)
-        if t == 0:
-            halve()
-        for b in range(4):
-            act(T.ess[:, K * b:K * b + K], T.eh[:, C * b:C * b + C].indirect(l5), AF.Copy, ["eh%d" % b, "ll%d" % t], ["ess%d" % b])
+        tq, tsc, lq, ls = ["%s%d" % (n, t) for n in ("tq", "tsc", "lq", "ls")]
+        o4, ll = X("o4", 24 * t, 24 * t + 20), X("ll", 24 * t, 24 * t + 20)
         last = t == R - 1
-        vcp(T.xw[:].indirect(T.rk[:, 0:23]), T.xc[:] if last else T.x0[:], ["rk", "xc"] + xk, ["xw"])
-        vsc(T.ext[:, 0:C], T.keepk[:, 0:C], T.xw[:, 0:C], 0.0, A.mult, A.add, ["keepk", "xw"], ["ext"])
-        vts(T.bl16[:], T.ext[:, 15:C:16], cp, 2.0 ** -17 if last else 2.0 ** -8, A.mult, A.mult, ["ext", "cp"], ["bl16"])
-        vts(T.xi[:], T.ext[:, 15:C:16], cp, None, A.mult, None, ["ext", "cp"], ["xi"])
-        vts(T.xi[:], T.xi[:], 9 if last else 0, 127, A.logical_shift_right, A.bitwise_and, ["xi"], ["xi"])
-        vcp(T.a16[:], T.xi[:], ["xi"], ["a16"])
 
-        for b in range(4):
-            act(T.bg[:, C * b:C * b + C], T.ess[:, K * b:K * b + K].indirect(T.bl16[:]), AF.Copy, ["ess%d" % b, "bl16"], ["bg%d" % b])
-        for b in range(4):
-            vtt(T.zt[:, b:4 * C:4], T.ts[:, K * b:K * b + K].indirect(T.a16[:]), T.bg[:, C * b:C * b + C], A.add,
-                ["ts%d" % b, "a16", "bg%d" % b], ["z%d" % b])
-        vq(T.zq[:], T.zs[:], T.zt[:], ["z%d" % b for b in range(4)], ["zq"])
-        for b in range(4):
-            mm(ps[4 + b][:, 0:C], T.wq[:, 128 * b:128 * b + 128], T.wp[:, 128 * b:128 * b + 128], T.zq[:], T.zs[:], True, True,
-               ["wq", "wp", "zq"], ["ps%d" % (4 + b)])
-        for b in range(4):
-            act(T.rr[:, C * b:C * b + C], ps[4 + b][:, 0:C], AF.Relu, ["ps%d" % (4 + b)], ["rr%d" % b], scale=0.03125)
-        if last:
-            vcp(T.oi[:], T.xw[:, 0:C], ["xw"], ["oi"])
-            vts(T.oi[:], T.oi[:], 511, None, A.bitwise_and, None, ["oi"], ["oi"])
+        if t == 0:
+            vq(tq, tsc, UO, C, X("xb"))
+            send(t, X(lq), X(tq))
         else:
-            pick_codes(t + 1)
-            pick_scales(t + 1)
+            mm(6, "urq", "urs", 0, tq, tsc, UO + H, W)
+            send(t, X(lq, UO + H, UO + C), X(tq, UO + H, UO + C))
+        send(t, X(ls), X(tsc))
+        mm(7, "urq", "urs", 0, tq, tsc, UO, C)
+        mm(0, "urq", "urs", 0, tq, tsc, UO, C)
+        if t == 0:
+            in_block(OWN, 0, H, ps(7, 0, H))
+            in_block(OWN, H, C, ps(7, H, C))
+        else:
+            in_block(OWN, H, C, ps(6, 0, W))
+        compares(OWN, OWN_S, lambda lo, hi: ps(7, lo, hi), lambda m, lo, hi: ps(5 if t and 16 * m < H else 0, lo, hi))
+        act(X("ssb"), ps(0, 0, C), AF.Copy)
+        places(OWN, "baseo", 0, 14, "rko", 16 * t)
+        sent = parts(OWN) if SPLIT_SEND else [(0, 14)]
+        for a, b in sent:
+            send(t, X("lr", 16 * t + a, 16 * t + b), X("rko", 16 * t + a, 16 * t + b))
+
+        pick("upq%d" % t, "ups%d" % t, 0, lq, ls, UO, X("l2"))
+        mm(2, "upq%d" % t, "ups%d" % t, 0, lq, ls, UO, C)
+        act(X("spb"), ps(2, 0, C), AF.Copy)
+        for a, b in parts(OWN):
+            vcp(by(X("ow"), X("rko", 16 * t + a, 16 * t + b)), X("nf", 16 * a, 16 * b))
+        if t == 0:
+            load("y", X("wq"), T.wc[:], [len(ops) - 1])
+            load("y", X("wp"), T.ws[:], [len(ops) - 2])
+            load("y", X("vb"), T.v[:], [len(ops) - 3])
+            vq("vq", "vs", 0, W, X("vb"))
+        vsc(X("oe1"), X("am", 0, K), X("ow", 0, K), 0.0, A.add, A.max)
+        vts(X("o1", 0, 5), X("oe1", 15, K, 16), offc, None, A.subtract)
+        act(X("sw", 0, K), by(X("ssb"), X("o1", 0, 5)), AF.Copy)
+        act(X("sp", GA + 96, GB), by(X("sw", 0, K), X("pil", 6, 14)), AF.Copy)
+        act(X("sp", GA, GA + 96), by(X("sw", 0, K), X("pil", 0, 6)), AF.Copy)
+        vsc(X("oex"), X("k4", 0, K), X("ow", 0, K), 0.0, A.mult, A.add)
+        vts(o4, X("oex", 3, K, 4), cpo, rcol, A.mult, A.add)
+        send(t, ll, o4)
+        act(X("ts"), by(X("xb"), o4), AF.Copy, 0.0, 0.5)
         for b in range(4):
-            vtt(state(t + 1)[:, b:4 * C:4], T.rr[:, C * b:C * b + C], T.zt[:, b:4 * C:4], A.add, ["rr%d" % b, "z%d" % b], ["t%d.%d" % (t + 1, b)])
+            mm(3 + b, "eq", "es", W * b, lq, ls, UO, C)
+            act(X("eh", b, 4 * C, 4), ps(3 + b, 0, C), AF.Copy, 0.0, 0.5)
+        act(X("ess"), by(X("eh"), ll), AF.Copy)
 
-    tq, tsc = T.tq3, T.tsc3
-    vq(tq[:], tsc[:], state(R)[:], tkeys(R), ["tq3"])
-    vcp(T.olf[:], T.oi[:], ["oi"], ["olf"])
-    mm(ps[0][:, 0:C], T.vq[:], T.vs[:], tq[:], tsc[:], True, True, ["vq", "tq3"], ["ps0"])
-    dma("y", T.oc[:], u8(tq[:]), "st", ["tq3"])
-    dma("s", T.osc[0:4, :], tsc[0:4, :], "st", ["tq3"])
-    act(T.yf[:], ps[0][:, 0:C], AF.Copy, ["ps0"], ["yf"])
-    dma("y", T.osc[4:8, :], tsc[32:36, :], "st", ["tq3"])
-    dma("y", T.ol[:], T.olf[0:128:16, :], "st", ["olf"])
-    dma("s", T.y[:], T.yf[:], "st", ["yf"])
-    dma("y", T.osc[8:12, :], tsc[64:68, :], "st", ["tq3"])
-    dma("s", T.osc[12:16, :], tsc[96:100, :], "st", ["tq3"])
+        for a, b in sent:
+            vcp(by(X("ew"), X("lr", 16 * t + a, 16 * t + b)), X("spb", 16 * a, 16 * b))
+        act(X("row", GB, NP), X("sw", K - (NP - GB), K), AF.Identity, X("ew", 0, 1))
+        act(X("row", K, GA), X("ew", 0, GA - K), AF.Identity, X("sw", 1, 2))
+        act(X("row", 0, K), X("ew", 0, K), AF.Identity, X("sw", 0, 1))
+        for lo, hi in [(GA + 96, GB), (GA, GA + 96)]:
+            vtt(X("row", lo, hi), by(X("ew"), X("pjl", (lo - GA) // 16, (hi - GA) // 16)), X("sp", lo, hi), A.add)
+        vsc(X("vp", GB, NP), X("m3", 0, 32), X("row", GB, NP), -BIG, A.add, A.max)
+        vsc(X("vp", K, GA), X("m3", 0, 32), X("row", K, GA), -BIG, A.add, A.max)
+        for lo, hi in [(GA + 96, GB), (GA, GA + 96)]:
+            in_block(PAIR, lo, hi, X("row", lo, hi))
+        compares(PAIR, PAIR_S, lambda lo, hi: X("row", lo, hi), lambda m, lo, hi: X("row", lo, hi))
+        places(PAIR, "basep", 7, 21, "rk", 0)
 
-    known = {q: {} for q in queues}
-    snap, need, waits = [], set(), []
-    for x, (q, fn, deps, kind) in enumerate(ops):
-        want = {}
-        for d in deps:
-            key, val = (ops[d[1]][0], d[1]) if d[0] == "op" else (d[1], d[2])
-            if known[q].get(key, -1) < val:
-                want[key] = max(want.get(key, -1), val)
-        mine = []
-        for key, val in sorted(want.items(), key=lambda kv: -kv[1] if kv[0] in qsem else 0):
-            if known[q].get(key, -1) >= val:
-                continue
-            mine.append((key, val))
-            known[q][key] = val
-            if key in qsem:
-                need.add(val)
-                for k2, v2 in snap[val].items():
-                    if known[q].get(k2, -1) < v2:
-                        known[q][k2] = v2
-        waits.append(mine)
-        snap.append(dict(known[q]))
-    number, cnt = {}, {q: 0 for q in qsem}
-    for x, o in enumerate(ops):
-        if x in need:
-            cnt[o[0]] += 1
-            number[x] = cnt[o[0]]
-    for x, (q, fn, deps, kind) in enumerate(ops):
-        for key, val in waits[x]:
-            if key in qsem:
-                queues[q].wait_ge(T.sem[qsem[key]], number[val])
+        for a, b in parts(PAIR):
+            vcp(by(X("xw"), X("rk", a, b)), X("xl" if last else "x0", 16 * a, 16 * b))
+        for lo, hi in LISTS:
+            vsc(X("ex4", lo, hi), X("k4", lo, hi), X("xw", lo, hi), 0.0, A.mult, A.add)
+            in_turn("ex4", lo)
+        for lo, hi in LISTS:
+            a, b = lo // 4, hi // 4
+            ends = X("ex4", lo + 3, hi, 4)
+            vts(X("xi", a, b), ends, cp, float(MID) if last else 0.0, A.mult, A.add)
+            vts(X("xk", a, b), X("xi", a, b), 127, None, A.bitwise_and)
+            vts(X("a4", a, b), X("xk", a, b), 4.0, rcol, A.mult, A.add)
+            if last:
+                vts(X("xj", a, b), X("xi", a, b), 7, 127, A.logical_shift_right, A.bitwise_and)
+                vts(X("b4", a, b), X("xj", a, b), 4.0, rcol, A.mult, A.add)
             else:
-                queues[q].wait_ge(T.sem[key], val)
-        ins = fn()
-        if x in need:
+                vts(X("b4", a, b), ends, cpb, rcol, A.mult, A.add)
+        if last:
+            act(X("olt"), X("xw", 0, C), AF.Identity, MAGIC, 2.0 ** -14)
+            act(X("olf"), X("olt"), AF.Identity, -MAGIC)
+            store("y", T.ol[:], X("olf"), T.olf[0:128:16, :])
+
+        nq, ns = "tq%d" % (t + 1), "tsc%d" % (t + 1)
+
+        def combine(lo, hi):
+            act(X("bg", 4 * lo, 4 * hi), by(X("ess"), X("b4", lo // 4, hi // 4)), AF.Copy)
+            in_turn("bg", lo)
+            vtt(X("zt", 4 * lo, 4 * hi), by(X("ts"), X("a4", lo // 4, hi // 4)), X("bg", 4 * lo, 4 * hi), A.add)
+
+        def layer(c, lo, hi):
+            vq("zq", "zs", W * c, W, X("zt", 4 * lo, 4 * (lo + W)))
+            for b in range(4):
+                bank = 4 * (1 - c) + b
+                mm(bank, "wq", "wp", W * b, "zq", "zs", W * c, W)
+                act(X("rr", 4 * lo + b, 4 * hi, 4), ps(bank, 0, hi - lo), AF.Relu, 0.0, 0.03125)
+
+        def add(lo, hi, b=0, step=1):
+            vtt(X("xb", 4 * lo + b, 4 * hi, step), X("rr", 4 * lo + b, 4 * hi, step), X("zt", 4 * lo + b, 4 * hi, step), A.add)
+        for lo, hi in PIECES:
+            if lo == H:
+                layer(0, 0, H)
+            combine(lo, hi)
+        layer(1, H, C)
+        for b in range(4):
+            add(0, H, b, 4)
+        vq(nq, ns, UO, W, X("xb", 0, 4 * W))
+        if last:
+            mm(4, "vq", "vs", 0, nq, ns, UO, W)
+            store("y", T.oc[:, 0:4 * H], X(nq, UO, UO + H))
+            act(X("yf", 0, H), ps(4, 0, H), AF.Copy)
+            store("y", T.y[:, 0:H], X("yf", 0, H))
+        else:
+            mm(4, "urq", "urs", 0, nq, ns, UO, W)
+            mm(5, "urq", "urs", 0, nq, ns, UO, W)
+            send(t + 1, X("lq%d" % (t + 1), 0, UO + H), X(nq, 0, UO + H))
+            in_block(OWN, 0, H, ps(4, 0, H))
+        for b in range(4):
+            add(W, C, b, 4)
+        add(H, W)
+        vq(nq, ns, UO + H, W, X("xb", 4 * H, 4 * C))
+
+    mm(5, "vq", "vs", 0, "tq3", "tsc3", UO + H, W)
+    act(X("yf", H, C), ps(5, 0, W), AF.Copy)
+    store("s", T.y[:, H:C], X("yf", H, C))
+    store("y", T.oc[:, 4 * H:4 * C], X("tq3", UO + H, UO + C))
+    for k in range(4):
+        store("y" if k else "s", T.osc[4 * k:4 * k + 4, :], X("tsc3", UO, UO + C), T.tsc3[32 * k:32 * k + 4, UO:UO + C])
+
+    order = schedule(ops)
+    at = {x: k for k, x in enumerate(order)}
+    known = {q: {} for q in queues}
+    snap, need, waits, waited = {}, set(), {}, set()
+    for x in order:
+        q = ops[x][0]
+        want = {}
+        for d, soft in ops[x][2]:
+            key, v = (ops[d][0], at[d]) if ops[d][5] is None else (ops[d][5], counts[ops[d][5]])
+            if not soft and known[q].get(key, -1) < v:
+                want[key] = max(want.get(key, -1), v)
+        waits[x] = []
+        for key, v in sorted(want.items(), key=lambda kv: -kv[1] if kv[0] in qsem else 0):
+            if known[q].get(key, -1) >= v:
+                continue
+            waits[x].append((key, v))
+            known[q][key] = v
+            if key in qsem:
+                need.add(v)
+                for k2, v2 in snap[v].items():
+                    known[q][k2] = max(known[q].get(k2, -1), v2)
+            else:
+                waited.add(key)
+        snap[at[x]] = dict(known[q])
+    number, cnt = {}, {q: 0 for q in qsem}
+    for k, x in enumerate(order):
+        if k in need:
+            cnt[ops[x][0]] += 1
+            number[k] = cnt[ops[x][0]]
+    for k, x in enumerate(order):
+        q = ops[x][0]
+        for key, v in waits[x]:
+            queues[q].wait_ge(T.sem[qsem.get(key, key)], number[v] if key in qsem else v)
+        ins = ops[x][1]()
+        if k in need:
             ins.then_inc(T.sem[qsem[q]], 1)
-    for name, val in totals.items():
-        g.wait_ge(T.sem[name], val)
+    for name, v in counts.items():
+        if name not in waited:
+            g.wait_ge(T.sem[name], v)

@@ -10,27 +10,41 @@ OFF = 1024.0
 KK = 2.0 ** 26
 MID = 5100
 MAGIC = 1.5 * 2.0 ** 23
+PMID = 160.0
 JW = 168
+GATHERED = [(176, 336)]
+MIXED = [(208, 336), (112, 208)]
 GA, GM, GB = 112, 224, 336
-H, W = 96, 128
+W = 128
+M = C - W
+RUNS = [128, 128, 128]
 UO = 16
-PIECES = [(0, 32), (32, 64), (64, 96), (128, 160), (160, 224), (96, 128)]
+PIECES = {96: [(0, 32), (32, 64), (64, 96), (128, 160), (160, 224)], 128: [(0, 32), (32, 80), (80, 128), (128, 160), (160, 224)]}
 LISTS = [(0, 64), (64, 224)]
 
-OWN_TILES = [(224, [13, 12, 11, "d"]), (128, [2, 1]), (128, [6, 5, 4, 3]), (160, [10, 9, 8, 7])]
-OWN_ZERO = [176, 0, 48, 112]
-OWN_V = [13, 12, 11]
-OWN_S = [5, 4, 3, 2, 1, 6, 7, 8, 9, 10]
+NB = W // 16
+OWN_TILES = [(0, ["d0", "l7", "l6", "l5"]), (128, ["l4", "l3", "l2", "l1"]), (256, ["u0", "u1", "u2", "u3"]), (352, ["u4", "u5", "u6", "u7"]),
+             (480, ["d1", "l13", "l12", "l11"]), (576, ["l10", "l9"])]
+OWN_ZERO = [(80, 128), (144, 256), (528, 576), (576, 672)]
+OWN_ALL = [x for o, bl in OWN_TILES for x in bl]
+OWN_V = ["u5", "u6", "u7", "l11", "l12", "l13"]
+WO = 704
+OWN_T2 = [(224, [13, 12, 11, "d"]), (128, [2, 1]), (128, [6, 5, 4, 3]), (160, [10, 9, 8, 7])]
+OWN_Z2 = [176, 0, 48, 112]
+OWN_V2 = [13, 12, 11]
+OWN_V0 = [13, 12, 11, 10]
+OWN_S = [m for m in range(1, 14) if m not in OWN_V2]
 OWN_RANGE = {m: (0, 16 * m) for m in range(1, 14)}
-PAIR_TILES = [(336, [22, 21, 20, "d"]), (128, [7, 6, 5]), (304, [19, 18, 17, 16]), (240, [15, 14, 13, 12]), (176, [11, 10, 9, 8])]
-PAIR_ZERO = [320, 0, 256, 192, 128]
-PAIR_V = [20, 19, 18, 17, 16, 15]
-PAIR_S = [22, 21, 5, 6, 7, 14, 13, 12, 11, 10, 9, 8]
+OWN_CUT = (10, 96)
+PAIR_TILES = [(336, [22, 21, 20, "d"]), (304, [19, 18, 17, 16]), (240, [15, 14, 13, 12]), (176, [11, 10, 9, 8]), (128, [7, 6, 5])]
+PAIR_ZERO = [320, 256, 192, 128, 0]
+PAIR_V = [20, 19, 18, 17, 16, 15, 6, 5]
+PAIR_S = [m for m in range(22, 4, -1) if m not in PAIR_V]
 PAIR_RANGE = {m: (0, 16 * m) for m in range(7, 21)}
 PAIR_RANGE.update({5: (0, 80), 6: (16, 80), 21: (0, 328), 22: (0, 328)})
-OWN_CUT, PAIR_CUT = (10, 96), (12, 112)
+PAIR_CUT = (12, 112)
+PAIR_RUNS = [(12, 23), (0, 12)]
 SPLIT_SEND = True
-WO = sum(w for w, _ in OWN_TILES)
 WP = sum(w for w, _ in PAIR_TILES)
 
 F, B, I, U, Q, S8 = "float32", "bfloat16", "int32", "uint16", "float8_e4m3fn_x4", "uint8"
@@ -38,18 +52,18 @@ SCRATCH = {}
 for _n, _w, _d in [
     ("xb", 4 * C, B), ("ub", 512, B), ("vb", 512, B), ("wq", 512, Q), ("wp", 512, S8),
     ("uq", W, Q), ("us", W, S8), ("vq", W, Q), ("vs", W, S8), ("urq", W, Q), ("urs", W, S8),
-    ("zb", 516, B), ("eb", 516, B), ("eq", 512, Q), ("es", 512, S8), ("cb", 512, B), ("cq", W, Q), ("cs", W, S8),
-    ("grp", W, B), ("pi", 1, I), ("li", 4, I), ("col", 12, F), ("xm", GB, B), ("xm4", C, B), ("b16", 24, F),
-    ("nf", C, F), ("x0", NP, F), ("xl", NP, F),
+    ("zb", 516, B), ("eb", 516, B), ("eq", 512, Q), ("es", 512, S8), ("cb", 1024, B), ("cq", 2 * W, Q), ("cs", 2 * W, S8),
+    ("grp", W, B), ("pi", 1, I), ("li", 4, I), ("col", 13, F), ("xm", GB, B), ("xm4", C, B), ("b16", 24, F),
+    ("nf", C, F), ("x0", NP, F), ("st4", 4 * K, F), ("stg", 4 * C, F),
     ("m3", GB, B), ("am", GB, B), ("ym", C, B), ("d0", C, B), ("keep0", C, B), ("k4", C, B),
     ("l16", 8, U), ("l2", 8, U), ("l8", 2, U), ("pil", 14, U), ("pjl", 14, U),
-    ("baseo", 14, F), ("basep", 24, F),
+    ("dmo", C, B), ("dmp", GB, B),
     ("mo", 4 * WO, B), ("moq", WO, Q), ("mos", WO, S8), ("mp", 4 * WP, B), ("mpq", WP, Q), ("mps", WP, S8),
-    ("yo", C, F), ("vo", C, F), ("yp", NP, F), ("vp", NP, F), ("tao", 1200, B), ("tap", 2400, B),
-    ("jo", 8 * JW, B), ("jp", 8 * JW, B), ("dgo", C, B), ("dgp", NP, B),
-    ("rso", 14, F), ("rsp", 24, F), ("po", 14, F), ("pp", 24, F), ("qo", 14, F), ("qp", 24, F), ("exo", C, F), ("exq", NP, F),
+    ("yo", C, F), ("vo", C, F), ("yp", NP, F), ("vp", NP, F), ("tao", 24 * W, B), ("tap", 2400, B),
+    ("jo", 16 * JW, B), ("jp", 8 * JW, B), ("dgo", C, B), ("dgp", NP, B),
+    ("rso", 24, F), ("rsp", 24, F), ("po", 14, F), ("pp", 24, F), ("qo", 14, F), ("qp", 24, F), ("exo", C, F), ("exq", NP, F),
     ("yro", 14, F), ("yrp", 24, F), ("rk", 24, U), ("ow", C, F), ("oex", K, F), ("oe1", K, F), ("o1", 6, U), ("ssb", C, F), ("spb", C, F), ("sw", C, F),
-    ("ew", C, F), ("sp", NP, F), ("row", NP, F), ("xw", NP, F), ("ex4", C, F), ("xi", 56, I), ("xj", 56, I), ("xk", 56, I),
+    ("ew", C, F), ("sp", NP, F), ("row", NP, F), ("xw", NP, F), ("ex4", C, F), ("xi", 56, I), ("xk", 56, I),
     ("a4", 56, U), ("b4", 56, U),
     ("ts", 4 * K, B), ("eh", 4 * C, B), ("ess", 4 * K, B), ("bg", 4 * C, B), ("zt", 4 * C, B), ("zq", 2 * W, Q), ("zs", 2 * W, S8),
     ("rr", 4 * C, F), ("olt", C, F), ("olf", C, F), ("yf", C, F),
@@ -67,47 +81,67 @@ A = AluOpType
 AF = ActivationFunctionType
 SIZE = {F: 4, B: 2, I: 4, U: 2, Q: 4, S8: 1}
 HOP = 250
-FAR = 1500
+PASSES = 3
+LOAD = 1800
+FIRST = 2500
+ZDMA = True
+FAR = 1200
 
 
 def schedule(ops):
     n = len(ops)
-    succ = [[] for _ in ops]
-    for x, o in enumerate(ops):
-        for d, soft in o[2]:
-            succ[d].append((x, soft))
-    chain = [0] * n
+    nodes = [(o[0], o[3]) for o in ops] + [("end", 0)]
+    pred = [[(d, 0 if soft else ops[d][4]) for d, soft in o[2]] for o in ops] + [[(x, o[4]) for x, o in enumerate(ops)]]
+    succ = [[] for _ in nodes]
+    for x, p in enumerate(pred):
+        for d, lag in p:
+            succ[d].append((x, lag))
+    chain = [0] * (n + 1)
     for x in range(n - 1, -1, -1):
-        chain[x] = ops[x][3] + max([(0 if soft else ops[x][4]) + chain[y] for y, soft in succ[x]] + [ops[x][4]])
-    left = [len(o[2]) for o in ops]
-    ready = [0] * n
+        chain[x] = nodes[x][1] + max(lag + chain[y] for y, lag in succ[x])
+    best = None
+    for _ in range(PASSES):
+        order, start = one_pass(nodes, pred, succ, chain)
+        if best is None or start[n] < best[0]:
+            best = (start[n], order[:-1])
+        back = one_pass(nodes, succ, pred, [start[x] + nodes[x][1] for x in range(n + 1)])[1]
+        chain = [back[x] + nodes[x][1] for x in range(n + 1)]
+    return best[1]
+
+
+def one_pass(nodes, pred, succ, chain):
+    n = len(nodes)
+    tail = [chain[x] - nodes[x][1] for x in range(n)]
+    left = [len(p) for p in pred]
+    ready, start = [0] * n, [0] * n
     free, cand = {}, {}
-    for x, o in enumerate(ops):
-        free[o[0]] = 0
-        cand.setdefault(o[0], [])
+    for x, (q, c) in enumerate(nodes):
+        free[q] = 0
+        cand.setdefault(q, [])
         if not left[x]:
-            cand[o[0]].append(x)
+            cand[q].append(x)
     order = []
     while len(order) < n:
-        q = min((q for q in cand if cand[q]), key=lambda q: max(free[q], min(ready[x] for x in cand[q])))
-        now = max(free[q], min(ready[x] for x in cand[q]))
-        pick = max((x for x in cand[q] if ready[x] <= now), key=lambda x: (chain[x], -x))
-        for y in sorted((x for x in cand[q] if now < ready[x] < now + ops[pick][3] and chain[x] > chain[pick]), key=lambda x: -chain[x])[:1]:
-            fits = [x for x in cand[q] if ready[x] <= now and now + ops[x][3] <= ready[y] + 20]
+        now, q = min((max(free[q], min(ready[x] for x in cand[q])), q) for q in cand if cand[q])
+        pick = max((x for x in cand[q] if ready[x] <= now), key=lambda x: (tail[x], -x))
+        soon = [x for x in cand[q] if now < ready[x] < now + nodes[pick][1] and tail[x] > tail[pick]]
+        if soon:
+            y = max(soon, key=lambda x: (tail[x], -x))
+            fits = [x for x in cand[q] if ready[x] <= now and now + nodes[x][1] <= ready[y] + 20]
             if fits:
-                pick = max(fits, key=lambda x: (chain[x], -x))
-            elif max(ready[y] + chain[y], ready[y] + ops[y][3] + chain[pick]) < max(now + chain[pick], now + ops[pick][3] + chain[y]):
+                pick = max(fits, key=lambda x: (tail[x], -x))
+            elif max(ready[y] + chain[y], ready[y] + nodes[y][1] + chain[pick]) < max(now + chain[pick], now + nodes[pick][1] + chain[y]):
                 pick = y
-        start = max(now, ready[pick])
-        free[q] = start + ops[pick][3]
+        start[pick] = max(now, ready[pick])
+        free[q] = start[pick] + nodes[pick][1]
         cand[q].remove(pick)
         order.append(pick)
-        for y, soft in succ[pick]:
-            ready[y] = max(ready[y], free[q] + (0 if soft else ops[pick][4]))
+        for y, lag in succ[pick]:
+            ready[y] = max(ready[y], free[q] + lag)
             left[y] -= 1
             if not left[y]:
-                cand[ops[y][0]].append(y)
-    return order
+                cand[nodes[y][0]].append(y)
+    return order, start
 
 
 def rank_program(g, core, T, topo):
@@ -226,7 +260,7 @@ def rank_program(g, core, T, topo):
     def load(q, out, src, after=()):
         sem = new_sem(16)
         ins = [src] if isinstance(src, tuple) else []
-        op(q, lambda: queues[q].dma_start(raw(out), val(src)).then_inc(T.sem[sem], 16), ins, [out], 60, FAR + row_bytes(out) // 2, sem, after)
+        op(q, lambda: queues[q].dma_start(raw(out), val(src)).then_inc(T.sem[sem], 16), ins, [out], 60, LOAD + row_bytes(out) // 2, sem, after)
 
     def store(q, out, a, part=None):
         counts["st"] += 16
@@ -240,9 +274,10 @@ def rank_program(g, core, T, topo):
         counts["loc"] += len(topo.engines(core, peers[t]))
         sem = new_sem(len(topo.engines(peers[t], core)))
         op("g", lambda: g.remote_dma(raw(out), raw(a), T.sem[sem], T.sem.loc, pid, rid, topo.mask(core, peers[t])), [a], [out],
-           360, FAR + row_bytes(a) + (FAR if t == 0 and a[1] > W else 0), sem)
+           360, FAR + row_bytes(a) + (FIRST if t == 0 and a[1] > W else 0), sem)
 
     lcol, gcol, qcol, rcol, offc, c1, cp, cpo, cpb = [X("col", i, i + 1) for i in range(9)]
+    tcol = X("col", 12, 13)
 
     def ps(bank, lo, hi):
         return X("ps%d" % bank, lo, hi)
@@ -263,16 +298,11 @@ def rank_program(g, core, T, topo):
         if i == 0 or LEN[i] != LEN[i - 1]:
             n = LEN.count(LEN[i])
             iota(X("x0", START[i], START[i] + n * LEN[i]), [[1, n], [1024, LEN[i]]], i)
-        if i == 0 or LEN[i - 1] > 1:
-            step, n = (16384 + 128, LEN[i]) if LEN[i] > 1 else (16384 + 1, K - i)
-            iota(X("xl", START[i], START[i] + n), [[step, n]], 16384 * START[i] + i - MID)
+            iota(X("st4", 4 * i, 4 * (i + n)), [[LEN[i], n], [0, 4]], START[i])
 
     vms(X("zb"), 0.0)
     vms(X("d0"), BIG)
     vms(X("d0", 0, C, 16), -BIG)
-    vms(X("rso"), 0.0)
-    vms(X("rsp"), 0.0)
-    vms(X("exq", GB, NP), 0.0)
     vts(X("li", 0, 1), X("pi"), 15, None, A.bitwise_and)
     vts(X("li", 1, 2), X("pi"), 4, None, A.logical_shift_right)
     vts(X("li", 2, 3), X("pi"), 2, 3, A.logical_shift_right, A.bitwise_and)
@@ -282,25 +312,28 @@ def rank_program(g, core, T, topo):
     vts(X("l8", 0, 1), lcol, 8.0, None, A.mult)
     vts(X("l2"), X("b16", 0, 8), 0.125, None, A.mult)
     vts(X("m3"), X("xm"), lcol, -BIG, A.is_equal, A.mult)
-    vts(offc, lcol, -OFF, 15 * OFF, A.mult, A.add)
-    vts(c1, lcol, OFF - 1, -15 * (OFF - 1), A.mult, A.add)
+    act(offc, lcol, AF.Identity, 15 * OFF, -OFF)
+    act(c1, lcol, AF.Identity, -15 * (OFF - 1), OFF - 1)
     for k in range(4):
         vts(X("cb", k, 512, 4), X("grp"), gcol, None, A.is_equal)
-    vq("cq", "cs", 0, W, X("cb"))
+    vq("cq", "cs", 0, W, X("cb", 0, 512))
     vts(X("col", 9, 12), X("xm", 0, 3), qcol, 1.0 / KK, A.is_lt, A.max)
     op("v", lambda: V.tensor_reduce(cp[0], T.col[:, 9:12], AxisListType.X, A.mult), [X("col", 9, 12)], [cp], 64)
-    vts(cpo, cp, 4.0, None, A.mult)
-    vts(cpb, cp, 1.0 / 256, None, A.mult)
+    act(cpo, cp, AF.Copy, 0.0, 4.0)
+    act(cpb, cp, AF.Copy, 0.0, 1.0 / 256)
     vts(X("k4"), X("xm4"), qcol, KK, A.not_equal, A.mult)
-    lo = min(PAIR_V)
-    vts(X("baseo"), X("b16", 0, 14), c1, None, A.add)
-    vts(X("pp", 0, 7), X("b16", 0, 7), lcol, offc, A.add, A.subtract)
-    vts(X("pp", 21, 23), X("b16", 21, 23), lcol, None, A.add)
-    vts(X("basep", 7, lo), X("b16", 7, lo), c1, None, A.add)
-    vts(X("basep", lo, 21), X("b16", lo, 21), c1, -128.0, A.add, A.add)
     act(X("ym"), X("m3", 0, C), AF.Identity, -BIG, -33.0)
     act(X("am"), X("m3"), AF.Identity, OFF, 65.0 * OFF / BIG)
-    act(X("keep0"), X("d0"), AF.Relu, 0.0, 1.0 / BIG)
+    vms(X("dmo"), BIG)
+    vms(X("dmp", GA, GB), BIG)
+    act(X("dmo", 0, C, 16), X("b16", 0, 14), AF.Copy, 0.0, -1.0)
+    act(X("dmp", GA, GB, 16), X("b16", 7, 21), AF.Identity, PMID, -1.0)
+    act(tcol, lcol, AF.Identity, PMID + 15.0, -2.0)
+    act(X("dgp", 15, GA, 16), X("b16", 0, 7), AF.Identity, tcol, -1.0)
+    act(X("dgp", GB + 15, NP, 16), X("b16", 21, 23), AF.Identity, tcol, -1.0)
+    act(X("exq", GB + 15, NP, 16), X("zb", 0, 2), AF.Identity, offc)
+    act(X("rso", 0, 2), X("zb", 0, 2), AF.Copy)
+    act(X("rsp", 0, 5), X("zb", 0, 5), AF.Copy)
     op("g", lambda: g.affine_select(T.eb[:], T.zb[:], [[1, 516]], A.not_equal, 1.0, -3, -4), [X("zb")], [X("eb")], 205 + 2 * 516)
     for b in range(4):
         vq("eq", "es", W * b, W, X("eb", 3 - b, 515 - b))
@@ -311,20 +344,21 @@ def rank_program(g, core, T, topo):
     vts(X("xk", 0, 14), X("xi", 0, 14), 127, None, A.bitwise_and)
     vcp(X("pil"), X("xk", 0, 14))
 
-    OWN = dict(m="mo", q="moq", s="mos", tiles=OWN_TILES, offs=tile_offsets(OWN_TILES), rng=OWN_RANGE, v=OWN_V, y="yo", val="vo",
-               tau="tao", junk="jo", dg="dgo", rs="rso", p="po", p2="qo", ext="exo", yr="yro", init=0.0, nb=14,
-               cut=OWN_CUT[0], y0=OWN_CUT[1], bank=3)
     PAIR = dict(m="mp", q="mpq", s="mps", tiles=PAIR_TILES, offs=tile_offsets(PAIR_TILES), rng=PAIR_RANGE, v=PAIR_V, y="yp", val="vp",
-                tau="tap", junk="jp", dg="dgp", rs="rsp", p="pp", p2="qp", ext="exq", yr="yrp", init=-128.0, nb=23,
+                tau="tap", junk="jp", dg="dgp", rs="rsp", p="pp", p2="qp", ext="exq", yr="yrp", dm="dmp", mid=PMID, nb=23,
                 cut=PAIR_CUT[0], y0=PAIR_CUT[1], bank=0)
 
     def zeros(Z, lows):
         return [(4 * (Z["offs"][k] + lo), 4 * (Z["offs"][k] + Z["tiles"][k][0])) for k, lo in enumerate(lows)]
-    for a, b in zeros(OWN, OWN_ZERO):
-        act(X("mo", a, b), X("zb", 0, b - a), AF.Copy)
-    for a, b in zeros(PAIR, PAIR_ZERO) + [(0, 4 * GA)]:
-        load("y", X("mp", a, b), X("zb", 0, b - a))
-    load("y", X("zt", 4 * H, 4 * W), X("zb", 0, 4 * (W - H)))
+    if ZDMA:
+        for a, b in zeros(PAIR, PAIR_ZERO) + [(0, 4 * GA)]:
+            load("y", X("mp", a, b), X("zb", 0, b - a))
+    else:
+        for a, b in zeros(PAIR, PAIR_ZERO):
+            act(X("mp", a, b), X("zb", 0, b - a), AF.Copy)
+        act(X("mp", 3, 4 * GA, 4), X("zb", 0, GA), AF.Copy)
+    if RUNS[0] < W:
+        load("y", X("zt", 4 * M, 4 * W), X("zb", 0, 4 * (W - M)))
 
     def slot(Z, m, lo, hi):
         k = [m in bl for w, bl in Z["tiles"]].index(True)
@@ -338,7 +372,7 @@ def rank_program(g, core, T, topo):
         vsc(X(Z["y"], lo, hi), X("ym", 0, hi - lo), src, 0.0, A.add, A.min)
         vsc(X(Z["val"], lo, hi), X("d0", 0, hi - lo), X(Z["y"], lo, hi), 0.0, A.min, A.max)
         vtt(slot(Z, "d", lo, hi), src, X(Z["val"], lo, hi), A.is_le)
-        vsc(X(Z["dg"], lo, hi), X("keep0", 0, hi - lo), slot(Z, "d", lo, hi), 0.0, A.mult, A.add)
+        vsc(X(Z["dg"], lo, hi), X(Z["dm"], lo, hi), slot(Z, "d", lo, hi), BIG, A.min, A.add)
 
     def compares(Z, sblocks, vsrc, ssrc):
         pos = 0
@@ -351,7 +385,7 @@ def rank_program(g, core, T, topo):
             lo, hi = Z["rng"][m]
             h, x = (hi - lo) // 2, sorted(Z["v"]).index(m)
             vts(slot(Z, m, lo, hi), vsrc(lo, hi), mine(Z, m), None, A.is_lt)
-            vsc(X(Z["junk"], (x + 1) * JW - h, (x + 1) * JW), slot(Z, m, lo, lo + h), slot(Z, m, lo + h, hi), Z["init"], A.add, A.add)
+            vsc(X(Z["junk"], (x + 1) * JW - h, (x + 1) * JW), slot(Z, m, lo, lo + h), slot(Z, m, lo + h, hi), -128.0, A.add, A.add)
 
     def places(Z, base, lo, hi, out, o0):
         nb, v0, nv, cut, y0 = Z["nb"], min(Z["v"]), len(Z["v"]), Z["cut"], Z["y0"]
@@ -361,18 +395,118 @@ def rank_program(g, core, T, topo):
             vq(Z["q"], Z["s"], o, w, X(Z["m"], 4 * o, 4 * (o + w)))
             if k in high:
                 mm(Z["bank"], "cq", "cs", 0, Z["q"], Z["s"], o + y0, w - y0, k == high[0], k == high[-1])
+                in_turn("count", k)
             if cut:
-                mm(1, "cq", "cs", 0, Z["q"], Z["s"], o, min(w, 16 * cut), k == 0, k == len(Z["tiles"]) - 1)
-        vtt(X(Z["p"], lo, hi), X(base, lo, hi), X(Z["dg"], 16 * lo + 15, 16 * hi, 16), A.subtract)
-        vtt(X(Z["p"], v0, v0 + nv), X(Z["p"], v0, v0 + nv), X(Z["junk"], JW - 1, nv * JW, JW), A.subtract)
-        for a, b, src in [(cut, nb, ps(Z["bank"], 16 * cut - y0, min(16 * nb, GB) - y0)), (0, cut, ps(1, 0, 16 * cut))][:2 if cut else 1]:
-            vtt(X(Z["p2"], a, b), X(Z["p"], a, b), X(Z["rs"], a, b), A.subtract)
+                mm(3, "cq", "cs", 0, Z["q"], Z["s"], o, min(w, 16 * cut), k == 0, k == len(Z["tiles"]) - 1)
+                in_turn("count", True)
+        for a, b, src in [(cut, nb, ps(Z["bank"], 16 * cut - y0, min(16 * nb, GB) - y0)), (0, cut, ps(3, 0, 16 * cut))][:2 if cut else 1]:
+            onv = [m for m in sorted(Z["v"]) if a <= m < b]
+            if onv:
+                x = sorted(Z["v"]).index(onv[0])
+                act(X(Z["rs"], onv[0], onv[-1] + 1), X(Z["junk"], (x + 1) * JW - 1, (x + len(onv)) * JW, JW), AF.Identity, 128.0)
+            vtt(X(Z["p2"], a, b), X(Z["dg"], 16 * a + 15, 16 * b, 16), X(Z["rs"], a, b), A.add)
             vsc(X(Z["ext"], 16 * a, 16 * a + src[1]), X("am", 0, src[1]), src, 0.0, A.add, A.max)
-            vtt(X(Z["yr"], a, b), X(Z["ext"], 16 * a + 15, 16 * b, 16), X(Z["p2"], a, b), A.add)
-            vcp(X(out, o0 + a, o0 + b), X(Z["yr"], a, b))
+            vtt(X(Z["yr"], a, b), X(Z["ext"], 16 * a + 15, 16 * b, 16), X(Z["p2"], a, b), A.subtract)
+            vts(X(out, o0 + a, o0 + b), X(Z["yr"], a, b), c1, Z["mid"], A.add, A.add)
 
     def parts(Z):
         return [(Z["cut"], Z["nb"]), (0, Z["cut"])][:2 if Z["cut"] else 1]
+
+    def own_slot(name, n):
+        k = [name in bl for o, bl in OWN_TILES].index(True)
+        a = 4 * OWN_TILES[k][0] + OWN_TILES[k][1].index(name)
+        return lambda lo=0, hi=n: X("mo", a + 4 * lo, a + 4 * (hi - 1) + 1, 4)
+
+    def own_compare(name, m, n, vsrc, ssrc, up):
+        out, x = own_slot(name, n), OWN_ALL.index(name)
+        if name in OWN_V:
+            k = OWN_V.index(name) + 1
+            vts(out(), vsrc, X("vo", 16 * m + 15, 16 * m + 16), None, A.is_gt if up else A.is_lt)
+            vsc(X("jo", k * JW - n // 2, k * JW), out(0, n // 2), out(n // 2, n), 0.0, A.add, A.add)
+        else:
+            act(X("tao", W * x, W * x + n), ssrc, AF.Sign, X("vo", 16 * m + 15, 16 * m + 16), -1.0)
+            act(out(), X("tao", W * x, W * x + n), AF.Relu, 0.0, -1.0 if up else 1.0, X("rso", m + 16 * up, m + 16 * up + 1))
+
+    def own_block(lo, hi, src, name):
+        n, out = hi - lo, own_slot(name, hi - lo)
+        vsc(X("yo", lo, hi), X("ym", 0, n), src, 0.0, A.add, A.min)
+        vsc(X("vo", lo, hi), X("d0", 0, n), X("yo", lo, hi), 0.0, A.min, A.max)
+        vtt(out(), src, X("vo", lo, hi), A.is_le)
+        vsc(X("dgo", lo, hi), X("keep0", 0, n), out(), 0.0, A.mult, A.add)
+        vtt(X("po", lo // 16, hi // 16), X("baseo", lo // 16, hi // 16), X("dgo", lo + 15, hi, 16), A.subtract)
+
+    def own_count(bank, tiles):
+        for k in tiles:
+            o = OWN_TILES[k][0]
+            mm(bank, "cq", "cs", W if OWN_TILES[k][1][0].startswith("u") else 0, "moq", "mos", o, W, k == tiles[0], k == tiles[-1])
+
+    def own_rowsums(out, a, kind, lo, hi, o):
+        m = lo
+        while m < hi:
+            onv = kind + str(m) in OWN_V
+            e = m
+            while e < hi and (kind + str(e) in OWN_V) == onv:
+                e += 1
+            k = OWN_V.index(kind + str(m)) + 1 if onv else 0
+            sums = X("jo", k * JW - 1, (k + e - m - 1) * JW, JW) if onv else X("rso", m + 16 * (kind == "u"), e + 16 * (kind == "u"))
+            vtt(X(out, m, e), X(a, m, e), sums, o)
+            m = e
+
+    def first_run(tq, tsc):
+        mm(4, "urq", "urs", 0, tq, tsc, UO, W)
+        mm(5, "urq", "urs", 0, tq, tsc, UO, W)
+        own_block(0, W, ps(4, 0, W), "d0")
+        for m in range(NB - 1, 0, -1):
+            own_compare("l%d" % m, m, 16 * m, ps(4, 0, 16 * m), ps(5, 0, 16 * m), False)
+        act(X("ssb", 0, W), ps(5, 0, W), AF.Copy)
+        for k in (0, 1):
+            vq("moq", "mos", W * k, W, X("mo", 4 * W * k, 4 * W * (k + 1)))
+        own_count(7, [0, 1])
+        vsc(X("exo", 0, W), X("am", 0, W), ps(7, 0, W), 0.0, A.add, A.max)
+        own_rowsums("qo", "po", "l", 0, NB, A.subtract)
+        vtt(X("po", 0, NB), X("qo", 0, NB), X("exo", 15, W, 16), A.add)
+
+    def second_run(tq, tsc, o0):
+        mm(6, "urq", "urs", 0, tq, tsc, UO + M, W)
+        mm(0, "urq", "urs", 0, tq, tsc, UO + M, W)
+        for m in range(NB):
+            own_compare("u%d" % m, m, M, ps(6, W - M, W), ps(0, W - M, W), True)
+        own_block(W, C, ps(6, W - M, W), "d1")
+        for m in range(13, NB, -1):
+            n = 16 * m - W
+            own_compare("l%d" % m, m, n, ps(6, W - M, W - M + n), ps(0, W - M, W - M + n), False)
+        act(X("ssb", W, C), ps(0, W - M, W), AF.Copy)
+        own_rowsums("yro", "po", "u", 0, NB, A.add)
+        vcp(X("rko", o0, o0 + NB), X("yro", 0, NB))
+        for k in (2, 4):
+            o = OWN_TILES[k][0]
+            vq("moq", "mos", o, 2 * M, X("mo", 4 * o, 4 * (o + 2 * M)))
+        own_count(3, [2, 3, 4, 5])
+        vsc(X("exo", W, C), X("am", 0, M), ps(3, 0, M), 0.0, A.add, A.max)
+        own_rowsums("qo", "po", "l", NB, 14, A.subtract)
+        vtt(X("yro", NB, 14), X("qo", NB, 14), X("exo", W + 15, C, 16), A.add)
+        vcp(X("rko", o0 + NB, o0 + 14), X("yro", NB, 14))
+
+    OWN = dict(m="mo", q="moq", s="mos", tiles=OWN_T2, offs=tile_offsets(OWN_T2), rng=OWN_RANGE, v=OWN_V2, y="yo", val="vo",
+               tau="tao", junk="jo", dg="dgo", rs="rso", p="po", p2="qo", ext="exo", yr="yro", dm="dmo", mid=0.0, nb=14,
+               cut=OWN_CUT[0], y0=OWN_CUT[1], bank=1)
+    for a, b in zeros(OWN, OWN_Z2):
+        act(X("mo", a, b), X("zb", 0, b - a), AF.Copy)
+
+    def first_run(tq, tsc):
+        mm(4, "urq", "urs", 0, tq, tsc, UO, W)
+        mm(5, "urq", "urs", 0, tq, tsc, UO, W)
+        in_block(OWN, 0, W, ps(4, 0, W))
+
+    def second_run(tq, tsc, o0):
+        mm(6, "urq", "urs", 0, tq, tsc, UO + M, W)
+        mm(7, "urq", "urs", 0, tq, tsc, UO, C)
+        mm(0, "urq", "urs", 0, tq, tsc, UO, C)
+        in_block(OWN, W, C, ps(6, W - M, W))
+        Z = dict(OWN, v=OWN_V2 if o0 else OWN_V0)
+        compares(Z, [m for m in range(1, 14) if m not in Z["v"]], lambda lo, hi: ps(7, lo, hi), lambda m, lo, hi: ps(5 if 16 * m < W else 0, lo, hi))
+        act(X("ssb"), ps(0, 0, C), AF.Copy)
+        places(Z, "baseo", 0, 14, "rko", o0)
 
     vq("uq", "us", 0, W, X("ub"))
     pick("urq", "urs", 0, "uq", "us", W, X("l16"))
@@ -387,28 +521,20 @@ def rank_program(g, core, T, topo):
         if t == 0:
             vq(tq, tsc, UO, C, X("xb"))
             send(t, X(lq), X(tq))
+            first_run(tq, tsc)
         else:
-            mm(6, "urq", "urs", 0, tq, tsc, UO + H, W)
-            send(t, X(lq, UO + H, UO + C), X(tq, UO + H, UO + C))
+            send(t, X(lq, UO + M, UO + C), X(tq, UO + M, UO + C))
         send(t, X(ls), X(tsc))
-        mm(7, "urq", "urs", 0, tq, tsc, UO, C)
-        mm(0, "urq", "urs", 0, tq, tsc, UO, C)
-        if t == 0:
-            in_block(OWN, 0, H, ps(7, 0, H))
-            in_block(OWN, H, C, ps(7, H, C))
-        else:
-            in_block(OWN, H, C, ps(6, 0, W))
-        compares(OWN, OWN_S, lambda lo, hi: ps(7, lo, hi), lambda m, lo, hi: ps(5 if t and 16 * m < H else 0, lo, hi))
-        act(X("ssb"), ps(0, 0, C), AF.Copy)
-        places(OWN, "baseo", 0, 14, "rko", 16 * t)
-        sent = parts(OWN) if SPLIT_SEND else [(0, 14)]
+        second_run(tq, tsc, 16 * t)
+        halves = parts(OWN)
+        sent = halves if SPLIT_SEND else [(0, 14)]
         for a, b in sent:
             send(t, X("lr", 16 * t + a, 16 * t + b), X("rko", 16 * t + a, 16 * t + b))
 
         pick("upq%d" % t, "ups%d" % t, 0, lq, ls, UO, X("l2"))
         mm(2, "upq%d" % t, "ups%d" % t, 0, lq, ls, UO, C)
         act(X("spb"), ps(2, 0, C), AF.Copy)
-        for a, b in parts(OWN):
+        for a, b in halves:
             vcp(by(X("ow"), X("rko", 16 * t + a, 16 * t + b)), X("nf", 16 * a, 16 * b))
         if t == 0:
             load("y", X("wq"), T.wc[:], [len(ops) - 1])
@@ -418,15 +544,16 @@ def rank_program(g, core, T, topo):
         vsc(X("oe1"), X("am", 0, K), X("ow", 0, K), 0.0, A.add, A.max)
         vts(X("o1", 0, 5), X("oe1", 15, K, 16), offc, None, A.subtract)
         act(X("sw", 0, K), by(X("ssb"), X("o1", 0, 5)), AF.Copy)
-        act(X("sp", GA + 96, GB), by(X("sw", 0, K), X("pil", 6, 14)), AF.Copy)
-        act(X("sp", GA, GA + 96), by(X("sw", 0, K), X("pil", 0, 6)), AF.Copy)
+        for lo, hi in GATHERED:
+            act(X("sp", lo, hi), by(X("sw", 0, K), X("pil", (lo - GA) // 16, (hi - GA) // 16)), AF.Copy)
         vsc(X("oex"), X("k4", 0, K), X("ow", 0, K), 0.0, A.mult, A.add)
         vts(o4, X("oex", 3, K, 4), cpo, rcol, A.mult, A.add)
         send(t, ll, o4)
         act(X("ts"), by(X("xb"), o4), AF.Copy, 0.0, 0.5)
         for b in range(4):
-            mm(3 + b, "eq", "es", W * b, lq, ls, UO, C)
-            act(X("eh", b, 4 * C, 4), ps(3 + b, 0, C), AF.Copy, 0.0, 0.5)
+            bank = [4, 5, 6, 1][b]
+            mm(bank, "eq", "es", W * b, lq, ls, UO, C)
+            act(X("eh", b, 4 * C, 4), ps(bank, 0, C), AF.Copy, 0.0, 0.5)
         act(X("ess"), by(X("eh"), ll), AF.Copy)
 
         for a, b in sent:
@@ -434,34 +561,37 @@ def rank_program(g, core, T, topo):
         act(X("row", GB, NP), X("sw", K - (NP - GB), K), AF.Identity, X("ew", 0, 1))
         act(X("row", K, GA), X("ew", 0, GA - K), AF.Identity, X("sw", 1, 2))
         act(X("row", 0, K), X("ew", 0, K), AF.Identity, X("sw", 0, 1))
-        for lo, hi in [(GA + 96, GB), (GA, GA + 96)]:
+        for i in range(1, K):
+            lo, hi = max(START[i], GA), min(START[i] + LEN[i], GATHERED[-1][0])
+            if lo < hi:
+                act(X("row", lo, hi), X("ew", lo - START[i], hi - START[i]), AF.Identity, X("sw", i, i + 1))
+        for lo, hi in GATHERED:
             vtt(X("row", lo, hi), by(X("ew"), X("pjl", (lo - GA) // 16, (hi - GA) // 16)), X("sp", lo, hi), A.add)
         vsc(X("vp", GB, NP), X("m3", 0, 32), X("row", GB, NP), -BIG, A.add, A.max)
         vsc(X("vp", K, GA), X("m3", 0, 32), X("row", K, GA), -BIG, A.add, A.max)
-        for lo, hi in [(GA + 96, GB), (GA, GA + 96)]:
+        for lo, hi in MIXED:
             in_block(PAIR, lo, hi, X("row", lo, hi))
         compares(PAIR, PAIR_S, lambda lo, hi: X("row", lo, hi), lambda m, lo, hi: X("row", lo, hi))
         places(PAIR, "basep", 7, 21, "rk", 0)
 
-        for a, b in parts(PAIR):
-            vcp(by(X("xw"), X("rk", a, b)), X("xl" if last else "x0", 16 * a, 16 * b))
+        for a, b in PAIR_RUNS:
+            vcp(by(X("xw"), X("rk", a, b)), X("x0", 16 * a, 16 * b))
         for lo, hi in LISTS:
             vsc(X("ex4", lo, hi), X("k4", lo, hi), X("xw", lo, hi), 0.0, A.mult, A.add)
             in_turn("ex4", lo)
         for lo, hi in LISTS:
             a, b = lo // 4, hi // 4
             ends = X("ex4", lo + 3, hi, 4)
-            vts(X("xi", a, b), ends, cp, float(MID) if last else 0.0, A.mult, A.add)
+            vts(X("xi", a, b), ends, cp, None, A.mult)
             vts(X("xk", a, b), X("xi", a, b), 127, None, A.bitwise_and)
             vts(X("a4", a, b), X("xk", a, b), 4.0, rcol, A.mult, A.add)
-            if last:
-                vts(X("xj", a, b), X("xi", a, b), 7, 127, A.logical_shift_right, A.bitwise_and)
-                vts(X("b4", a, b), X("xj", a, b), 4.0, rcol, A.mult, A.add)
-            else:
-                vts(X("b4", a, b), ends, cpb, rcol, A.mult, A.add)
+            vts(X("b4", a, b), ends, cpb, rcol, A.mult, A.add)
         if last:
-            act(X("olt"), X("xw", 0, C), AF.Identity, MAGIC, 2.0 ** -14)
-            act(X("olf"), X("olt"), AF.Identity, -MAGIC)
+            act(X("olt"), X("xw", 0, C), AF.Identity, MAGIC, 1.0 / 1024)
+            act(X("yo"), X("olt"), AF.Identity, -MAGIC)
+            for lo, hi in [(0, 64), (64, 144), (144, C)]:
+                act(X("stg", 4 * lo, 4 * hi), by(X("st4"), X("a4", lo // 4, hi // 4)), AF.Copy)
+                vtt(X("olf", lo, hi), X("stg", 4 * lo, 4 * hi, 4), X("yo", lo, hi), A.add)
             store("y", T.ol[:], X("olf"), T.olf[0:128:16, :])
 
         nq, ns = "tq%d" % (t + 1), "tsc%d" % (t + 1)
@@ -471,42 +601,45 @@ def rank_program(g, core, T, topo):
             in_turn("bg", lo)
             vtt(X("zt", 4 * lo, 4 * hi), by(X("ts"), X("a4", lo // 4, hi // 4)), X("bg", 4 * lo, 4 * hi), A.add)
 
+        H = RUNS[t]
+
         def layer(c, lo, hi):
-            vq("zq", "zs", W * c, W, X("zt", 4 * lo, 4 * (lo + W)))
+            vq("zq", "zs", W * c, W, X("zt", 4 * M * c, 4 * (M * c + W)))
             for b in range(4):
                 bank = 4 * (1 - c) + b
                 mm(bank, "wq", "wp", W * b, "zq", "zs", W * c, W)
-                act(X("rr", 4 * lo + b, 4 * hi, 4), ps(bank, 0, hi - lo), AF.Relu, 0.0, 0.03125)
+                act(X("rr", 4 * lo + b, 4 * hi, 4), ps(bank, lo - M * c, hi - M * c), AF.Relu, 0.0, 0.03125)
 
         def add(lo, hi, b=0, step=1):
             vtt(X("xb", 4 * lo + b, 4 * hi, step), X("rr", 4 * lo + b, 4 * hi, step), X("zt", 4 * lo + b, 4 * hi, step), A.add)
-        for lo, hi in PIECES:
-            if lo == H:
-                layer(0, 0, H)
+        for lo, hi in PIECES[H]:
             combine(lo, hi)
+            if hi == (W if H == W else C):
+                layer(0, 0, H)
+        if H < W:
+            combine(H, W)
         layer(1, H, C)
         for b in range(4):
             add(0, H, b, 4)
         vq(nq, ns, UO, W, X("xb", 0, 4 * W))
         if last:
             mm(4, "vq", "vs", 0, nq, ns, UO, W)
-            store("y", T.oc[:, 0:4 * H], X(nq, UO, UO + H))
+            store("y", T.oc[:, 0:4 * M], X(nq, UO, UO + M))
             act(X("yf", 0, H), ps(4, 0, H), AF.Copy)
             store("y", T.y[:, 0:H], X("yf", 0, H))
         else:
-            mm(4, "urq", "urs", 0, nq, ns, UO, W)
-            mm(5, "urq", "urs", 0, nq, ns, UO, W)
-            send(t + 1, X("lq%d" % (t + 1), 0, UO + H), X(nq, 0, UO + H))
-            in_block(OWN, 0, H, ps(4, 0, H))
+            send(t + 1, X("lq%d" % (t + 1), 0, UO + M), X(nq, 0, UO + M))
+            first_run(nq, ns)
         for b in range(4):
             add(W, C, b, 4)
-        add(H, W)
-        vq(nq, ns, UO + H, W, X("xb", 4 * H, 4 * C))
+        if H < W:
+            add(H, W)
+        vq(nq, ns, UO + M, W, X("xb", 4 * M, 4 * C))
 
-    mm(5, "vq", "vs", 0, "tq3", "tsc3", UO + H, W)
-    act(X("yf", H, C), ps(5, 0, W), AF.Copy)
+    mm(5, "vq", "vs", 0, "tq3", "tsc3", UO + M, W)
+    act(X("yf", H, C), ps(5, H - M, W), AF.Copy)
     store("s", T.y[:, H:C], X("yf", H, C))
-    store("y", T.oc[:, 4 * H:4 * C], X("tq3", UO + H, UO + C))
+    store("y", T.oc[:, 4 * M:4 * C], X("tq3", UO + M, UO + C))
     for k in range(4):
         store("y" if k else "s", T.osc[4 * k:4 * k + 4, :], X("tsc3", UO, UO + C), T.tsc3[32 * k:32 * k + 4, UO:UO + C])
 

from concourse.mybir import dt, AluOpType, AxisListType, ActivationFunctionType

C, K, R = 224, 80, 3
STEP = [1, 2, 4]
LEN = [K // (i + 1) for i in range(K)]
START = [sum(LEN[:i]) for i in range(K)]
NP = sum(LEN)
BIG = 2.0 ** 93
OFF = 1024.0
KK = 2.0 ** 26
MID = 5100
MAGIC = 1.5 * 2.0 ** 23
PMID = 160.0
JW = 168
GATHERED = [(176, 336)]
MIXED = [(208, 336), (112, 208)]
GA, GM, GB = 112, 224, 336
W = 128
M = C - W
RUNS = [128, 128, 128]
UO = 16
PIECES = {96: [(0, 32), (32, 64), (64, 96), (128, 160), (160, 224)], 128: [(0, 32), (32, 80), (80, 128), (128, 160), (160, 224)]}
LISTS = [(0, 64), (64, 224)]

NB = W // 16
OWN_TILES = [(0, ["d0", "l7", "l6", "l5"]), (128, ["l4", "l3", "l2", "l1"]), (256, ["u0", "u1", "u2", "u3"]), (352, ["u4", "u5", "u6", "u7"]),
             (480, ["d1", "l13", "l12", "l11"]), (576, ["l10", "l9"])]
OWN_ZERO = [(80, 128), (144, 256), (528, 576), (576, 672)]
OWN_ALL = [x for o, bl in OWN_TILES for x in bl]
OWN_V = ["u5", "u6", "u7", "l11", "l12", "l13"]
WO = 704
OWN_T2 = [(224, [13, 12, 11, "d"]), (128, [2, 1]), (128, [6, 5, 4, 3]), (160, [10, 9, 8, 7])]
OWN_Z2 = [176, 0, 48, 112]
OWN_V2 = [13, 12, 11]
OWN_V0 = [13, 12, 11, 10]
OWN_S = [m for m in range(1, 14) if m not in OWN_V2]
OWN_RANGE = {m: (0, 16 * m) for m in range(1, 14)}
OWN_CUT = (10, 96)
PAIR_TILES = [(336, [22, 21, 20, "d"]), (304, [19, 18, 17, 16]), (240, [15, 14, 13, 12]), (176, [11, 10, 9, 8]), (128, [7, 6, 5])]
PAIR_ZERO = [320, 256, 192, 128, 0]
PAIR_V = [20, 19, 18, 17, 16, 15, 6, 5]
PAIR_S = [m for m in range(22, 4, -1) if m not in PAIR_V]
PAIR_RANGE = {m: (0, 16 * m) for m in range(7, 21)}
PAIR_RANGE.update({5: (0, 80), 6: (16, 80), 21: (0, 328), 22: (0, 328)})
PAIR_CUT = (12, 112)
PAIR_RUNS = [(12, 23), (0, 12)]
SPLIT_SEND = True
WP = sum(w for w, _ in PAIR_TILES)

F, B, I, U, Q, S8 = "float32", "bfloat16", "int32", "uint16", "float8_e4m3fn_x4", "uint8"
SCRATCH = {}
for _n, _w, _d in [
    ("xb", 4 * C, B), ("ub", 512, B), ("vb", 512, B), ("wq", 512, Q), ("wp", 512, S8),
    ("uq", W, Q), ("us", W, S8), ("vq", W, Q), ("vs", W, S8), ("urq", W, Q), ("urs", W, S8),
    ("zb", 516, B), ("eb", 516, B), ("eq", 512, Q), ("es", 512, S8), ("cb", 1024, B), ("cq", 2 * W, Q), ("cs", 2 * W, S8),
    ("grp", W, B), ("pi", 1, I), ("li", 4, I), ("col", 13, F), ("xm", GB, B), ("xm4", C, B), ("b16", 24, F),
    ("nf", C, F), ("x0", NP, F), ("st4", 4 * K, F), ("stg", 4 * C, F),
    ("m3", GB, B), ("am", GB, B), ("ym", C, B), ("d0", C, B), ("keep0", C, B), ("k4", C, B),
    ("l16", 8, U), ("l2", 8, U), ("l8", 2, U), ("pil", 14, U), ("pjl", 14, U),
    ("dmo", C, B), ("dmp", GB, B),
    ("mo", 4 * WO, B), ("moq", WO, Q), ("mos", WO, S8), ("mp", 4 * WP, B), ("mpq", WP, Q), ("mps", WP, S8),
    ("yo", C, F), ("vo", C, F), ("yp", NP, F), ("vp", NP, F), ("tao", 24 * W, B), ("tap", 2400, B),
    ("jo", 16 * JW, B), ("jp", 8 * JW, B), ("dgo", C, B), ("dgp", NP, B),
    ("rso", 24, F), ("rsp", 24, F), ("po", 14, F), ("pp", 24, F), ("qo", 14, F), ("qp", 24, F), ("exo", C, F), ("exq", NP, F),
    ("yro", 14, F), ("yrp", 24, F), ("rk", 24, U), ("ow", C, F), ("oex", K, F), ("oe1", K, F), ("o1", 6, U), ("ssb", C, F), ("spb", C, F), ("sw", C, F),
    ("ew", C, F), ("sp", NP, F), ("row", NP, F), ("xw", NP, F), ("ex4", C, F), ("xi", 56, I), ("xk", 56, I),
    ("a4", 56, U), ("b4", 56, U),
    ("ts", 4 * K, B), ("eh", 4 * C, B), ("ess", 4 * K, B), ("bg", 4 * C, B), ("zt", 4 * C, B), ("zq", 2 * W, Q), ("zs", 2 * W, S8),
    ("rr", 4 * C, F), ("olt", C, F), ("olf", C, F), ("yf", C, F),
    ("rko", 16 * R, U), ("lr", 16 * R, U), ("o4", 24 * R, U), ("ll", 24 * R, U),
    ("tq3", UO + C, Q), ("tsc3", UO + C, S8),
] + [(n + str(t), w, d) for t in range(R) for n, w, d in [
    ("lq", UO + C, Q), ("ls", UO + C, S8), ("upq", W, Q), ("ups", W, S8), ("tq", UO + C, Q), ("tsc", UO + C, S8)]]:
    SCRATCH[_n] = ("sbuf", [128, _w], _d)
for _t in range(8):
    SCRATCH["ps%d" % _t] = ("psum", [128, 512], F)

SEMAPHORES = ["qv", "qs", "qp", "qg", "loc", "st"] + ["d%d" % k for k in range(40)]

A = AluOpType
AF = ActivationFunctionType
SIZE = {F: 4, B: 2, I: 4, U: 2, Q: 4, S8: 1}
HOP = 250
PASSES = 3
LOAD = 1800
FIRST = 2500
ZDMA = True
FAR = 1200


def schedule(ops):
    n = len(ops)
    nodes = [(o[0], o[3]) for o in ops] + [("end", 0)]
    pred = [[(d, 0 if soft else ops[d][4]) for d, soft in o[2]] for o in ops] + [[(x, o[4]) for x, o in enumerate(ops)]]
    succ = [[] for _ in nodes]
    for x, p in enumerate(pred):
        for d, lag in p:
            succ[d].append((x, lag))
    chain = [0] * (n + 1)
    for x in range(n - 1, -1, -1):
        chain[x] = nodes[x][1] + max(lag + chain[y] for y, lag in succ[x])
    best = None
    for _ in range(PASSES):
        order, start = one_pass(nodes, pred, succ, chain)
        if best is None or start[n] < best[0]:
            best = (start[n], order[:-1])
        back = one_pass(nodes, succ, pred, [start[x] + nodes[x][1] for x in range(n + 1)])[1]
        chain = [back[x] + nodes[x][1] for x in range(n + 1)]
    return best[1]


def one_pass(nodes, pred, succ, chain):
    n = len(nodes)
    tail = [chain[x] - nodes[x][1] for x in range(n)]
    left = [len(p) for p in pred]
    ready, start = [0] * n, [0] * n
    free, cand = {}, {}
    for x, (q, c) in enumerate(nodes):
        free[q] = 0
        cand.setdefault(q, [])
        if not left[x]:
            cand[q].append(x)
    order = []
    while len(order) < n:
        now, q = min((max(free[q], min(ready[x] for x in cand[q])), q) for q in cand if cand[q])
        pick = max((x for x in cand[q] if ready[x] <= now), key=lambda x: (tail[x], -x))
        soon = [x for x in cand[q] if now < ready[x] < now + nodes[pick][1] and tail[x] > tail[pick]]
        if soon:
            y = max(soon, key=lambda x: (tail[x], -x))
            fits = [x for x in cand[q] if ready[x] <= now and now + nodes[x][1] <= ready[y] + 20]
            if fits:
                pick = max(fits, key=lambda x: (tail[x], -x))
            elif max(ready[y] + chain[y], ready[y] + nodes[y][1] + chain[pick]) < max(now + chain[pick], now + nodes[pick][1] + chain[y]):
                pick = y
        start[pick] = max(now, ready[pick])
        free[q] = start[pick] + nodes[pick][1]
        cand[q].remove(pick)
        order.append(pick)
        for y, lag in succ[pick]:
            ready[y] = max(ready[y], free[q] + lag)
            left[y] -= 1
            if not left[y]:
                cand[nodes[y][0]].append(y)
    return order, start


def rank_program(g, core, T, topo):
    rank = T.rank_of(core)
    if rank is None:
        return
    queues = {"v": g.vector, "s": g.scalar, "p": g.tensor, "g": g, "y": g.sync}
    qsem = {"v": "qv", "s": "qs", "p": "qp", "g": "qg"}
    ops = []
    wrote, read = {}, {}
    counts = {"loc": 0, "st": 0}

    def X(name, lo=0, hi=None, step=1):
        where, shape, d = SCRATCH[name]
        hi = shape[1] if hi is None else hi
        cols = range(lo, hi, step)
        mask = 1 if where == "psum" else sum(1 << c for c in cols) if step > 1 else ((1 << (hi - lo)) - 1) << lo
        return (T[name][:, lo:hi:step] if step > 1 else T[name][:, lo:hi], len(cols), [(name, mask)], SIZE[d] == 2, where)

    def by(win, off, cast=None):
        a = win[0].bitcast(cast) if cast else win[0]
        return (a.indirect(off[0]), 16 * off[1], win[2] + off[2], False, "list")

    def val(a):
        return a[0] if isinstance(a, tuple) else a

    def op(q, fn, ins, outs, cycles, lag=HOP, sem=None, after=()):
        me, deps = len(ops), {x: False for x in after}
        rd = [r for a in ins if isinstance(a, tuple) for r in a[2]]
        wr = [a[2][0] for a in outs]
        rd += [r for a in outs for r in a[2][1:]]
        for name, mask in rd:
            deps.update({x: False for m, x in wrote.get(name, []) if m & mask})
            if name.startswith("ps"):
                deps.update({x: False for m, x in read.get(name, []) if ops[x][0] != q})
        for name, mask in wr:
            for m, x in wrote.get(name, []):
                if m & mask:
                    deps[x] = q == "p" and ops[x][0] == "p"
            deps.update({x: False for m, x in read.get(name, []) if m & mask})
        ops.append([q, fn, sorted(deps.items()), cycles, lag, sem])
        for name, mask in rd:
            read.setdefault(name, []).append((mask, me))
        for name, mask in wr:
            wrote[name] = [(m & ~mask, x) for m, x in wrote.get(name, []) if m & ~mask] + [(mask, me)]
            read[name] = [(m & ~mask, x) for m, x in read.get(name, []) if m & ~mask]
        return me

    turn = {}

    def in_turn(name, again):
        if again:
            ops[-1][2].append((turn[name], True))
        turn[name] = len(ops) - 1

    V, S, P = g.vector, g.scalar, g.tensor

    def cost(out, ins, rate=1.0):
        if out[4] == "list":
            return 60 + 3.8 * out[1]
        if ins[0][4] == "list":
            return 70 + 1.56 * out[1]
        return max(64, out[1] * rate * (0.5 if out[3] and all(a[3] for a in ins) else 1))

    def vts(out, a, s1, s2, o0, o1=None):
        more = () if o1 is None else (o1,)
        op("v", lambda: V.tensor_scalar(out[0], a[0], val(s1), val(s2), o0, *more), [a, s1, s2], [out], cost(out, [a]))

    def vtt(out, a, b, o):
        both = a[4] == b[4] == "sbuf"
        op("v", lambda: V.tensor_tensor(out[0], a[0], b[0], o), [a, b], [out], max(64, 2 * out[1]) if both else cost(out, [a, b]))

    def vcp(out, a):
        op("v", lambda: V.tensor_copy(out[0], a[0]), [a], [out], cost(out, [a]))

    def vms(out, c):
        op("v", lambda: V.memset(out[0], c), [], [out], cost(out, [out]))

    def vsc(out, d0, d1, init, o0, o1):
        op("v", lambda: V.tensor_tensor_scan(out[0], d0[0], d1[0], init, o0, o1), [d0, d1], [out], cost(out, [d0, d1]))

    def vq(q, s, lo, n, a):
        out, sc = X(q, lo, lo + n), X(s, lo, lo + n)
        op("v", lambda: V.quantize_mx(out[0], sc[0], a[0]), [a], [out, sc], 15 + 0.265 * a[1])

    def act(out, a, f, bias=0.0, scale=1.0, acc=None):
        kw = {} if acc is None else {"accum_out": acc[0]}
        op("s", lambda: S.activation(out[0], a[0], f, bias=val(bias), scale=val(scale), **kw), [a, bias, scale],
           [out] + ([] if acc is None else [acc]), (cost(out, [a]) if a[4] == "list" else max(64, out[1])) + (0 if acc is None else 24))

    def pick(q2, s2, lo, q, s, n, off):
        out, a = X(q2, lo, lo + 16 * off[1]), by(X(q, 0, n), off, dt.uint32)
        op("v", lambda: V.tensor_copy(out[0].bitcast(dt.uint32), a[0]), [a], [out], cost(out, [a]))
        so, sa = X(s2, lo, lo + 16 * off[1]), by(X(s, 0, n), off)
        op("s", lambda: S.activation(so[0], sa[0], AF.Copy), [sa], [so], cost(so, [sa]))

    def mm(bank, lq, ls, l0, rq, rs, r0, n, start=True, stop=True):
        a = [X("ps%d" % bank, 0, n), X(lq, l0, l0 + W), X(ls, l0, l0 + W), X(rq, r0, r0 + n), X(rs, r0, r0 + n)]
        op("p", lambda: P.matmul_mx(*[x[0] for x in a], start, stop), a[1:], a[:1], n + 16)

    def iota(out, pat, base, cm=0):
        kw = {} if SCRATCH[out[2][0][0]][2] == I else {"allow_small_or_imprecise_dtypes": True}
        op("g", lambda: g.iota(out[0], pat, base, cm, **kw), [], [out], 160 + 2 * out[1])

    def new_sem(n):
        name = "d%d" % (len(counts) - 2)
        counts[name] = n
        return name

    def raw(a):
        return a[0].bitcast(dt.uint8) if SCRATCH[a[2][0][0]][2] == Q else a[0]

    def row_bytes(a):
        return a[1] * SIZE[SCRATCH[a[2][0][0]][2]]

    def load(q, out, src, after=()):
        sem = new_sem(16)
        ins = [src] if isinstance(src, tuple) else []
        op(q, lambda: queues[q].dma_start(raw(out), val(src)).then_inc(T.sem[sem], 16), ins, [out], 60, LOAD + row_bytes(out) // 2, sem, after)

    def store(q, out, a, part=None):
        counts["st"] += 16
        src = raw(a) if part is None else part
        op(q, lambda: queues[q].dma_start(out, src).then_inc(T.sem.st, 16), [a], [], 60, FAR + row_bytes(a) // 2, "st")

    peers = [T.cores[rank ^ STEP[t]] for t in range(R)]

    def send(t, out, a):
        rid, pid = topo.addr(peers[t], core)
        counts["loc"] += len(topo.engines(core, peers[t]))
        sem = new_sem(len(topo.engines(peers[t], core)))
        op("g", lambda: g.remote_dma(raw(out), raw(a), T.sem[sem], T.sem.loc, pid, rid, topo.mask(core, peers[t])), [a], [out],
           360, FAR + row_bytes(a) + (FIRST if t == 0 and a[1] > W else 0), sem)

    lcol, gcol, qcol, rcol, offc, c1, cp, cpo, cpb = [X("col", i, i + 1) for i in range(9)]
    tcol = X("col", 12, 13)

    def ps(bank, lo, hi):
        return X("ps%d" % bank, lo, hi)

    def tile_offsets(tiles):
        return [sum(w for w, _ in tiles[:k]) for k in range(len(tiles))]

    load("y", X("ub"), T.u[:])
    load("s", X("xb"), T.x[:])

    iota(X("pi"), [[0, 1]], 0, 1)
    iota(X("b16"), [[16, 24]], 0)
    iota(X("xm"), [[0, GB // 16], [1, 16]], 0)
    iota(X("grp"), [[1, 8], [0, 16]], 0)
    iota(X("xm4"), [[0, C // 4], [1, 4]], 0)
    iota(X("nf"), [[1, C]], 0)
    for i in range(K):
        if i == 0 or LEN[i] != LEN[i - 1]:
            n = LEN.count(LEN[i])
            iota(X("x0", START[i], START[i] + n * LEN[i]), [[1, n], [1024, LEN[i]]], i)
            iota(X("st4", 4 * i, 4 * (i + n)), [[LEN[i], n], [0, 4]], START[i])

    vms(X("zb"), 0.0)
    vms(X("d0"), BIG)
    vms(X("d0", 0, C, 16), -BIG)
    vts(X("li", 0, 1), X("pi"), 15, None, A.bitwise_and)
    vts(X("li", 1, 2), X("pi"), 4, None, A.logical_shift_right)
    vts(X("li", 2, 3), X("pi"), 2, 3, A.logical_shift_right, A.bitwise_and)
    vts(X("li", 3, 4), X("pi"), 3, None, A.bitwise_and)
    vcp(X("col", 0, 4), X("li"))
    vcp(X("l16"), X("b16", 0, 8))
    vts(X("l8", 0, 1), lcol, 8.0, None, A.mult)
    vts(X("l2"), X("b16", 0, 8), 0.125, None, A.mult)
    vts(X("m3"), X("xm"), lcol, -BIG, A.is_equal, A.mult)
    act(offc, lcol, AF.Identity, 15 * OFF, -OFF)
    act(c1, lcol, AF.Identity, -15 * (OFF - 1), OFF - 1)
    for k in range(4):
        vts(X("cb", k, 512, 4), X("grp"), gcol, None, A.is_equal)
    vq("cq", "cs", 0, W, X("cb", 0, 512))
    vts(X("col", 9, 12), X("xm", 0, 3), qcol, 1.0 / KK, A.is_lt, A.max)
    op("v", lambda: V.tensor_reduce(cp[0], T.col[:, 9:12], AxisListType.X, A.mult), [X("col", 9, 12)], [cp], 64)
    act(cpo, cp, AF.Copy, 0.0, 4.0)
    act(cpb, cp, AF.Copy, 0.0, 1.0 / 256)
    vts(X("k4"), X("xm4"), qcol, KK, A.not_equal, A.mult)
    act(X("ym"), X("m3", 0, C), AF.Identity, -BIG, -33.0)
    act(X("am"), X("m3"), AF.Identity, OFF, 65.0 * OFF / BIG)
    vms(X("dmo"), BIG)
    vms(X("dmp", GA, GB), BIG)
    act(X("dmo", 0, C, 16), X("b16", 0, 14), AF.Copy, 0.0, -1.0)
    act(X("dmp", GA, GB, 16), X("b16", 7, 21), AF.Identity, PMID, -1.0)
    act(tcol, lcol, AF.Identity, PMID + 15.0, -2.0)
    act(X("dgp", 15, GA, 16), X("b16", 0, 7), AF.Identity, tcol, -1.0)
    act(X("dgp", GB + 15, NP, 16), X("b16", 21, 23), AF.Identity, tcol, -1.0)
    act(X("exq", GB + 15, NP, 16), X("zb", 0, 2), AF.Identity, offc)
    act(X("rso", 0, 2), X("zb", 0, 2), AF.Copy)
    act(X("rsp", 0, 5), X("zb", 0, 5), AF.Copy)
    op("g", lambda: g.affine_select(T.eb[:], T.zb[:], [[1, 516]], A.not_equal, 1.0, -3, -4), [X("zb")], [X("eb")], 205 + 2 * 516)
    for b in range(4):
        vq("eq", "es", W * b, W, X("eb", 3 - b, 515 - b))
    act(X("olt"), X("x0", GA, GB), AF.Copy, 0.0, 1.0 / 128)
    vsc(X("olf"), X("am", 0, C), X("olt"), 0.0, A.add, A.max)
    vts(X("xi", 0, 14), X("olf", 15, C, 16), offc, 128.0, A.subtract, A.mult)
    vts(X("pjl"), X("olf", 15, C, 16), offc, 0.125, A.subtract, A.mult)
    vts(X("xk", 0, 14), X("xi", 0, 14), 127, None, A.bitwise_and)
    vcp(X("pil"), X("xk", 0, 14))

    PAIR = dict(m="mp", q="mpq", s="mps", tiles=PAIR_TILES, offs=tile_offsets(PAIR_TILES), rng=PAIR_RANGE, v=PAIR_V, y="yp", val="vp",
                tau="tap", junk="jp", dg="dgp", rs="rsp", p="pp", p2="qp", ext="exq", yr="yrp", dm="dmp", mid=PMID, nb=23,
                cut=PAIR_CUT[0], y0=PAIR_CUT[1], bank=0)

    def zeros(Z, lows):
        return [(4 * (Z["offs"][k] + lo), 4 * (Z["offs"][k] + Z["tiles"][k][0])) for k, lo in enumerate(lows)]
    if ZDMA:
        for a, b in zeros(PAIR, PAIR_ZERO) + [(0, 4 * GA)]:
            load("y", X("mp", a, b), X("zb", 0, b - a))
    else:
        for a, b in zeros(PAIR, PAIR_ZERO):
            act(X("mp", a, b), X("zb", 0, b - a), AF.Copy)
        act(X("mp", 3, 4 * GA, 4), X("zb", 0, GA), AF.Copy)
    if RUNS[0] < W:
        load("y", X("zt", 4 * M, 4 * W), X("zb", 0, 4 * (W - M)))

    def slot(Z, m, lo, hi):
        k = [m in bl for w, bl in Z["tiles"]].index(True)
        t = Z["tiles"][k][1].index(m)
        return X(Z["m"], 4 * (Z["offs"][k] + lo) + t, 4 * (Z["offs"][k] + hi - 1) + t + 1, 4)

    def mine(Z, m):
        return X(Z["val"], 16 * m + 15, 16 * m + 16)

    def in_block(Z, lo, hi, src):
        vsc(X(Z["y"], lo, hi), X("ym", 0, hi - lo), src, 0.0, A.add, A.min)
        vsc(X(Z["val"], lo, hi), X("d0", 0, hi - lo), X(Z["y"], lo, hi), 0.0, A.min, A.max)
        vtt(slot(Z, "d", lo, hi), src, X(Z["val"], lo, hi), A.is_le)
        vsc(X(Z["dg"], lo, hi), X(Z["dm"], lo, hi), slot(Z, "d", lo, hi), BIG, A.min, A.add)

    def compares(Z, sblocks, vsrc, ssrc):
        pos = 0
        for m in sblocks:
            lo, hi = Z["rng"][m]
            act(X(Z["tau"], pos, pos + hi - lo), ssrc(m, lo, hi), AF.Sign, mine(Z, m), -1.0)
            act(slot(Z, m, lo, hi), X(Z["tau"], pos, pos + hi - lo), AF.Relu, acc=X(Z["rs"], m, m + 1))
            pos += hi - lo
        for m in Z["v"]:
            lo, hi = Z["rng"][m]
            h, x = (hi - lo) // 2, sorted(Z["v"]).index(m)
            vts(slot(Z, m, lo, hi), vsrc(lo, hi), mine(Z, m), None, A.is_lt)
            vsc(X(Z["junk"], (x + 1) * JW - h, (x + 1) * JW), slot(Z, m, lo, lo + h), slot(Z, m, lo + h, hi), -128.0, A.add, A.add)

    def places(Z, base, lo, hi, out, o0):
        nb, v0, nv, cut, y0 = Z["nb"], min(Z["v"]), len(Z["v"]), Z["cut"], Z["y0"]
        high = [k for k, (w, bl) in enumerate(Z["tiles"]) if w > 16 * cut]
        for k, (w, bl) in enumerate(Z["tiles"]):
            o = Z["offs"][k]
            vq(Z["q"], Z["s"], o, w, X(Z["m"], 4 * o, 4 * (o + w)))
            if k in high:
                mm(Z["bank"], "cq", "cs", 0, Z["q"], Z["s"], o + y0, w - y0, k == high[0], k == high[-1])
                in_turn("count", k)
            if cut:
                mm(3, "cq", "cs", 0, Z["q"], Z["s"], o, min(w, 16 * cut), k == 0, k == len(Z["tiles"]) - 1)
                in_turn("count", True)
        for a, b, src in [(cut, nb, ps(Z["bank"], 16 * cut - y0, min(16 * nb, GB) - y0)), (0, cut, ps(3, 0, 16 * cut))][:2 if cut else 1]:
            onv = [m for m in sorted(Z["v"]) if a <= m < b]
            if onv:
                x = sorted(Z["v"]).index(onv[0])
                act(X(Z["rs"], onv[0], onv[-1] + 1), X(Z["junk"], (x + 1) * JW - 1, (x + len(onv)) * JW, JW), AF.Identity, 128.0)
            vtt(X(Z["p2"], a, b), X(Z["dg"], 16 * a + 15, 16 * b, 16), X(Z["rs"], a, b), A.add)
            vsc(X(Z["ext"], 16 * a, 16 * a + src[1]), X("am", 0, src[1]), src, 0.0, A.add, A.max)
            vtt(X(Z["yr"], a, b), X(Z["ext"], 16 * a + 15, 16 * b, 16), X(Z["p2"], a, b), A.subtract)
            vts(X(out, o0 + a, o0 + b), X(Z["yr"], a, b), c1, Z["mid"], A.add, A.add)

    def parts(Z):
        return [(Z["cut"], Z["nb"]), (0, Z["cut"])][:2 if Z["cut"] else 1]

    def own_slot(name, n):
        k = [name in bl for o, bl in OWN_TILES].index(True)
        a = 4 * OWN_TILES[k][0] + OWN_TILES[k][1].index(name)
        return lambda lo=0, hi=n: X("mo", a + 4 * lo, a + 4 * (hi - 1) + 1, 4)

    def own_compare(name, m, n, vsrc, ssrc, up):
        out, x = own_slot(name, n), OWN_ALL.index(name)
        if name in OWN_V:
            k = OWN_V.index(name) + 1
            vts(out(), vsrc, X("vo", 16 * m + 15, 16 * m + 16), None, A.is_gt if up else A.is_lt)
            vsc(X("jo", k * JW - n // 2, k * JW), out(0, n // 2), out(n // 2, n), 0.0, A.add, A.add)
        else:
            act(X("tao", W * x, W * x + n), ssrc, AF.Sign, X("vo", 16 * m + 15, 16 * m + 16), -1.0)
            act(out(), X("tao", W * x, W * x + n), AF.Relu, 0.0, -1.0 if up else 1.0, X("rso", m + 16 * up, m + 16 * up + 1))

    def own_block(lo, hi, src, name):
        n, out = hi - lo, own_slot(name, hi - lo)
        vsc(X("yo", lo, hi), X("ym", 0, n), src, 0.0, A.add, A.min)
        vsc(X("vo", lo, hi), X("d0", 0, n), X("yo", lo, hi), 0.0, A.min, A.max)
        vtt(out(), src, X("vo", lo, hi), A.is_le)
        vsc(X("dgo", lo, hi), X("keep0", 0, n), out(), 0.0, A.mult, A.add)
        vtt(X("po", lo // 16, hi // 16), X("baseo", lo // 16, hi // 16), X("dgo", lo + 15, hi, 16), A.subtract)

    def own_count(bank, tiles):
        for k in tiles:
            o = OWN_TILES[k][0]
            mm(bank, "cq", "cs", W if OWN_TILES[k][1][0].startswith("u") else 0, "moq", "mos", o, W, k == tiles[0], k == tiles[-1])

    def own_rowsums(out, a, kind, lo, hi, o):
        m = lo
        while m < hi:
            onv = kind + str(m) in OWN_V
            e = m
            while e < hi and (kind + str(e) in OWN_V) == onv:
                e += 1
            k = OWN_V.index(kind + str(m)) + 1 if onv else 0
            sums = X("jo", k * JW - 1, (k + e - m - 1) * JW, JW) if onv else X("rso", m + 16 * (kind == "u"), e + 16 * (kind == "u"))
            vtt(X(out, m, e), X(a, m, e), sums, o)
            m = e

    def first_run(tq, tsc):
        mm(4, "urq", "urs", 0, tq, tsc, UO, W)
        mm(5, "urq", "urs", 0, tq, tsc, UO, W)
        own_block(0, W, ps(4, 0, W), "d0")
        for m in range(NB - 1, 0, -1):
            own_compare("l%d" % m, m, 16 * m, ps(4, 0, 16 * m), ps(5, 0, 16 * m), False)
        act(X("ssb", 0, W), ps(5, 0, W), AF.Copy)
        for k in (0, 1):
            vq("moq", "mos", W * k, W, X("mo", 4 * W * k, 4 * W * (k + 1)))
        own_count(7, [0, 1])
        vsc(X("exo", 0, W), X("am", 0, W), ps(7, 0, W), 0.0, A.add, A.max)
        own_rowsums("qo", "po", "l", 0, NB, A.subtract)
        vtt(X("po", 0, NB), X("qo", 0, NB), X("exo", 15, W, 16), A.add)

    def second_run(tq, tsc, o0):
        mm(6, "urq", "urs", 0, tq, tsc, UO + M, W)
        mm(0, "urq", "urs", 0, tq, tsc, UO + M, W)
        for m in range(NB):
            own_compare("u%d" % m, m, M, ps(6, W - M, W), ps(0, W - M, W), True)
        own_block(W, C, ps(6, W - M, W), "d1")
        for m in range(13, NB, -1):
            n = 16 * m - W
            own_compare("l%d" % m, m, n, ps(6, W - M, W - M + n), ps(0, W - M, W - M + n), False)
        act(X("ssb", W, C), ps(0, W - M, W), AF.Copy)
        own_rowsums("yro", "po", "u", 0, NB, A.add)
        vcp(X("rko", o0, o0 + NB), X("yro", 0, NB))
        for k in (2, 4):
            o = OWN_TILES[k][0]
            vq("moq", "mos", o, 2 * M, X("mo", 4 * o, 4 * (o + 2 * M)))
        own_count(3, [2, 3, 4, 5])
        vsc(X("exo", W, C), X("am", 0, M), ps(3, 0, M), 0.0, A.add, A.max)
        own_rowsums("qo", "po", "l", NB, 14, A.subtract)
        vtt(X("yro", NB, 14), X("qo", NB, 14), X("exo", W + 15, C, 16), A.add)
        vcp(X("rko", o0 + NB, o0 + 14), X("yro", NB, 14))

    OWN = dict(m="mo", q="moq", s="mos", tiles=OWN_T2, offs=tile_offsets(OWN_T2), rng=OWN_RANGE, v=OWN_V2, y="yo", val="vo",
               tau="tao", junk="jo", dg="dgo", rs="rso", p="po", p2="qo", ext="exo", yr="yro", dm="dmo", mid=0.0, nb=14,
               cut=OWN_CUT[0], y0=OWN_CUT[1], bank=1)
    for a, b in zeros(OWN, OWN_Z2):
        act(X("mo", a, b), X("zb", 0, b - a), AF.Copy)

    def first_run(tq, tsc):
        mm(4, "urq", "urs", 0, tq, tsc, UO, W)
        mm(5, "urq", "urs", 0, tq, tsc, UO, W)
        in_block(OWN, 0, W, ps(4, 0, W))

    def second_run(tq, tsc, o0):
        mm(6, "urq", "urs", 0, tq, tsc, UO + M, W)
        mm(7, "urq", "urs", 0, tq, tsc, UO, C)
        mm(0, "urq", "urs", 0, tq, tsc, UO, C)
        in_block(OWN, W, C, ps(6, W - M, W))
        Z = dict(OWN, v=OWN_V2 if o0 else OWN_V0)
        compares(Z, [m for m in range(1, 14) if m not in Z["v"]], lambda lo, hi: ps(7, lo, hi), lambda m, lo, hi: ps(5 if 16 * m < W else 0, lo, hi))
        act(X("ssb"), ps(0, 0, C), AF.Copy)
        places(Z, "baseo", 0, 14, "rko", o0)

    vq("uq", "us", 0, W, X("ub"))
    pick("urq", "urs", 0, "uq", "us", W, X("l16"))
    for t in range(R):
        pick("tq%d" % t, "tsc%d" % t, 0, "uq", "us", W, X("l8", 0, 1))

    for t in range(R):
        tq, tsc, lq, ls = ["%s%d" % (n, t) for n in ("tq", "tsc", "lq", "ls")]
        o4, ll = X("o4", 24 * t, 24 * t + 20), X("ll", 24 * t, 24 * t + 20)
        last = t == R - 1

        if t == 0:
            vq(tq, tsc, UO, C, X("xb"))
            send(t, X(lq), X(tq))
            first_run(tq, tsc)
        else:
            send(t, X(lq, UO + M, UO + C), X(tq, UO + M, UO + C))
        send(t, X(ls), X(tsc))
        second_run(tq, tsc, 16 * t)
        halves = parts(OWN)
        sent = halves if SPLIT_SEND else [(0, 14)]
        for a, b in sent:
            send(t, X("lr", 16 * t + a, 16 * t + b), X("rko", 16 * t + a, 16 * t + b))

        pick("upq%d" % t, "ups%d" % t, 0, lq, ls, UO, X("l2"))
        mm(2, "upq%d" % t, "ups%d" % t, 0, lq, ls, UO, C)
        act(X("spb"), ps(2, 0, C), AF.Copy)
        for a, b in halves:
            vcp(by(X("ow"), X("rko", 16 * t + a, 16 * t + b)), X("nf", 16 * a, 16 * b))
        if t == 0:
            load("y", X("wq"), T.wc[:], [len(ops) - 1])
            load("y", X("wp"), T.ws[:], [len(ops) - 2])
            load("y", X("vb"), T.v[:], [len(ops) - 3])
            vq("vq", "vs", 0, W, X("vb"))
        vsc(X("oe1"), X("am", 0, K), X("ow", 0, K), 0.0, A.add, A.max)
        vts(X("o1", 0, 5), X("oe1", 15, K, 16), offc, None, A.subtract)
        act(X("sw", 0, K), by(X("ssb"), X("o1", 0, 5)), AF.Copy)
        for lo, hi in GATHERED:
            act(X("sp", lo, hi), by(X("sw", 0, K), X("pil", (lo - GA) // 16, (hi - GA) // 16)), AF.Copy)
        vsc(X("oex"), X("k4", 0, K), X("ow", 0, K), 0.0, A.mult, A.add)
        vts(o4, X("oex", 3, K, 4), cpo, rcol, A.mult, A.add)
        send(t, ll, o4)
        act(X("ts"), by(X("xb"), o4), AF.Copy, 0.0, 0.5)
        for b in range(4):
            bank = [4, 5, 6, 1][b]
            mm(bank, "eq", "es", W * b, lq, ls, UO, C)
            act(X("eh", b, 4 * C, 4), ps(bank, 0, C), AF.Copy, 0.0, 0.5)
        act(X("ess"), by(X("eh"), ll), AF.Copy)

        for a, b in sent:
            vcp(by(X("ew"), X("lr", 16 * t + a, 16 * t + b)), X("spb", 16 * a, 16 * b))
        act(X("row", GB, NP), X("sw", K - (NP - GB), K), AF.Identity, X("ew", 0, 1))
        act(X("row", K, GA), X("ew", 0, GA - K), AF.Identity, X("sw", 1, 2))
        act(X("row", 0, K), X("ew", 0, K), AF.Identity, X("sw", 0, 1))
        for i in range(1, K):
            lo, hi = max(START[i], GA), min(START[i] + LEN[i], GATHERED[-1][0])
            if lo < hi:
                act(X("row", lo, hi), X("ew", lo - START[i], hi - START[i]), AF.Identity, X("sw", i, i + 1))
        for lo, hi in GATHERED:
            vtt(X("row", lo, hi), by(X("ew"), X("pjl", (lo - GA) // 16, (hi - GA) // 16)), X("sp", lo, hi), A.add)
        vsc(X("vp", GB, NP), X("m3", 0, 32), X("row", GB, NP), -BIG, A.add, A.max)
        vsc(X("vp", K, GA), X("m3", 0, 32), X("row", K, GA), -BIG, A.add, A.max)
        for lo, hi in MIXED:
            in_block(PAIR, lo, hi, X("row", lo, hi))
        compares(PAIR, PAIR_S, lambda lo, hi: X("row", lo, hi), lambda m, lo, hi: X("row", lo, hi))
        places(PAIR, "basep", 7, 21, "rk", 0)

        for a, b in PAIR_RUNS:
            vcp(by(X("xw"), X("rk", a, b)), X("x0", 16 * a, 16 * b))
        for lo, hi in LISTS:
            vsc(X("ex4", lo, hi), X("k4", lo, hi), X("xw", lo, hi), 0.0, A.mult, A.add)
            in_turn("ex4", lo)
        for lo, hi in LISTS:
            a, b = lo // 4, hi // 4
            ends = X("ex4", lo + 3, hi, 4)
            vts(X("xi", a, b), ends, cp, None, A.mult)
            vts(X("xk", a, b), X("xi", a, b), 127, None, A.bitwise_and)
            vts(X("a4", a, b), X("xk", a, b), 4.0, rcol, A.mult, A.add)
            vts(X("b4", a, b), ends, cpb, rcol, A.mult, A.add)
        if last:
            act(X("olt"), X("xw", 0, C), AF.Identity, MAGIC, 1.0 / 1024)
            act(X("yo"), X("olt"), AF.Identity, -MAGIC)
            for lo, hi in [(0, 64), (64, 144), (144, C)]:
                act(X("stg", 4 * lo, 4 * hi), by(X("st4"), X("a4", lo // 4, hi // 4)), AF.Copy)
                vtt(X("olf", lo, hi), X("stg", 4 * lo, 4 * hi, 4), X("yo", lo, hi), A.add)
            store("y", T.ol[:], X("olf"), T.olf[0:128:16, :])

        nq, ns = "tq%d" % (t + 1), "tsc%d" % (t + 1)

        def combine(lo, hi):
            act(X("bg", 4 * lo, 4 * hi), by(X("ess"), X("b4", lo // 4, hi // 4)), AF.Copy)
            in_turn("bg", lo)
            vtt(X("zt", 4 * lo, 4 * hi), by(X("ts"), X("a4", lo // 4, hi // 4)), X("bg", 4 * lo, 4 * hi), A.add)

        H = RUNS[t]

        def layer(c, lo, hi):
            vq("zq", "zs", W * c, W, X("zt", 4 * M * c, 4 * (M * c + W)))
            for b in range(4):
                bank = 4 * (1 - c) + b
                mm(bank, "wq", "wp", W * b, "zq", "zs", W * c, W)
                act(X("rr", 4 * lo + b, 4 * hi, 4), ps(bank, lo - M * c, hi - M * c), AF.Relu, 0.0, 0.03125)

        def add(lo, hi, b=0, step=1):
            vtt(X("xb", 4 * lo + b, 4 * hi, step), X("rr", 4 * lo + b, 4 * hi, step), X("zt", 4 * lo + b, 4 * hi, step), A.add)
        for lo, hi in PIECES[H]:
            combine(lo, hi)
            if hi == (W if H == W else C):
                layer(0, 0, H)
        if H < W:
            combine(H, W)
        layer(1, H, C)
        for b in range(4):
            add(0, H, b, 4)
        vq(nq, ns, UO, W, X("xb", 0, 4 * W))
        if last:
            mm(4, "vq", "vs", 0, nq, ns, UO, W)
            store("y", T.oc[:, 0:4 * M], X(nq, UO, UO + M))
            act(X("yf", 0, H), ps(4, 0, H), AF.Copy)
            store("y", T.y[:, 0:H], X("yf", 0, H))
        else:
            send(t + 1, X("lq%d" % (t + 1), 0, UO + M), X(nq, 0, UO + M))
            first_run(nq, ns)
        for b in range(4):
            add(W, C, b, 4)
        if H < W:
            add(H, W)
        vq(nq, ns, UO + M, W, X("xb", 4 * M, 4 * C))

    mm(5, "vq", "vs", 0, "tq3", "tsc3", UO + M, W)
    act(X("yf", H, C), ps(5, H - M, W), AF.Copy)
    store("s", T.y[:, H:C], X("yf", H, C))
    store("y", T.oc[:, 4 * M:4 * C], X("tq3", UO + M, UO + C))
    for k in range(4):
        store("y" if k else "s", T.osc[4 * k:4 * k + 4, :], X("tsc3", UO, UO + C), T.tsc3[32 * k:32 * k + 4, UO:UO + C])

    order = schedule(ops)
    at = {x: k for k, x in enumerate(order)}
    known = {q: {} for q in queues}
    snap, need, waits, waited = {}, set(), {}, set()
    for x in order:
        q = ops[x][0]
        want = {}
        for d, soft in ops[x][2]:
            key, v = (ops[d][0], at[d]) if ops[d][5] is None else (ops[d][5], counts[ops[d][5]])
            if not soft and known[q].get(key, -1) < v:
                want[key] = max(want.get(key, -1), v)
        waits[x] = []
        for key, v in sorted(want.items(), key=lambda kv: -kv[1] if kv[0] in qsem else 0):
            if known[q].get(key, -1) >= v:
                continue
            waits[x].append((key, v))
            known[q][key] = v
            if key in qsem:
                need.add(v)
                for k2, v2 in snap[v].items():
                    known[q][k2] = max(known[q].get(k2, -1), v2)
            else:
                waited.add(key)
        snap[at[x]] = dict(known[q])
    number, cnt = {}, {q: 0 for q in qsem}
    for k, x in enumerate(order):
        if k in need:
            cnt[ops[x][0]] += 1
            number[k] = cnt[ops[x][0]]
    for k, x in enumerate(order):
        q = ops[x][0]
        for key, v in waits[x]:
            queues[q].wait_ge(T.sem[qsem.get(key, key)], number[v] if key in qsem else v)
        ins = ops[x][1]()
        if k in need:
            ins.then_inc(T.sem[qsem[q]], 1)
    for name, v in counts.items():
        if name not in waited:
            g.wait_ge(T.sem[name], v)
